import numpy as np
import ml_dtypes


def mxq(x, axis, fmt="e4m3"):
    dtype, down = {"e4m3": (ml_dtypes.float8_e4m3fn, 7), "e5m2": (ml_dtypes.float8_e5m2, 14)}[fmt]
    v = np.moveaxis(np.asarray(x, np.float32).astype(ml_dtypes.bfloat16).astype(np.float64), axis, -1)
    blocks = v.reshape(v.shape[:-1] + (-1, 32))
    amax = np.abs(blocks).max(-1, keepdims=True)
    byte = np.maximum(np.where(amax > 0, np.frexp(amax)[1] - 1 + 127, 0) - down, 1)
    scale = np.exp2(byte - 127.0)
    codes = (blocks / scale).astype(np.float32).astype(dtype).astype(np.float64)
    return np.moveaxis((codes * scale).reshape(v.shape), -1, axis)


WIDE = False


def mx_kscale(k):
    if not WIDE:
        return np.ones(k)
    levels = np.array([10, -10, 5, -5, 0])
    if k % 512:
        return np.exp2(np.random.permutation(np.resize(levels, k // 32))).repeat(32)
    a = np.empty((k // 512, 16))
    for p in range(k // 512):
        a[p, :8] = np.random.permutation(np.resize(levels, 8))
        for g in range(8):
            far = levels[np.abs(levels - a[p, g]) >= 10]
            a[p, g + 8] = far[np.random.randint(len(far))]
    return np.exp2(a.ravel()).repeat(32)


def f64(x):
    return np.asarray(x).astype(np.float64)


def striped(idx):
    return np.tile(idx.reshape(-1, 16).T, (8, 1)).astype(np.uint16)


def unstriped(offs):
    return offs[:16].T.reshape(-1).astype(np.int64)


K, T, D, S, V, H, N = 512, 2048, 2, 1024, 512, 1024, 128
P = 2 ** 7


def setup_inputs():
    n = np.random.standard_normal
    s = mx_kscale(K)[:, None]
    u = mx_kscale(H)
    q = np.random.permutation(S)
    return {
        "xT": (n((K, T)) * s).astype(np.float32),
        "w1": (n((K, H)) / np.sqrt(K) / s * u).astype(np.float32),
        "w2": (n((H, N)) / np.sqrt(H) / u[:, None]).astype(np.float32),
        "gate": np.tile(np.random.uniform(0.2, 1.0, (D, 1, V)) / np.sqrt(D), (1, P, 1)).astype(np.float32),
        "offs": striped(np.random.permutation(T)[:S]),
        "pos1": striped(q[:V]),
        "pos2": striped(q[V:]),
    }


def reference(xT, w1, w2, gate, offs, pos1, pos2):
    h = mxq(f64(w1), 0, "e4m3").T @ mxq(f64(xT)[:, unstriped(offs)], 0, "e4m3")
    z = sum(f64(gate)[d, :1] * h[:, unstriped(p)] for d, p in enumerate((pos1, pos2)))
    return mxq(f64(w2), 0, "e4m3").T @ mxq(z, 0, "e4m3")

@@ -1,0 +1,321 @@
+from contextlib import ExitStack
+
+import concourse.mybir as mybir
+from concourse.masks import make_identity
+
+K, T, S, V, H, N = 512, 2048, 1024, 512, 1024, 128
+P = 128
+FLOPS = 2 * K * H * S + 2 * H * N * V
+
+F32 = mybir.dt.float32
+BF16 = mybir.dt.bfloat16
+U32 = mybir.dt.uint32
+U16 = mybir.dt.uint16
+U8 = mybir.dt.uint8
+FP8X4 = mybir.dt.float8_e4m3fn_x4
+COPY = mybir.ActivationFunctionType.Copy
+MULT = mybir.AluOpType.mult
+ADD = mybir.AluOpType.add
+
+
+def tile_picked_sage_none_e_kernel(tc, xT, w1, w2, gate, offs, pos1, pos2, out):
+    nc = tc.nc
+    with ExitStack() as ctx:
+        lists = ctx.enter_context(tc.tile_pool(name="lists", bufs=1))
+        sb = ctx.enter_context(tc.tile_pool(name="sb", bufs=1))
+        ps = ctx.enter_context(tc.psum_pool(name="ps", bufs=1))
+        ps_o = ctx.enter_context(tc.psum_pool(name="ps_o", bufs=3))
+        ps_t = ctx.enter_context(tc.psum_pool(name="ps_t", bufs=2))
+        ps_b = ctx.enter_context(tc.psum_pool(name="ps_b", bufs=2))
+
+        offs_t = lists.tile([P, S // 16], U16, name="offs_t")
+        pos1_t = lists.tile([P, V // 16], U16, name="pos1_t")
+        pos2_t = lists.tile([P, V // 16], U16, name="pos2_t")
+
+        warm = sb.tile([P, 1], F32, name="warm")
+        warm_out = sb.tile([P, 1], F32, name="warm_out")
+        nc.gpsimd.memset(warm[:], 0.0)
+        nc.scalar.activation(warm_out[:], warm[:], COPY)
+        ident32 = sb.tile([P, P], F32, name="ident32")
+        ident16 = sb.tile([P, P], BF16, name="ident16")
+        make_identity(nc, ident32[:])
+        make_identity(nc, ident16[:])
+
+        x_view = xT.rearrange("(p j) t -> p j t", j=4)
+        x_raw = []
+        for u, c0, c1 in ((0, 0, 1024), (0, 1024, 1536), (0, 1536, 2048), (1, 0, 1024), (1, 1024, 1536), (1, 1536, 1792), (1, 1792, 2048)):
+            raw = sb.tile([P, 2, c1 - c0], F32, name="x_raw_%d_%d" % (u, c0))
+            nc.sync.dma_start(raw[:], x_view[:, 2 * u : 2 * u + 2, c0:c1])
+            x_raw.append((u, c0, raw))
+            if len(x_raw) == 1:
+                nc.sync.dma_start(offs_t[:], offs)
+        w1_view = w1.rearrange("(p j) i -> p j i", j=4)
+        w1_raw = []
+
+        def load_w1(piece):
+            raw = sb.tile([P, 4, 256], F32, name="w1_raw_%d" % piece)
+            nc.sync.dma_start(raw[:], w1_view[:, :, 256 * piece : 256 * piece + 256])
+            w1_raw.append(raw)
+
+        load_w1(0)
+        load_w1(1)
+        w2_raw = sb.tile([P, 2, 4, N], F32, name="w2_raw")
+        w2_view = w2.rearrange("(g p t) n -> g p t n", g=2, t=4)
+        for g in range(2):
+            nc.sync.dma_start(w2_raw[:, g], w2_view[g])
+        nc.sync.dma_start(pos1_t[:], pos1)
+        nc.sync.dma_start(pos2_t[:], pos2)
+        gates = sb.tile([P, 2, V], F32, name="gates")
+        nc.sync.dma_start(gates[:], gate.rearrange("d p v -> p d v"))
+        load_w1(2)
+        load_w1(3)
+
+        pairs = []
+        for u in range(2):
+            pt = sb.tile([P, T, 2], BF16, name="pairs_%d" % u)
+            pairs.append(pt)
+        picked = sb.tile([P, S, 4], BF16, name="picked", align_bytes=64)
+        picked_words = picked[:].rearrange("p n q -> p (n q)").bitcast(U32).rearrange("p (n u) -> p n u", u=2)
+        xc0 = sb.tile([P, 512], U32, name="xc0", align_bytes=64)
+        xs = sb.tile([P, S], U8, name="xs", align_bytes=64)
+
+        def cast_x(i, a, b, scalar):
+            u, c0, raw = x_raw[i]
+            dst = pairs[u][:, c0 + a : c0 + b, :]
+            src = raw[:, :, a:b].rearrange("p e t -> p t e")
+            if scalar:
+                nc.scalar.activation(dst, src, COPY)
+            else:
+                nc.vector.tensor_copy(dst, src)
+
+        def gather_x(u, n0, n1):
+            window = pairs[u][:].rearrange("p t e -> p (t e)").bitcast(U32)
+            nc.vector.tensor_copy(picked_words[:, n0:n1, u], window.indirect(offs_t[:, n0 // 16 : n1 // 16]))
+
+        def quant_x(n0, n1):
+            nc.vector.quantize_mx(
+                out=xc[n0 // 512][:].bitcast(FP8X4),
+                scales=xs[:, n0:n1],
+                in_=picked[:, n0:n1, :].rearrange("p n q -> p (n q)"),
+            )
+
+        w1b, w1c, w1s = [], [], []
+        for g in range(2):
+            b = [None, None]
+            b[0] = sb.tile([P, 1, P, 4], BF16, name="w1b_%d_0" % g, align_bytes=64)
+            b[1] = sb.tile([P, 3, P, 4], BF16, name="w1b_%d_1" % g, align_bytes=64)
+            c = sb.tile([P, 4 * P], U32, name="w1c_%d" % g, align_bytes=64)
+            s = sb.tile([P, 4 * P], U8, name="w1s_%d" % g, align_bytes=64)
+            w1b.append(b)
+            w1c.append(c)
+            w1s.append(s)
+        xc1 = sb.tile([P, 512], U32, name="xc1", tag="w1b_0_0", align_bytes=64)
+        xc = (xc0, xc1)
+
+        def cast_w1(piece, rest):
+            g, half = divmod(piece, 2)
+            t0, t1 = ((0, 1), (1, 4))[rest]
+            dst = w1b[g][rest][:, :, 64 * half : 64 * half + 64, :].rearrange("p t m j -> p m t j")
+            src = w1_raw[piece][:].rearrange("p j (m t) -> p m t j", t=4)[:, :, t0:t1, :]
+            nc.scalar.activation(dst, src, COPY)
+
+        def quant_w1(g, t0, t1):
+            nc.vector.quantize_mx(
+                out=w1c[g][:, P * t0 : P * t1].bitcast(FP8X4),
+                scales=w1s[g][:, P * t0 : P * t1],
+                in_=w1b[g][min(t0, 1)][:, max(t0 - 1, 0) : max(t1 - 1, 1)].rearrange("p t m j -> p (t m j)"),
+            )
+
+        w2b = sb.tile([P, 2, N, 4], BF16, name="w2b", tag="w1b_0_1", align_bytes=64)
+        w2c = sb.tile([P, 2 * N], U32, name="w2c", align_bytes=64)
+        w2s = sb.tile([P, 2 * N], U8, name="w2s", align_bytes=64)
+
+        h = []
+        for b in range(8):
+            ht = sb.tile([P, S], F32, name="h_%d" % b)
+            h.append(ht)
+        t01, z, zc, zs = [], [], [], []
+        for g in range(2):
+            pair = []
+            for d in range(2):
+                if g:
+                    tt = sb.tile([P, 4, V], F32, name="term_%d" % d)
+                    pair.append([tt[:, t] for t in range(4)] + [tt])
+                else:
+                    blocks = []
+                    for t in range(4):
+                        tag = "w1b_1_%d" % d if t == 3 else "term_%d_%d" % (t, d)
+                        tt = sb.tile([P, V], F32, name="term_%d_%d" % (t, d), tag=tag, align_bytes=64)
+                        blocks.append(tt)
+                    pair.append(blocks)
+            t01.append(pair)
+            zt = sb.tile([P, V, 4], BF16, name="z_%d" % g, align_bytes=64)
+            zct = sb.tile([P, V], U32, name="zc_%d" % g, align_bytes=64)
+            zst = sb.tile([P, V], U8, name="zs_%d" % g, align_bytes=64)
+            z.append(zt)
+            zc.append(zct)
+            zs.append(zst)
+        out_t = sb.tile([P, V], F32, name="out_t")
+
+        def layer1(b):
+            g, t = divmod(b, 4)
+            for half in range(2):
+                n = slice(512 * half, 512 * half + 512)
+                acc = (ps_o if half else ps).tile([P, 512], F32, name="acc_%d" % half)
+                nc.tensor.matmul_mx(
+                    out=acc[:],
+                    lhsT=w1c[g][:, P * t : P * t + P].bitcast(FP8X4),
+                    lhsT_scale=w1s[g][:, P * t : P * t + P],
+                    rhs=xc[half][:].bitcast(FP8X4),
+                    rhs_scale=xs[:, n],
+                    start=True,
+                    stop=True,
+                )
+                nc.scalar.activation(h[b][:, n], acc[:], COPY)
+
+        pos = (pos1_t, pos2_t)
+
+        def gather_h(b, d, v0, v1):
+            g, t = divmod(b, 4)
+            nc.vector.tensor_tensor(
+                t01[g][d][t][:, v0:v1],
+                h[b][:].indirect(pos[d][:, v0 // 16 : v1 // 16]),
+                gates[:, d, v0:v1],
+                MULT,
+            )
+
+        def add_z(g, v0, v1):
+            dst = z[g][:, v0:v1, :].rearrange("p (c i) t -> p c t i", i=4)
+            a = t01[g][0][4][:, :, v0:v1].rearrange("p t (c i) -> p c t i", i=4)
+            b = t01[g][1][4][:, :, v0:v1].rearrange("p t (c i) -> p c t i", i=4)
+            nc.vector.tensor_tensor(dst, a, b, ADD)
+
+        back = {}
+
+        def fold(b, v0, v1):
+            g, t = divmod(b, 4)
+            sum_t = ps_t.tile([P, v1 - v0], F32, name="sum_t")
+            for v in range(v0, v1, P):
+                for d in range(2):
+                    nc.tensor.matmul(
+                        out=sum_t[:, v - v0 : v - v0 + P],
+                        lhsT=t01[g][d][t][:, v : v + P],
+                        rhs=ident32[:],
+                        start=d == 0,
+                        stop=d == 1,
+                        is_transpose=True,
+                    )
+            z_t = sb.tile([P, v1 - v0], BF16, name="z_t_%d" % b)
+            nc.scalar.activation(z_t[:], sum_t[:], COPY)
+            for v in range(v0, v1, P):
+                key = (g, v // 256)
+                if key not in back:
+                    back[key] = ps_b.tile([P, 4, 256], BF16, name="back")
+                nc.tensor.transpose(back[key][:, t, v % 256 : v % 256 + P], z_t[:, v - v0 : v - v0 + P], ident16[:])
+
+        def weave_z(g, half):
+            nc.scalar.copy(z[g][:, 256 * half : 256 * half + 256, :], back[g, half][:].rearrange("p t v -> p v t"))
+
+        def quant_z(g, v0, v1):
+            nc.vector.quantize_mx(
+                out=zc[g][:, v0:v1].bitcast(FP8X4),
+                scales=zs[g][:, v0:v1],
+                in_=z[g][:, v0:v1, :].rearrange("p v t -> p (v t)"),
+            )
+
+        def layer2(v0, v1):
+            acc = ps_o.tile([P, v1 - v0], F32, name="acc_1")
+            for g in range(2):
+                nc.tensor.matmul_mx(
+                    out=acc[:],
+                    lhsT=w2c[:, N * g : N * g + N].bitcast(FP8X4),
+                    lhsT_scale=w2s[:, N * g : N * g + N],
+                    rhs=zc[g][:, v0:v1].bitcast(FP8X4),
+                    rhs_scale=zs[g][:, v0:v1],
+                    start=g == 0,
+                    stop=g == 1,
+                )
+            nc.scalar.activation(out_t[:, v0:v1], acc[:], COPY)
+            nc.sync.dma_start(out[:, v0:v1], out_t[:, v0:v1])
+
+        cast_x(0, 0, 512, False)
+        cast_x(0, 512, 1024, True)
+        cast_x(1, 0, 512, False)
+        cast_x(2, 0, 352, False)
+        cast_x(2, 352, 512, True)
+        gather_x(0, 0, 1024)
+        cast_x(3, 0, 704, True)
+        cast_x(3, 704, 1024, False)
+        cast_x(4, 0, 512, False)
+        cast_x(5, 0, 256, True)
+        cast_x(6, 0, 256, False)
+        gather_x(1, 0, 512)
+        gather_x(1, 512, 1024)
+        cast_w1(0, 0)
+        cast_w1(0, 1)
+        cast_w1(1, 0)
+        cast_w1(1, 1)
+        quant_x(0, 512)
+        quant_w1(0, 0, 1)
+        quant_x(512, 1024)
+        layer1(0)
+        quant_w1(0, 1, 2)
+        quant_w1(0, 2, 4)
+        layer1(1)
+        nc.vector.tensor_copy(w2b[:], w2_raw[:].rearrange("p g t n -> p g n t"))
+        layer1(2)
+        layer1(3)
+        cast_w1(2, 0)
+        cast_w1(3, 0)
+        cast_w1(2, 1)
+        cast_w1(3, 1)
+        gather_h(0, 0, 0, V)
+        gather_h(0, 1, 0, V)
+        nc.vector.quantize_mx(
+            out=w2c[:].bitcast(FP8X4), scales=w2s[:], in_=w2b[:].rearrange("p g n t -> p (g n t)")
+        )
+        gather_h(1, 0, 0, V)
+        gather_h(1, 1, 0, V)
+        fold(0, 0, V)
+        gather_h(2, 0, 0, V)
+        gather_h(2, 1, 0, V)
+        quant_w1(1, 0, 1)
+        layer1(4)
+        fold(1, 0, V)
+        gather_h(3, 0, 0, V)
+        quant_w1(1, 1, 2)
+        quant_w1(1, 2, 4)
+        gather_h(3, 1, 0, V)
+        layer1(5)
+        fold(2, 0, V)
+        gather_h(4, 0, 0, V)
+        gather_h(4, 1, 0, V)
+        layer1(6)
+        fold(3, 0, V)
+        gather_h(5, 0, 0, V)
+        gather_h(5, 1, 0, V)
+        layer1(7)
+        fold(4, 0, 256)
+        fold(5, 0, 256)
+        weave_z(0, 0)
+        weave_z(0, 1)
+        gather_h(6, 0, 0, 256)
+        gather_h(6, 1, 0, 256)
+        fold(6, 0, 256)
+        gather_h(7, 0, 0, 256)
+        gather_h(7, 1, 0, 256)
+        fold(7, 0, 256)
+        weave_z(1, 0)
+        quant_z(0, 0, 512)
+        gather_h(6, 0, 256, 512)
+        gather_h(6, 1, 256, 512)
+        gather_h(7, 0, 256, 512)
+        gather_h(7, 1, 256, 512)
+        add_z(1, 256, 384)
+        add_z(1, 384, 512)
+        quant_z(1, 0, 256)
+        layer2(0, 256)
+        quant_z(1, 256, 384)
+        layer2(256, 384)
+        quant_z(1, 384, 512)
+        layer2(384, 512)

@@ -5,6 +5,7 @@ from concourse.masks import make_identity
 
 K, T, S, V, H, N = 512, 2048, 1024, 512, 1024, 128
 P = 128
+TURN = 384
 FLOPS = 2 * K * H * S + 2 * H * N * V
 
 F32 = mybir.dt.float32
@@ -24,9 +25,6 @@ def tile_picked_sage_none_e_kernel(tc, xT, w1, w2, gate, offs, pos1, pos2, out):
         lists = ctx.enter_context(tc.tile_pool(name="lists", bufs=1))
         sb = ctx.enter_context(tc.tile_pool(name="sb", bufs=1))
         ps = ctx.enter_context(tc.psum_pool(name="ps", bufs=1))
-        ps_o = ctx.enter_context(tc.psum_pool(name="ps_o", bufs=3))
-        ps_t = ctx.enter_context(tc.psum_pool(name="ps_t", bufs=2))
-        ps_b = ctx.enter_context(tc.psum_pool(name="ps_b", bufs=2))
 
         offs_t = lists.tile([P, S // 16], U16, name="offs_t")
         pos1_t = lists.tile([P, V // 16], U16, name="pos1_t")
@@ -36,48 +34,46 @@ def tile_picked_sage_none_e_kernel(tc, xT, w1, w2, gate, offs, pos1, pos2, out):
         warm_out = sb.tile([P, 1], F32, name="warm_out")
         nc.gpsimd.memset(warm[:], 0.0)
         nc.scalar.activation(warm_out[:], warm[:], COPY)
-        ident32 = sb.tile([P, P], F32, name="ident32")
-        ident16 = sb.tile([P, P], BF16, name="ident16")
-        make_identity(nc, ident32[:])
-        make_identity(nc, ident16[:])
+        ident = sb.tile([P, P], F32, name="ident")
+        make_identity(nc, ident[:])
+
+        bank = {}
+        for name in "ABCDEFGH":
+            whole = ps.tile([P, 512], F32, name="bank_" + name)
+            bank[name] = whole
 
         x_view = xT.rearrange("(p j) t -> p j t", j=4)
         x_raw = []
-        for u, c0, c1 in ((0, 0, 1024), (0, 1024, 1536), (0, 1536, 2048), (1, 0, 1024), (1, 1024, 1536), (1, 1536, 1792), (1, 1792, 2048)):
+        for u, c0, c1 in ((0, 0, 1024), (0, 1024, 2048), (1, 0, 1024), (1, 1024, 1792), (1, 1792, 2048)):
             raw = sb.tile([P, 2, c1 - c0], F32, name="x_raw_%d_%d" % (u, c0))
             nc.sync.dma_start(raw[:], x_view[:, 2 * u : 2 * u + 2, c0:c1])
             x_raw.append((u, c0, raw))
             if len(x_raw) == 1:
                 nc.sync.dma_start(offs_t[:], offs)
         w1_view = w1.rearrange("(p j) i -> p j i", j=4)
-        w1_raw = []
-
-        def load_w1(piece):
-            raw = sb.tile([P, 4, 256], F32, name="w1_raw_%d" % piece)
+        w1_lo = []
+        for piece in range(2):
+            raw = sb.tile([P, 4, 256], F32, name="w1_lo_%d" % piece)
             nc.sync.dma_start(raw[:], w1_view[:, :, 256 * piece : 256 * piece + 256])
-            w1_raw.append(raw)
-
-        load_w1(0)
-        load_w1(1)
+            w1_lo.append(raw)
         w2_raw = sb.tile([P, 2, 4, N], F32, name="w2_raw")
-        w2_view = w2.rearrange("(g p t) n -> g p t n", g=2, t=4)
-        for g in range(2):
-            nc.sync.dma_start(w2_raw[:, g], w2_view[g])
+        nc.sync.dma_start(w2_raw[:], w2.rearrange("(g p t) n -> p g t n", g=2, t=4))
         nc.sync.dma_start(pos1_t[:], pos1)
         nc.sync.dma_start(pos2_t[:], pos2)
         gates = sb.tile([P, 2, V], F32, name="gates")
         nc.sync.dma_start(gates[:], gate.rearrange("d p v -> p d v"))
-        load_w1(2)
-        load_w1(3)
+        w1_hi = sb.tile([P, 4, 512], F32, name="w1_hi", align_bytes=64)
+        nc.sync.dma_start(w1_hi[:], w1_view[:, :, 512:1024])
 
         pairs = []
         for u in range(2):
             pt = sb.tile([P, T, 2], BF16, name="pairs_%d" % u)
             pairs.append(pt)
-        picked = sb.tile([P, S, 4], BF16, name="picked", align_bytes=64)
-        picked_words = picked[:].rearrange("p n q -> p (n q)").bitcast(U32).rearrange("p (n u) -> p n u", u=2)
-        xc0 = sb.tile([P, 512], U32, name="xc0", align_bytes=64)
-        xs = sb.tile([P, S], U8, name="xs", align_bytes=64)
+        picked = []
+        for half in range(2):
+            pk = sb.tile([P, 4 * 512], BF16, name="picked_%d" % half, align_bytes=64)
+            picked.append(pk)
+        fetched = sb.tile([P, 2, S], U32, name="fetched")
 
         def cast_x(i, a, b, scalar):
             u, c0, raw = x_raw[i]
@@ -90,232 +86,267 @@ def tile_picked_sage_none_e_kernel(tc, xT, w1, w2, gate, offs, pos1, pos2, out):
 
         def gather_x(u, n0, n1):
             window = pairs[u][:].rearrange("p t e -> p (t e)").bitcast(U32)
-            nc.vector.tensor_copy(picked_words[:, n0:n1, u], window.indirect(offs_t[:, n0 // 16 : n1 // 16]))
+            nc.vector.tensor_copy(fetched[:, u, n0:n1], window.indirect(offs_t[:, n0 // 16 : n1 // 16]))
 
-        def quant_x(n0, n1):
+        def weave_x(n0, n1):
+            words = picked[n0 // 512][:].bitcast(U32).rearrange("p (n u) -> p n u", u=2)
+            nc.scalar.copy(words[:, n0 % 512 : n0 % 512 + n1 - n0], fetched[:, :, n0:n1].rearrange("p u n -> p n u"))
+
+        xc, xs = [], []
+
+        def quant_x(half, tag):
+            codes = sb.tile([P, 512], U32, name="xc_%d" % half, tag=tag, align_bytes=64)
+            scales = sb.tile([P, 512], U8, name="xs_%d" % half, align_bytes=64)
             nc.vector.quantize_mx(
-                out=xc[n0 // 512][:].bitcast(FP8X4),
-                scales=xs[:, n0:n1],
-                in_=picked[:, n0:n1, :].rearrange("p n q -> p (n q)"),
+                out=codes[:].bitcast(FP8X4),
+                scales=scales[:],
+                in_=picked[half][:],
             )
+            xc.append(codes)
+            xs.append(scales)
 
-        w1b, w1c, w1s = [], [], []
-        for g in range(2):
-            b = [None, None]
-            b[0] = sb.tile([P, 1, P, 4], BF16, name="w1b_%d_0" % g, align_bytes=64)
-            b[1] = sb.tile([P, 3, P, 4], BF16, name="w1b_%d_1" % g, align_bytes=64)
-            c = sb.tile([P, 4 * P], U32, name="w1c_%d" % g, align_bytes=64)
-            s = sb.tile([P, 4 * P], U8, name="w1s_%d" % g, align_bytes=64)
-            w1b.append(b)
-            w1c.append(c)
-            w1s.append(s)
-        xc1 = sb.tile([P, 512], U32, name="xc1", tag="w1b_0_0", align_bytes=64)
-        xc = (xc0, xc1)
+        term_lo = []
+        for b in range(4):
+            lo = sb.tile([P, 2 * V], F32, name="term_%d" % b, tag="picked_1" if b == 0 else "term_%d" % b, align_bytes=64)
+            term_lo.append(lo)
 
-        def cast_w1(piece, rest):
-            g, half = divmod(piece, 2)
-            t0, t1 = ((0, 1), (1, 4))[rest]
-            dst = w1b[g][rest][:, :, 64 * half : 64 * half + 64, :].rearrange("p t m j -> p m t j")
-            src = w1_raw[piece][:].rearrange("p j (m t) -> p m t j", t=4)[:, :, t0:t1, :]
-            nc.scalar.activation(dst, src, COPY)
+        w1b, w1c, w1s = {}, {}, {}
 
-        def quant_w1(g, t0, t1):
-            nc.vector.quantize_mx(
-                out=w1c[g][:, P * t0 : P * t1].bitcast(FP8X4),
-                scales=w1s[g][:, P * t0 : P * t1],
-                in_=w1b[g][min(t0, 1)][:, max(t0 - 1, 0) : max(t1 - 1, 1)].rearrange("p t m j -> p (t m j)"),
-            )
+        def cast_w1_lo(b):
+            if b == 3:
+                wide = term_lo[0][:, 0:256].bitcast(BF16)
+            else:
+                own = sb.tile([P, 4 * P], BF16, name="w1b_%d" % b, align_bytes=64)
+                wide = own[:]
+            dst = wide.rearrange("p (c i j) -> p c j i", i=2, j=4)
+            src = w1_lo[b // 2][:, :, P * (b % 2) : P * (b % 2) + P].rearrange("p j (c i) -> p c j i", i=2)
+            if b in (0, 3):
+                nc.vector.tensor_copy(dst, src)
+            else:
+                nc.scalar.activation(dst, src, COPY)
+            w1b[b] = (wide, 1)
 
-        w2b = sb.tile([P, 2, N, 4], BF16, name="w2b", tag="w1b_0_1", align_bytes=64)
+        def cast_w1_hi(u):
+            if u == 0:
+                own = sb.tile([P, 8 * P], BF16, name="w1b_4", align_bytes=64)
+                wide = own[:]
+            else:
+                wide = term_lo[2][:, 256:768].bitcast(BF16)
+            src = w1_hi[:].rearrange("p j (m t) -> p m j t", t=4)[:, :, :, 2 * u : 2 * u + 2]
+            nc.scalar.activation(wide.rearrange("p (e m j) -> p m j e", e=2, j=4), src, COPY)
+            w1b[4 + 2 * u] = (wide, 2)
+
+        def quant_w1(b0, tag):
+            wide, blocks = w1b[b0]
+            codes = sb.tile([P, P * blocks], U32, name="w1c_%d" % b0, tag=tag, align_bytes=64)
+            scales = sb.tile([P, P * blocks], U8, name="w1s_%d" % b0, align_bytes=64)
+            nc.vector.quantize_mx(out=codes[:].bitcast(FP8X4), scales=scales[:], in_=wide)
+            for i in range(blocks):
+                w1c[b0 + i] = codes[:, P * i : P * i + P]
+                w1s[b0 + i] = scales[:, P * i : P * i + P]
+
+        w2b = term_lo[0][:, 256:768].bitcast(BF16)
         w2c = sb.tile([P, 2 * N], U32, name="w2c", align_bytes=64)
         w2s = sb.tile([P, 2 * N], U8, name="w2s", align_bytes=64)
 
-        h = []
-        for b in range(8):
-            ht = sb.tile([P, S], F32, name="h_%d" % b)
-            h.append(ht)
-        t01, z, zc, zs = [], [], [], []
-        for g in range(2):
-            pair = []
-            for d in range(2):
-                if g:
-                    tt = sb.tile([P, 4, V], F32, name="term_%d" % d)
-                    pair.append([tt[:, t] for t in range(4)] + [tt])
-                else:
-                    blocks = []
-                    for t in range(4):
-                        tag = "w1b_1_%d" % d if t == 3 else "term_%d_%d" % (t, d)
-                        tt = sb.tile([P, V], F32, name="term_%d_%d" % (t, d), tag=tag, align_bytes=64)
-                        blocks.append(tt)
-                    pair.append(blocks)
-            t01.append(pair)
-            zt = sb.tile([P, V, 4], BF16, name="z_%d" % g, align_bytes=64)
-            zct = sb.tile([P, V], U32, name="zc_%d" % g, align_bytes=64)
-            zst = sb.tile([P, V], U8, name="zs_%d" % g, align_bytes=64)
-            z.append(zt)
-            zc.append(zct)
-            zs.append(zst)
-        out_t = sb.tile([P, V], F32, name="out_t")
+        def cast_w2():
+            nc.vector.tensor_copy(
+                w2b.rearrange("p (g c i t) -> p g c t i", g=2, i=2, t=4), w2_raw[:].rearrange("p g t (c i) -> p g c t i", i=2)
+            )
+            nc.vector.quantize_mx(
+                out=w2c[:].bitcast(FP8X4), scales=w2s[:], in_=w2b
+            )
 
-        def layer1(b):
-            g, t = divmod(b, 4)
+        h = {}
+
+        def layer1(b, banks):
+            ht = sb.tile([P, S], F32, name="h_%d" % b, tag="w1_hi" if b == 3 else "h_%d" % b, align_bytes=64)
+            h[b] = ht
             for half in range(2):
-                n = slice(512 * half, 512 * half + 512)
-                acc = (ps_o if half else ps).tile([P, 512], F32, name="acc_%d" % half)
+                acc = bank[banks[half]]
                 nc.tensor.matmul_mx(
                     out=acc[:],
-                    lhsT=w1c[g][:, P * t : P * t + P].bitcast(FP8X4),
-                    lhsT_scale=w1s[g][:, P * t : P * t + P],
+                    lhsT=w1c[b].bitcast(FP8X4),
+                    lhsT_scale=w1s[b],
                     rhs=xc[half][:].bitcast(FP8X4),
-                    rhs_scale=xs[:, n],
+                    rhs_scale=xs[half][:],
                     start=True,
                     stop=True,
                 )
-                nc.scalar.activation(h[b][:, n], acc[:], COPY)
+                nc.scalar.activation(ht[:, 512 * half : 512 * half + 512], acc[:], COPY)
 
         pos = (pos1_t, pos2_t)
+        term = {}
+        for b in range(4):
+            for d in range(2):
+                term[b, d] = term_lo[b][:, V * d : V * d + V]
+        turned = sb.tile([P, 2, 4, TURN], F32, name="term_turned")
+        rest = V - TURN
+        tail = sb.tile([P, 6 * rest + 2 * V], F32, name="term_added", tag="term_3", align_bytes=64)
+        added = tail[:, 0 : 8 * rest].rearrange("p (t d v) -> p d t v", t=4, d=2)
+        for d in range(2):
+            for t in range(4):
+                term[4 + t, d] = turned[:, d, t]
 
-        def gather_h(b, d, v0, v1):
-            g, t = divmod(b, 4)
-            nc.vector.tensor_tensor(
-                t01[g][d][t][:, v0:v1],
-                h[b][:].indirect(pos[d][:, v0 // 16 : v1 // 16]),
-                gates[:, d, v0:v1],
-                MULT,
+        def gather_h(b, v0, v1):
+            for d in range(2):
+                dst = term[b, d][:, v0:v1] if v0 < TURN else added[:, d, b - 4, v0 - TURN : v1 - TURN]
+                nc.vector.tensor_tensor(
+                    dst,
+                    h[b][:].indirect(pos[d][:, v0 // 16 : v1 // 16]),
+                    gates[:, d, v0:v1],
+                    MULT,
+                )
+
+        def add_turned(dst, b, v):
+            for d in range(2):
+                nc.tensor.matmul(
+                    out=dst, lhsT=term[b, d][:, v : v + P], rhs=ident[:], start=d == 0, stop=d == 1, is_transpose=True
+                )
+
+        zt_lo = sb.tile([P, 4, 2, P, 2], BF16, name="zt_lo", tag="w1b_4", align_bytes=64)
+        zt_hi = sb.tile([P, 3, 2, P, 2], BF16, name="zt_hi", align_bytes=64)
+        z = {(0, 0): tail[:, 6 * rest :].bitcast(BF16).rearrange("p (v t) -> p v t", t=4)}
+        for v0, v1, tag in ((0, 256, "z_1_0"), (256, 384, "z_1_256"), (384, 512, "z_1_0")):
+            zg = sb.tile([P, v1 - v0, 4], BF16, name="z_1_%d" % v0, tag=tag, align_bytes=64)
+            z[1, v0] = zg[:]
+
+        def fold_lo(b, name):
+            sums = bank[name][:].rearrange("p (vb c) -> p vb c", vb=4)
+            for vb in range(4):
+                add_turned(sums[:, vb], b, P * vb)
+            nc.scalar.copy(
+                zt_lo[:, :, :, 32 * b : 32 * b + 32, :], sums.rearrange("p vb (m u e) -> p vb u m e", u=2, e=2)
             )
 
-        def add_z(g, v0, v1):
-            dst = z[g][:, v0:v1, :].rearrange("p (c i) t -> p c t i", i=4)
-            a = t01[g][0][4][:, :, v0:v1].rearrange("p t (c i) -> p c t i", i=4)
-            b = t01[g][1][4][:, :, v0:v1].rearrange("p t (c i) -> p c t i", i=4)
+        def sum_hi(b, vbs, name):
+            sums = bank[name][:].rearrange("p (q e m) -> p q e m", q=2, e=2)
+            for vb in vbs:
+                add_turned(sums[:, vb if vb < 2 else (b - 4) // 2, b % 2], b, P * vb)
+
+        def round_hi(dst, name):
+            nc.scalar.copy(dst, bank[name][:].rearrange("p (q e m) -> p q m e", q=2, e=2))
+
+        def turn_back(zt, vb0, count, dst, name):
+            back = bank[name][:, 0 : 2 * P * count].rearrange("p (u v) -> p u v", u=2)
+            words = zt[:].rearrange("p vb u m e -> p (vb u m e)").bitcast(F32)
+            for vb in range(count):
+                for u in range(2):
+                    w0 = P * (2 * (vb0 + vb) + u)
+                    nc.tensor.transpose(back[:, u, P * vb : P * vb + P], words[:, w0 : w0 + P], ident[:])
+            dst = dst.rearrange("p v t -> p (v t)").bitcast(F32)
+            nc.scalar.copy(dst.rearrange("p (v u) -> p v u", u=2), back.rearrange("p u v -> p v u"))
+
+        def add_z(v0, v1):
+            dst = z[1, v0].rearrange("p (c i) t -> p c t i", i=2)
+            a = added[:, 0, :, v0 - TURN : v1 - TURN].rearrange("p t (c i) -> p c t i", i=2)
+            b = added[:, 1, :, v0 - TURN : v1 - TURN].rearrange("p t (c i) -> p c t i", i=2)
             nc.vector.tensor_tensor(dst, a, b, ADD)
 
-        back = {}
-
-        def fold(b, v0, v1):
-            g, t = divmod(b, 4)
-            sum_t = ps_t.tile([P, v1 - v0], F32, name="sum_t")
-            for v in range(v0, v1, P):
-                for d in range(2):
-                    nc.tensor.matmul(
-                        out=sum_t[:, v - v0 : v - v0 + P],
-                        lhsT=t01[g][d][t][:, v : v + P],
-                        rhs=ident32[:],
-                        start=d == 0,
-                        stop=d == 1,
-                        is_transpose=True,
-                    )
-            z_t = sb.tile([P, v1 - v0], BF16, name="z_t_%d" % b)
-            nc.scalar.activation(z_t[:], sum_t[:], COPY)
-            for v in range(v0, v1, P):
-                key = (g, v // 256)
-                if key not in back:
-                    back[key] = ps_b.tile([P, 4, 256], BF16, name="back")
-                nc.tensor.transpose(back[key][:, t, v % 256 : v % 256 + P], z_t[:, v - v0 : v - v0 + P], ident16[:])
-
-        def weave_z(g, half):
-            nc.scalar.copy(z[g][:, 256 * half : 256 * half + 256, :], back[g, half][:].rearrange("p t v -> p v t"))
+        zc0 = sb.tile([P, V], U32, name="zc_0", tag="h_6", align_bytes=64)
+        zc1 = sb.tile([P, V], U32, name="zc_1", tag="zt_hi", align_bytes=64)
+        zc = (zc0, zc1)
+        zs = []
+        for g in range(2):
+            zsg = sb.tile([P, V], U8, name="zs_%d" % g, align_bytes=64)
+            zs.append(zsg)
 
         def quant_z(g, v0, v1):
             nc.vector.quantize_mx(
                 out=zc[g][:, v0:v1].bitcast(FP8X4),
                 scales=zs[g][:, v0:v1],
-                in_=z[g][:, v0:v1, :].rearrange("p v t -> p (v t)"),
+                in_=z[g, v0].rearrange("p v t -> p (v t)"),
             )
 
-        def layer2(v0, v1):
-            acc = ps_o.tile([P, v1 - v0], F32, name="acc_1")
-            for g in range(2):
+        def layer2(v0, v1, name, order):
+            acc = bank[name][:, 0 : v1 - v0]
+            for g in order:
                 nc.tensor.matmul_mx(
-                    out=acc[:],
+                    out=acc,
                     lhsT=w2c[:, N * g : N * g + N].bitcast(FP8X4),
                     lhsT_scale=w2s[:, N * g : N * g + N],
                     rhs=zc[g][:, v0:v1].bitcast(FP8X4),
                     rhs_scale=zs[g][:, v0:v1],
-                    start=g == 0,
-                    stop=g == 1,
+                    start=g == order[0],
+                    stop=g == order[1],
                 )
-            nc.scalar.activation(out_t[:, v0:v1], acc[:], COPY)
-            nc.sync.dma_start(out[:, v0:v1], out_t[:, v0:v1])
+            out_t = sb.tile([P, v1 - v0], F32, name="out_%d" % v0)
+            nc.scalar.activation(out_t[:], acc, COPY)
+            nc.sync.dma_start(out[:, v0:v1], out_t[:])
 
-        cast_x(0, 0, 512, False)
-        cast_x(0, 512, 1024, True)
-        cast_x(1, 0, 512, False)
-        cast_x(2, 0, 352, False)
-        cast_x(2, 352, 512, True)
+        cast_x(0, 0, 640, False)
+        cast_x(0, 640, 1024, True)
+        cast_x(1, 0, 704, False)
+        cast_x(1, 704, 1024, True)
         gather_x(0, 0, 1024)
-        cast_x(3, 0, 704, True)
-        cast_x(3, 704, 1024, False)
-        cast_x(4, 0, 512, False)
-        cast_x(5, 0, 256, True)
-        cast_x(6, 0, 256, False)
-        gather_x(1, 0, 512)
-        gather_x(1, 512, 1024)
-        cast_w1(0, 0)
-        cast_w1(0, 1)
-        cast_w1(1, 0)
-        cast_w1(1, 1)
-        quant_x(0, 512)
-        quant_w1(0, 0, 1)
-        quant_x(512, 1024)
-        layer1(0)
-        quant_w1(0, 1, 2)
-        quant_w1(0, 2, 4)
-        layer1(1)
-        nc.vector.tensor_copy(w2b[:], w2_raw[:].rearrange("p g t n -> p g n t"))
-        layer1(2)
-        layer1(3)
-        cast_w1(2, 0)
-        cast_w1(3, 0)
-        cast_w1(2, 1)
-        cast_w1(3, 1)
-        gather_h(0, 0, 0, V)
-        gather_h(0, 1, 0, V)
-        nc.vector.quantize_mx(
-            out=w2c[:].bitcast(FP8X4), scales=w2s[:], in_=w2b[:].rearrange("p g n t -> p (g n t)")
-        )
-        gather_h(1, 0, 0, V)
-        gather_h(1, 1, 0, V)
-        fold(0, 0, V)
-        gather_h(2, 0, 0, V)
-        gather_h(2, 1, 0, V)
-        quant_w1(1, 0, 1)
-        layer1(4)
-        fold(1, 0, V)
-        gather_h(3, 0, 0, V)
-        quant_w1(1, 1, 2)
-        quant_w1(1, 2, 4)
-        gather_h(3, 1, 0, V)
-        layer1(5)
-        fold(2, 0, V)
-        gather_h(4, 0, 0, V)
-        gather_h(4, 1, 0, V)
-        layer1(6)
-        fold(3, 0, V)
-        gather_h(5, 0, 0, V)
-        gather_h(5, 1, 0, V)
-        layer1(7)
-        fold(4, 0, 256)
-        fold(5, 0, 256)
-        weave_z(0, 0)
-        weave_z(0, 1)
-        gather_h(6, 0, 0, 256)
-        gather_h(6, 1, 0, 256)
-        fold(6, 0, 256)
-        gather_h(7, 0, 0, 256)
-        gather_h(7, 1, 0, 256)
-        fold(7, 0, 256)
-        weave_z(1, 0)
+        cast_x(2, 0, 768, True)
+        cast_x(2, 768, 1024, False)
+        cast_x(3, 0, 512, False)
+        cast_x(3, 512, 768, True)
+        cast_x(4, 0, 160, False)
+        cast_x(4, 160, 256, True)
+        for n0 in range(0, S, 256):
+            gather_x(1, n0, n0 + 256)
+            weave_x(n0, n0 + 256)
+        cast_w1_lo(0)
+        cast_w1_lo(1)
+        cast_w1_lo(2)
+        quant_x(0, "xc_0")
+        quant_w1(0, "w1c_0")
+        quant_x(1, "w1b_0")
+        quant_w1(1, "w1c_1")
+        quant_w1(2, "w1b_1")
+        cast_w1_lo(3)
+        quant_w1(3, "w1c_3")
+        cast_w2()
+        layer1(0, "AB")
+        layer1(1, "CD")
+        layer1(2, "AB")
+        cast_w1_hi(0)
+        cast_w1_hi(1)
+        quant_w1(4, "w1c_4")
+        quant_w1(6, "w1c_6")
+        layer1(3, "CD")
+        layer1(4, "EF")
+        layer1(5, "GH")
+        layer1(6, "BD")
+        layer1(7, "FH")
+        gather_h(0, 0, V)
+        fold_lo(0, "A")
+        gather_h(1, 0, V)
+        fold_lo(1, "C")
+        gather_h(2, 0, V)
+        fold_lo(2, "B")
+        gather_h(3, 0, V)
+        fold_lo(3, "F")
+        turn_back(zt_lo, 0, 2, z[0, 0][:, 0:256], "A")
+        turn_back(zt_lo, 2, 2, z[0, 0][:, 256:512], "C")
+        gather_h(4, 0, TURN)
+        gather_h(5, 0, TURN)
+        sum_hi(4, (0, 1), "F")
+        sum_hi(5, (0, 1), "F")
+        round_hi(zt_hi[:, 0:2, 0], "F")
+        sum_hi(4, (2,), "C")
+        sum_hi(5, (2,), "C")
+        gather_h(6, 0, TURN)
+        sum_hi(6, (0, 1), "A")
+        sum_hi(6, (2,), "C")
+        gather_h(7, 0, TURN)
+        sum_hi(7, (0, 1), "A")
+        sum_hi(7, (2,), "C")
+        round_hi(zt_hi[:, 0:2, 1], "A")
+        round_hi(zt_hi[:, 2], "C")
+        turn_back(zt_hi, 0, 2, z[1, 0], "E")
+        turn_back(zt_hi, 2, 1, z[1, 256], "G")
+        gather_h(4, TURN, V)
+        gather_h(5, TURN, V)
+        gather_h(6, TURN, V)
         quant_z(0, 0, 512)
-        gather_h(6, 0, 256, 512)
-        gather_h(6, 1, 256, 512)
-        gather_h(7, 0, 256, 512)
-        gather_h(7, 1, 256, 512)
-        add_z(1, 256, 384)
-        add_z(1, 384, 512)
+        gather_h(7, TURN, V)
         quant_z(1, 0, 256)
-        layer2(0, 256)
+        layer2(0, 256, "D", (1, 0))
+        add_z(384, 512)
         quant_z(1, 256, 384)
-        layer2(256, 384)
+        layer2(256, 384, "H", (1, 0))
         quant_z(1, 384, 512)
-        layer2(384, 512)
+        layer2(384, 512, "G", (0, 1))

@@ -24,6 +24,7 @@ def tile_picked_sage_none_e_kernel(tc, xT, w1, w2, gate, offs, pos1, pos2, out):
     with ExitStack() as ctx:
         lists = ctx.enter_context(tc.tile_pool(name="lists", bufs=1))
         sb = ctx.enter_context(tc.tile_pool(name="sb", bufs=1))
+        shared = ctx.enter_context(tc.tile_pool(name="shared", bufs=1))
         ps = ctx.enter_context(tc.psum_pool(name="ps", bufs=1))
 
         offs_t = lists.tile([P, S // 16], U16, name="offs_t")
@@ -62,18 +63,19 @@ def tile_picked_sage_none_e_kernel(tc, xT, w1, w2, gate, offs, pos1, pos2, out):
         nc.sync.dma_start(pos2_t[:], pos2)
         gates = sb.tile([P, 2, V], F32, name="gates")
         nc.sync.dma_start(gates[:], gate.rearrange("d p v -> p d v"))
-        w1_hi = sb.tile([P, 4, 512], F32, name="w1_hi", align_bytes=64)
+        w1_hi = shared.tile([P, 4, 512], F32, name="w1_hi", offset=0)
         nc.sync.dma_start(w1_hi[:], w1_view[:, :, 512:1024])
 
         pairs = []
         for u in range(2):
             pt = sb.tile([P, T, 2], BF16, name="pairs_%d" % u)
             pairs.append(pt)
-        picked = []
+        picked, fetched = [], []
         for half in range(2):
             pk = sb.tile([P, 4 * 512], BF16, name="picked_%d" % half, align_bytes=64)
             picked.append(pk)
-        fetched = sb.tile([P, 2, S], U32, name="fetched")
+            ft = sb.tile([P, 2, 512], U32, name="fetched_%d" % half, align_bytes=64)
+            fetched.append(ft)
 
         def cast_x(i, a, b, scalar):
             u, c0, raw = x_raw[i]
@@ -86,16 +88,18 @@ def tile_picked_sage_none_e_kernel(tc, xT, w1, w2, gate, offs, pos1, pos2, out):
 
         def gather_x(u, n0, n1):
             window = pairs[u][:].rearrange("p t e -> p (t e)").bitcast(U32)
-            nc.vector.tensor_copy(fetched[:, u, n0:n1], window.indirect(offs_t[:, n0 // 16 : n1 // 16]))
+            dst = fetched[n0 // 512][:, u, n0 % 512 : n0 % 512 + n1 - n0]
+            nc.vector.tensor_copy(dst, window.indirect(offs_t[:, n0 // 16 : n1 // 16]))
 
         def weave_x(n0, n1):
             words = picked[n0 // 512][:].bitcast(U32).rearrange("p (n u) -> p n u", u=2)
-            nc.scalar.copy(words[:, n0 % 512 : n0 % 512 + n1 - n0], fetched[:, :, n0:n1].rearrange("p u n -> p n u"))
+            cols = slice(n0 % 512, n0 % 512 + n1 - n0)
+            nc.scalar.copy(words[:, cols], fetched[n0 // 512][:, :, cols].rearrange("p u n -> p n u"))
 
         xc, xs = [], []
 
-        def quant_x(half, tag):
-            codes = sb.tile([P, 512], U32, name="xc_%d" % half, tag=tag, align_bytes=64)
+        def quant_x(half):
+            codes = sb.tile([P, 512], U32, name="xc_%d" % half, align_bytes=64)
             scales = sb.tile([P, 512], U8, name="xs_%d" % half, align_bytes=64)
             nc.vector.quantize_mx(
                 out=codes[:].bitcast(FP8X4),
@@ -107,19 +111,22 @@ def tile_picked_sage_none_e_kernel(tc, xT, w1, w2, gate, offs, pos1, pos2, out):
 
         term_lo = []
         for b in range(4):
-            lo = sb.tile([P, 2 * V], F32, name="term_%d" % b, tag="picked_1" if b == 0 else "term_%d" % b, align_bytes=64)
+            if b == 2:
+                lo = shared.tile([P, 2 * V], F32, name="term_2", offset=4 * S)
+            else:
+                lo = sb.tile([P, 2 * V], F32, name="term_%d" % b, tag="term_%d" % b if b else "fetched_1", align_bytes=64)
             term_lo.append(lo)
 
         w1b, w1c, w1s = {}, {}, {}
 
         def cast_w1_lo(b):
             if b == 3:
-                wide = term_lo[0][:, 0:256].bitcast(BF16)
+                wide = term_lo[0][:, 512:768].bitcast(BF16)
             else:
                 own = sb.tile([P, 4 * P], BF16, name="w1b_%d" % b, align_bytes=64)
                 wide = own[:]
-            dst = wide.rearrange("p (c i j) -> p c j i", i=2, j=4)
-            src = w1_lo[b // 2][:, :, P * (b % 2) : P * (b % 2) + P].rearrange("p j (c i) -> p c j i", i=2)
+            dst = wide.rearrange("p (c i j) -> p c j i", i=4, j=4)
+            src = w1_lo[b // 2][:, :, P * (b % 2) : P * (b % 2) + P].rearrange("p j (c i) -> p c j i", i=4)
             if b in (0, 3):
                 nc.vector.tensor_copy(dst, src)
             else:
@@ -127,17 +134,15 @@ def tile_picked_sage_none_e_kernel(tc, xT, w1, w2, gate, offs, pos1, pos2, out):
             w1b[b] = (wide, 1)
 
         def cast_w1_hi(u):
-            if u == 0:
-                own = sb.tile([P, 8 * P], BF16, name="w1b_4", align_bytes=64)
-                wide = own[:]
-            else:
-                wide = term_lo[2][:, 256:768].bitcast(BF16)
+            own = sb.tile([P, 8 * P], BF16, name="w1b_%d" % (4 + 2 * u), align_bytes=64)
+            wide = own[:]
             src = w1_hi[:].rearrange("p j (m t) -> p m j t", t=4)[:, :, :, 2 * u : 2 * u + 2]
             nc.scalar.activation(wide.rearrange("p (e m j) -> p m j e", e=2, j=4), src, COPY)
             w1b[4 + 2 * u] = (wide, 2)
 
-        def quant_w1(b0, tag):
+        def quant_w1(b0):
             wide, blocks = w1b[b0]
+            tag = "w1c_%d" % b0 if b0 else "fetched_0"
             codes = sb.tile([P, P * blocks], U32, name="w1c_%d" % b0, tag=tag, align_bytes=64)
             scales = sb.tile([P, P * blocks], U8, name="w1s_%d" % b0, align_bytes=64)
             nc.vector.quantize_mx(out=codes[:].bitcast(FP8X4), scales=scales[:], in_=wide)
@@ -145,22 +150,25 @@ def tile_picked_sage_none_e_kernel(tc, xT, w1, w2, gate, offs, pos1, pos2, out):
                 w1c[b0 + i] = codes[:, P * i : P * i + P]
                 w1s[b0 + i] = scales[:, P * i : P * i + P]
 
-        w2b = term_lo[0][:, 256:768].bitcast(BF16)
+        w2b = term_lo[0][:, 0:512].bitcast(BF16)
         w2c = sb.tile([P, 2 * N], U32, name="w2c", align_bytes=64)
         w2s = sb.tile([P, 2 * N], U8, name="w2s", align_bytes=64)
 
         def cast_w2():
             nc.vector.tensor_copy(
-                w2b.rearrange("p (g c i t) -> p g c t i", g=2, i=2, t=4), w2_raw[:].rearrange("p g t (c i) -> p g c t i", i=2)
+                w2b.rearrange("p (g c i t) -> p g c t i", g=2, i=4, t=4), w2_raw[:].rearrange("p g t (c i) -> p g c t i", i=4)
             )
-            nc.vector.quantize_mx(
-                out=w2c[:].bitcast(FP8X4), scales=w2s[:], in_=w2b
-            )
+
+        def quant_w2():
+            nc.vector.quantize_mx(out=w2c[:].bitcast(FP8X4), scales=w2s[:], in_=w2b)
 
         h = {}
 
         def layer1(b, banks):
-            ht = sb.tile([P, S], F32, name="h_%d" % b, tag="w1_hi" if b == 3 else "h_%d" % b, align_bytes=64)
+            if b == 3:
+                ht = shared.tile([P, S], F32, name="h_3", offset=0)
+            else:
+                ht = sb.tile([P, S], F32, name="h_%d" % b)
             h[b] = ht
             for half in range(2):
                 acc = bank[banks[half]]
@@ -180,13 +188,11 @@ def tile_picked_sage_none_e_kernel(tc, xT, w1, w2, gate, offs, pos1, pos2, out):
         for b in range(4):
             for d in range(2):
                 term[b, d] = term_lo[b][:, V * d : V * d + V]
-        turned = sb.tile([P, 2, 4, TURN], F32, name="term_turned")
-        rest = V - TURN
-        tail = sb.tile([P, 6 * rest + 2 * V], F32, name="term_added", tag="term_3", align_bytes=64)
-        added = tail[:, 0 : 8 * rest].rearrange("p (t d v) -> p d t v", t=4, d=2)
+        turned = sb.tile([P, 2, 4 * TURN], F32, name="term_turned")
+        added = turned[:, :, TURN - P : 2 * TURN].rearrange("p d (t v) -> p d t v", t=4)
         for d in range(2):
             for t in range(4):
-                term[4 + t, d] = turned[:, d, t]
+                term[4 + t, d] = turned[:, d, TURN * t : TURN * t + TURN]
 
         def gather_h(b, v0, v1):
             for d in range(2):
@@ -206,10 +212,11 @@ def tile_picked_sage_none_e_kernel(tc, xT, w1, w2, gate, offs, pos1, pos2, out):
 
         zt_lo = sb.tile([P, 4, 2, P, 2], BF16, name="zt_lo", tag="w1b_4", align_bytes=64)
         zt_hi = sb.tile([P, 3, 2, P, 2], BF16, name="zt_hi", align_bytes=64)
-        z = {(0, 0): tail[:, 6 * rest :].bitcast(BF16).rearrange("p (v t) -> p v t", t=4)}
-        for v0, v1, tag in ((0, 256, "z_1_0"), (256, 384, "z_1_256"), (384, 512, "z_1_0")):
-            zg = sb.tile([P, v1 - v0, 4], BF16, name="z_1_%d" % v0, tag=tag, align_bytes=64)
-            z[1, v0] = zg[:]
+        z = {}
+        for g, v0, v1 in ((0, 0, 512), (1, 0, 256), (1, 256, 384), (1, 384, 512)):
+            tag = "z_%d_%d" % (g, 0 if v1 == V else v0)
+            zg = sb.tile([P, v1 - v0, 4], BF16, name="z_%d_%d" % (g, v0), tag=tag, align_bytes=64)
+            z[g, v0] = zg[:]
 
         def fold_lo(b, name):
             sums = bank[name][:].rearrange("p (vb c) -> p vb c", vb=4)
@@ -238,12 +245,12 @@ def tile_picked_sage_none_e_kernel(tc, xT, w1, w2, gate, offs, pos1, pos2, out):
             nc.scalar.copy(dst.rearrange("p (v u) -> p v u", u=2), back.rearrange("p u v -> p v u"))
 
         def add_z(v0, v1):
-            dst = z[1, v0].rearrange("p (c i) t -> p c t i", i=2)
-            a = added[:, 0, :, v0 - TURN : v1 - TURN].rearrange("p t (c i) -> p c t i", i=2)
-            b = added[:, 1, :, v0 - TURN : v1 - TURN].rearrange("p t (c i) -> p c t i", i=2)
+            dst = z[1, v0].rearrange("p (c i) t -> p c t i", i=4)
+            a = added[:, 0, :, v0 - TURN : v1 - TURN].rearrange("p t (c i) -> p c t i", i=4)
+            b = added[:, 1, :, v0 - TURN : v1 - TURN].rearrange("p t (c i) -> p c t i", i=4)
             nc.vector.tensor_tensor(dst, a, b, ADD)
 
-        zc0 = sb.tile([P, V], U32, name="zc_0", tag="h_6", align_bytes=64)
+        zc0 = sb.tile([P, V], U32, name="zc_0", align_bytes=64)
         zc1 = sb.tile([P, V], U32, name="zc_1", tag="zt_hi", align_bytes=64)
         zc = (zc0, zc1)
         zs = []
@@ -278,7 +285,8 @@ def tile_picked_sage_none_e_kernel(tc, xT, w1, w2, gate, offs, pos1, pos2, out):
         cast_x(0, 640, 1024, True)
         cast_x(1, 0, 704, False)
         cast_x(1, 704, 1024, True)
-        gather_x(0, 0, 1024)
+        gather_x(0, 0, 512)
+        gather_x(0, 512, 1024)
         cast_x(2, 0, 768, True)
         cast_x(2, 768, 1024, False)
         cast_x(3, 0, 512, False)
@@ -291,21 +299,22 @@ def tile_picked_sage_none_e_kernel(tc, xT, w1, w2, gate, offs, pos1, pos2, out):
         cast_w1_lo(0)
         cast_w1_lo(1)
         cast_w1_lo(2)
-        quant_x(0, "xc_0")
-        quant_w1(0, "w1c_0")
-        quant_x(1, "w1b_0")
-        quant_w1(1, "w1c_1")
-        quant_w1(2, "w1b_1")
-        cast_w1_lo(3)
-        quant_w1(3, "w1c_3")
+        quant_x(0)
+        quant_w1(0)
+        quant_x(1)
         cast_w2()
+        cast_w1_lo(3)
+        quant_w2()
+        quant_w1(1)
+        quant_w1(2)
+        quant_w1(3)
         layer1(0, "AB")
         layer1(1, "CD")
         layer1(2, "AB")
         cast_w1_hi(0)
         cast_w1_hi(1)
-        quant_w1(4, "w1c_4")
-        quant_w1(6, "w1c_6")
+        quant_w1(4)
+        quant_w1(6)
         layer1(3, "CD")
         layer1(4, "EF")
         layer1(5, "GH")
@@ -338,10 +347,10 @@ def tile_picked_sage_none_e_kernel(tc, xT, w1, w2, gate, offs, pos1, pos2, out):
         round_hi(zt_hi[:, 2], "C")
         turn_back(zt_hi, 0, 2, z[1, 0], "E")
         turn_back(zt_hi, 2, 1, z[1, 256], "G")
-        gather_h(4, TURN, V)
         gather_h(5, TURN, V)
         gather_h(6, TURN, V)
         quant_z(0, 0, 512)
+        gather_h(4, TURN, V)
         gather_h(7, TURN, V)
         quant_z(1, 0, 256)
         layer2(0, 256, "D", (1, 0))

@@ -14,7 +14,6 @@ U32 = mybir.dt.uint32
 U16 = mybir.dt.uint16
 U8 = mybir.dt.uint8
 FP8X4 = mybir.dt.float8_e4m3fn_x4
-COPY = mybir.ActivationFunctionType.Copy
 MULT = mybir.AluOpType.mult
 ADD = mybir.AluOpType.add
 
@@ -31,10 +30,6 @@ def tile_picked_sage_none_e_kernel(tc, xT, w1, w2, gate, offs, pos1, pos2, out):
         pos1_t = lists.tile([P, V // 16], U16, name="pos1_t")
         pos2_t = lists.tile([P, V // 16], U16, name="pos2_t")
 
-        warm = sb.tile([P, 1], F32, name="warm")
-        warm_out = sb.tile([P, 1], F32, name="warm_out")
-        nc.gpsimd.memset(warm[:], 0.0)
-        nc.scalar.activation(warm_out[:], warm[:], COPY)
         ident = sb.tile([P, P], F32, name="ident")
         make_identity(nc, ident[:])
 
@@ -82,7 +77,7 @@ def tile_picked_sage_none_e_kernel(tc, xT, w1, w2, gate, offs, pos1, pos2, out):
             dst = pairs[u][:, c0 + a : c0 + b, :]
             src = raw[:, :, a:b].rearrange("p e t -> p t e")
             if scalar:
-                nc.scalar.activation(dst, src, COPY)
+                nc.scalar.copy(dst, src)
             else:
                 nc.vector.tensor_copy(dst, src)
 
@@ -130,14 +125,14 @@ def tile_picked_sage_none_e_kernel(tc, xT, w1, w2, gate, offs, pos1, pos2, out):
             if b in (0, 3):
                 nc.vector.tensor_copy(dst, src)
             else:
-                nc.scalar.activation(dst, src, COPY)
+                nc.scalar.copy(dst, src)
             w1b[b] = (wide, 1)
 
         def cast_w1_hi(u):
             own = sb.tile([P, 8 * P], BF16, name="w1b_%d" % (4 + 2 * u), align_bytes=64)
             wide = own[:]
             src = w1_hi[:].rearrange("p j (m t) -> p m j t", t=4)[:, :, :, 2 * u : 2 * u + 2]
-            nc.scalar.activation(wide.rearrange("p (e m j) -> p m j e", e=2, j=4), src, COPY)
+            nc.scalar.copy(wide.rearrange("p (e m j) -> p m j e", e=2, j=4), src)
             w1b[4 + 2 * u] = (wide, 2)
 
         def quant_w1(b0):
@@ -181,7 +176,7 @@ def tile_picked_sage_none_e_kernel(tc, xT, w1, w2, gate, offs, pos1, pos2, out):
                     start=True,
                     stop=True,
                 )
-                nc.scalar.activation(ht[:, 512 * half : 512 * half + 512], acc[:], COPY)
+                nc.scalar.copy(ht[:, 512 * half : 512 * half + 512], acc[:])
 
         pos = (pos1_t, pos2_t)
         term = {}
@@ -214,7 +209,7 @@ def tile_picked_sage_none_e_kernel(tc, xT, w1, w2, gate, offs, pos1, pos2, out):
         zt_hi = sb.tile([P, 3, 2, P, 2], BF16, name="zt_hi", align_bytes=64)
         z = {}
         for g, v0, v1 in ((0, 0, 512), (1, 0, 256), (1, 256, 384), (1, 384, 512)):
-            tag = "z_%d_%d" % (g, 0 if v1 == V else v0)
+            tag = "zt_hi" if v0 == TURN else "z_%d_%d" % (g, v0)
             zg = sb.tile([P, v1 - v0, 4], BF16, name="z_%d_%d" % (g, v0), tag=tag, align_bytes=64)
             z[g, v0] = zg[:]
 
@@ -226,13 +221,13 @@ def tile_picked_sage_none_e_kernel(tc, xT, w1, w2, gate, offs, pos1, pos2, out):
                 zt_lo[:, :, :, 32 * b : 32 * b + 32, :], sums.rearrange("p vb (m u e) -> p vb u m e", u=2, e=2)
             )
 
-        def sum_hi(b, vbs, name):
+        def sum_hi(b, vb, name, slot):
             sums = bank[name][:].rearrange("p (q e m) -> p q e m", q=2, e=2)
-            for vb in vbs:
-                add_turned(sums[:, vb if vb < 2 else (b - 4) // 2, b % 2], b, P * vb)
+            add_turned(sums[:, slot, b % 2], b, P * vb)
 
-        def round_hi(dst, name):
-            nc.scalar.copy(dst, bank[name][:].rearrange("p (q e m) -> p q m e", q=2, e=2))
+        def round_hi(dst, name, slots):
+            sums = bank[name][:].rearrange("p (q e m) -> p q m e", q=2, e=2)
+            nc.scalar.copy(dst, sums[:, 0:slots])
 
         def turn_back(zt, vb0, count, dst, name):
             back = bank[name][:, 0 : 2 * P * count].rearrange("p (u v) -> p u v", u=2)
@@ -251,7 +246,7 @@ def tile_picked_sage_none_e_kernel(tc, xT, w1, w2, gate, offs, pos1, pos2, out):
             nc.vector.tensor_tensor(dst, a, b, ADD)
 
         zc0 = sb.tile([P, V], U32, name="zc_0", align_bytes=64)
-        zc1 = sb.tile([P, V], U32, name="zc_1", tag="zt_hi", align_bytes=64)
+        zc1 = sb.tile([P, V], U32, name="zc_1", align_bytes=64)
         zc = (zc0, zc1)
         zs = []
         for g in range(2):
@@ -278,7 +273,7 @@ def tile_picked_sage_none_e_kernel(tc, xT, w1, w2, gate, offs, pos1, pos2, out):
                     stop=g == order[1],
                 )
             out_t = sb.tile([P, v1 - v0], F32, name="out_%d" % v0)
-            nc.scalar.activation(out_t[:], acc, COPY)
+            nc.scalar.copy(out_t[:], acc)
             nc.sync.dma_start(out[:, v0:v1], out_t[:])
 
         cast_x(0, 0, 640, False)
@@ -302,12 +297,12 @@ def tile_picked_sage_none_e_kernel(tc, xT, w1, w2, gate, offs, pos1, pos2, out):
         quant_x(0)
         quant_w1(0)
         quant_x(1)
-        cast_w2()
         cast_w1_lo(3)
-        quant_w2()
         quant_w1(1)
-        quant_w1(2)
+        cast_w2()
         quant_w1(3)
+        quant_w2()
+        quant_w1(2)
         layer1(0, "AB")
         layer1(1, "CD")
         layer1(2, "AB")
@@ -332,20 +327,22 @@ def tile_picked_sage_none_e_kernel(tc, xT, w1, w2, gate, offs, pos1, pos2, out):
         turn_back(zt_lo, 2, 2, z[0, 0][:, 256:512], "C")
         gather_h(4, 0, TURN)
         gather_h(5, 0, TURN)
-        sum_hi(4, (0, 1), "F")
-        sum_hi(5, (0, 1), "F")
-        round_hi(zt_hi[:, 0:2, 0], "F")
-        sum_hi(4, (2,), "C")
-        sum_hi(5, (2,), "C")
-        gather_h(6, 0, TURN)
-        sum_hi(6, (0, 1), "A")
-        sum_hi(6, (2,), "C")
-        gather_h(7, 0, TURN)
-        sum_hi(7, (0, 1), "A")
-        sum_hi(7, (2,), "C")
-        round_hi(zt_hi[:, 0:2, 1], "A")
-        round_hi(zt_hi[:, 2], "C")
-        turn_back(zt_hi, 0, 2, z[1, 0], "E")
+        for b in (4, 5):
+            for vb in range(2):
+                sum_hi(b, vb, "F", vb)
+        round_hi(zt_hi[:, 0:2, 0], "F", 2)
+        sum_hi(4, 2, "C", 0)
+        sum_hi(5, 2, "C", 0)
+        for b in (6, 7):
+            gather_h(b, 0, TURN)
+            sum_hi(b, 0, "A", 0)
+            sum_hi(b, 1, "F", 0)
+            sum_hi(b, 2, "C", 1)
+        round_hi(zt_hi[:, 0:1, 1], "A", 1)
+        round_hi(zt_hi[:, 1:2, 1], "F", 1)
+        turn_back(zt_hi, 0, 1, z[1, 0][:, 0:P], "E")
+        turn_back(zt_hi, 1, 1, z[1, 0][:, P : 2 * P], "G")
+        round_hi(zt_hi[:, 2], "C", 2)
         turn_back(zt_hi, 2, 1, z[1, 256], "G")
         gather_h(5, TURN, V)
         gather_h(6, TURN, V)
@@ -353,9 +350,9 @@ def tile_picked_sage_none_e_kernel(tc, xT, w1, w2, gate, offs, pos1, pos2, out):
         gather_h(4, TURN, V)
         gather_h(7, TURN, V)
         quant_z(1, 0, 256)
-        layer2(0, 256, "D", (1, 0))
+        layer2(0, 256, "E", (0, 1))
         add_z(384, 512)
         quant_z(1, 256, 384)
-        layer2(256, 384, "H", (1, 0))
+        layer2(256, 384, "G", (0, 1))
         quant_z(1, 384, 512)
-        layer2(384, 512, "G", (0, 1))
+        layer2(384, 512, "F", (0, 1))

@@ -312,17 +312,17 @@ def tile_picked_sage_none_e_kernel(tc, xT, w1, w2, gate, offs, pos1, pos2, out):
         quant_w1(6)
         layer1(3, "CD")
         layer1(4, "EF")
-        layer1(5, "GH")
-        layer1(6, "BD")
-        layer1(7, "FH")
         gather_h(0, 0, V)
         fold_lo(0, "A")
         gather_h(1, 0, V)
         fold_lo(1, "C")
+        layer1(5, "GH")
         gather_h(2, 0, V)
-        fold_lo(2, "B")
+        fold_lo(2, "A")
+        layer1(6, "BD")
         gather_h(3, 0, V)
-        fold_lo(3, "F")
+        fold_lo(3, "C")
+        layer1(7, "FH")
         turn_back(zt_lo, 0, 2, z[0, 0][:, 0:256], "A")
         turn_back(zt_lo, 2, 2, z[0, 0][:, 256:512], "C")
         gather_h(4, 0, TURN)

@@ -6,6 +6,7 @@ from concourse.masks import make_identity
 K, T, S, V, H, N = 512, 2048, 1024, 512, 1024, 128
 P = 128
 TURN = 384
+PLAIN = 4
 FLOPS = 2 * K * H * S + 2 * H * N * V
 
 F32 = mybir.dt.float32
@@ -16,6 +17,7 @@ U8 = mybir.dt.uint8
 FP8X4 = mybir.dt.float8_e4m3fn_x4
 MULT = mybir.AluOpType.mult
 ADD = mybir.AluOpType.add
+COPY = mybir.ActivationFunctionType.Copy
 
 
 def tile_picked_sage_none_e_kernel(tc, xT, w1, w2, gate, offs, pos1, pos2, out):
@@ -33,6 +35,10 @@ def tile_picked_sage_none_e_kernel(tc, xT, w1, w2, gate, offs, pos1, pos2, out):
         ident = sb.tile([P, P], F32, name="ident")
         make_identity(nc, ident[:])
 
+        warm = sb.tile([P, 2], F32, name="warm")
+        nc.vector.memset(warm[:, 0:1], 0.0)
+        nc.scalar.activation(warm[:, 1:2], warm[:, 0:1], COPY)
+
         bank = {}
         for name in "ABCDEFGH":
             whole = ps.tile([P, 512], F32, name="bank_" + name)
@@ -40,92 +46,91 @@ def tile_picked_sage_none_e_kernel(tc, xT, w1, w2, gate, offs, pos1, pos2, out):
 
         x_view = xT.rearrange("(p j) t -> p j t", j=4)
         x_raw = []
-        for u, c0, c1 in ((0, 0, 1024), (0, 1024, 2048), (1, 0, 1024), (1, 1024, 1792), (1, 1792, 2048)):
-            raw = sb.tile([P, 2, c1 - c0], F32, name="x_raw_%d_%d" % (u, c0))
-            nc.sync.dma_start(raw[:], x_view[:, 2 * u : 2 * u + 2, c0:c1])
-            x_raw.append((u, c0, raw))
-            if len(x_raw) == 1:
+        for j in range(4):
+            raw = sb.tile([P, T], F32, name="x_raw_%d" % j)
+            nc.sync.dma_start(raw[:], x_view[:, j, :])
+            x_raw.append(raw)
+            if j == 0:
                 nc.sync.dma_start(offs_t[:], offs)
-        w1_view = w1.rearrange("(p j) i -> p j i", j=4)
-        w1_lo = []
-        for piece in range(2):
-            raw = sb.tile([P, 4, 256], F32, name="w1_lo_%d" % piece)
-            nc.sync.dma_start(raw[:], w1_view[:, :, 256 * piece : 256 * piece + 256])
-            w1_lo.append(raw)
-        w2_raw = sb.tile([P, 2, 4, N], F32, name="w2_raw")
-        nc.sync.dma_start(w2_raw[:], w2.rearrange("(g p t) n -> p g t n", g=2, t=4))
         nc.sync.dma_start(pos1_t[:], pos1)
         nc.sync.dma_start(pos2_t[:], pos2)
+        w1_view = w1.rearrange("(p j) i -> p j i", j=4)
+        w1_lo = []
         gates = sb.tile([P, 2, V], F32, name="gates")
-        nc.sync.dma_start(gates[:], gate.rearrange("d p v -> p d v"))
+        for b0, b1 in ((0, 2), (2, 4)):
+            raw = sb.tile([P, 4, P * (b1 - b0)], F32, name="w1_lo_%d" % b0, align_bytes=64)
+            nc.sync.dma_start(raw[:], w1_view[:, :, P * b0 : P * b1])
+            w1_lo.extend(raw[:, :, P * i : P * i + P] for i in range(b1 - b0))
+        for d in range(2):
+            nc.sync.dma_start(gates[:, d, :], gate[d])
         w1_hi = shared.tile([P, 4, 512], F32, name="w1_hi", offset=0)
         nc.sync.dma_start(w1_hi[:], w1_view[:, :, 512:1024])
+        w2_raw = sb.tile([P, 2, 4, N], F32, name="w2_raw")
+        nc.sync.dma_start(w2_raw[:], w2.rearrange("(g p t) n -> p g t n", g=2, t=4))
 
-        pairs = []
-        for u in range(2):
-            pt = sb.tile([P, T, 2], BF16, name="pairs_%d" % u)
-            pairs.append(pt)
-        picked, fetched = [], []
+        picked = []
         for half in range(2):
             pk = sb.tile([P, 4 * 512], BF16, name="picked_%d" % half, align_bytes=64)
             picked.append(pk)
-            ft = sb.tile([P, 2, 512], U32, name="fetched_%d" % half, align_bytes=64)
-            fetched.append(ft)
 
-        def cast_x(i, a, b, scalar):
-            u, c0, raw = x_raw[i]
-            dst = pairs[u][:, c0 + a : c0 + b, :]
-            src = raw[:, :, a:b].rearrange("p e t -> p t e")
-            if scalar:
-                nc.scalar.copy(dst, src)
+        def slots(n0, n1):
+            return picked[n0 // 512][:].rearrange("p (n t) -> p n t", t=4)[:, n0 % 512 : n0 % 512 + n1 - n0]
+
+        def looked_up(j, n0, n1):
+            return x_raw[j][:].indirect(offs_t[:, n0 // 16 : n1 // 16])
+
+        fetched = {}
+
+        def gather_x(j, q):
+            if q:
+                ft = sb.tile([P, 256], BF16, name="fetched_%d_%d" % (j, q), align_bytes=64)
+                nc.scalar.activation(ft[:], looked_up(j, 256 * q, 256 * q + 256), COPY)
+                fetched[j, q] = ft
             else:
-                nc.vector.tensor_copy(dst, src)
+                nc.vector.tensor_copy(slots(0, 256)[:, :, j], looked_up(j, 0, 256))
 
-        def gather_x(u, n0, n1):
-            window = pairs[u][:].rearrange("p t e -> p (t e)").bitcast(U32)
-            dst = fetched[n0 // 512][:, u, n0 % 512 : n0 % 512 + n1 - n0]
-            nc.vector.tensor_copy(dst, window.indirect(offs_t[:, n0 // 16 : n1 // 16]))
-
-        def weave_x(n0, n1):
-            words = picked[n0 // 512][:].bitcast(U32).rearrange("p (n u) -> p n u", u=2)
-            cols = slice(n0 % 512, n0 % 512 + n1 - n0)
-            nc.scalar.copy(words[:, cols], fetched[n0 // 512][:, :, cols].rearrange("p u n -> p n u"))
+        def place_x(j, q):
+            nc.vector.tensor_copy(slots(256 * q, 256 * q + 256)[:, :, j], fetched[j, q][:])
 
         xc, xs = [], []
-
-        def quant_x(half):
-            codes = sb.tile([P, 512], U32, name="xc_%d" % half, align_bytes=64)
+        for half in range(2):
+            codes = sb.tile([P, 512], U32, name="xc_%d" % half, tag="w1_lo_0" if half else "xc_0", align_bytes=64)
             scales = sb.tile([P, 512], U8, name="xs_%d" % half, align_bytes=64)
-            nc.vector.quantize_mx(
-                out=codes[:].bitcast(FP8X4),
-                scales=scales[:],
-                in_=picked[half][:],
-            )
             xc.append(codes)
             xs.append(scales)
+
+        def quant_x(n0, n1):
+            cols = slice(n0 % 512, n0 % 512 + n1 - n0)
+            nc.vector.quantize_mx(
+                out=xc[n0 // 512][:, cols].bitcast(FP8X4),
+                scales=xs[n0 // 512][:, cols],
+                in_=picked[n0 // 512][:, 4 * cols.start : 4 * cols.stop],
+            )
 
         term_lo = []
         for b in range(4):
             if b == 2:
                 lo = shared.tile([P, 2 * V], F32, name="term_2", offset=4 * S)
             else:
-                lo = sb.tile([P, 2 * V], F32, name="term_%d" % b, tag="term_%d" % b if b else "fetched_1", align_bytes=64)
+                lo = sb.tile([P, 2 * V], F32, name="term_%d" % b, align_bytes=64)
             term_lo.append(lo)
 
         w1b, w1c, w1s = {}, {}, {}
 
-        def cast_w1_lo(b):
-            if b == 3:
-                wide = term_lo[0][:, 512:768].bitcast(BF16)
-            else:
+        w1b_mid = sb.tile([P, 8 * P], BF16, name="w1b_mid", tag="picked_1", align_bytes=64)
+
+        def cast_w1_lo(b, scalar):
+            if scalar:
                 own = sb.tile([P, 4 * P], BF16, name="w1b_%d" % b, align_bytes=64)
                 wide = own[:]
-            dst = wide.rearrange("p (c i j) -> p c j i", i=4, j=4)
-            src = w1_lo[b // 2][:, :, P * (b % 2) : P * (b % 2) + P].rearrange("p j (c i) -> p c j i", i=4)
-            if b in (0, 3):
-                nc.vector.tensor_copy(dst, src)
             else:
+                wide = w1b_mid[:, 4 * P * (b - 2) : 4 * P * (b - 1)]
+            dst = wide.rearrange("p (c i j) -> p c j i", i=4, j=4)
+            src = w1_lo[b].rearrange("p j (c i) -> p c j i", i=4)
+            if scalar:
                 nc.scalar.copy(dst, src)
+            else:
+                nc.vector.tensor_copy(dst, src)
             w1b[b] = (wide, 1)
 
         def cast_w1_hi(u):
@@ -137,46 +142,49 @@ def tile_picked_sage_none_e_kernel(tc, xT, w1, w2, gate, offs, pos1, pos2, out):
 
         def quant_w1(b0):
             wide, blocks = w1b[b0]
-            tag = "w1c_%d" % b0 if b0 else "fetched_0"
-            codes = sb.tile([P, P * blocks], U32, name="w1c_%d" % b0, tag=tag, align_bytes=64)
+            codes = sb.tile([P, P * blocks], U32, name="w1c_%d" % b0, align_bytes=64)
             scales = sb.tile([P, P * blocks], U8, name="w1s_%d" % b0, align_bytes=64)
             nc.vector.quantize_mx(out=codes[:].bitcast(FP8X4), scales=scales[:], in_=wide)
             for i in range(blocks):
                 w1c[b0 + i] = codes[:, P * i : P * i + P]
                 w1s[b0 + i] = scales[:, P * i : P * i + P]
 
-        w2b = term_lo[0][:, 0:512].bitcast(BF16)
-        w2c = sb.tile([P, 2 * N], U32, name="w2c", align_bytes=64)
-        w2s = sb.tile([P, 2 * N], U8, name="w2s", align_bytes=64)
+        w2b_t = sb.tile([P, 8 * N], BF16, name="w2b", align_bytes=64)
+        w2b = w2b_t[:]
+        w2q = []
 
         def cast_w2():
-            nc.vector.tensor_copy(
+            nc.scalar.copy(
                 w2b.rearrange("p (g c i t) -> p g c t i", g=2, i=4, t=4), w2_raw[:].rearrange("p g t (c i) -> p g c t i", i=4)
             )
 
         def quant_w2():
+            w2c = sb.tile([P, 2 * N], U32, name="w2c", tag="h_5", align_bytes=64)
+            w2s = sb.tile([P, 2 * N], U8, name="w2s", align_bytes=64)
+            w2q.extend([w2c, w2s])
             nc.vector.quantize_mx(out=w2c[:].bitcast(FP8X4), scales=w2s[:], in_=w2b)
 
         h = {}
 
-        def layer1(b, banks):
+        def layer1(b, banks, cuts=(0, 512, 1024)):
             if b == 3:
                 ht = shared.tile([P, S], F32, name="h_3", offset=0)
             else:
-                ht = sb.tile([P, S], F32, name="h_%d" % b)
+                ht = sb.tile([P, S], F32, name="h_%d" % b, align_bytes=64)
             h[b] = ht
-            for half in range(2):
-                acc = bank[banks[half]]
+            for name, n0, n1 in zip(banks, cuts, cuts[1:]):
+                acc = bank[name][:, 0 : n1 - n0]
+                cols = slice(n0 % 512, n0 % 512 + n1 - n0)
                 nc.tensor.matmul_mx(
-                    out=acc[:],
+                    out=acc,
                     lhsT=w1c[b].bitcast(FP8X4),
                     lhsT_scale=w1s[b],
-                    rhs=xc[half][:].bitcast(FP8X4),
-                    rhs_scale=xs[half][:],
+                    rhs=xc[n0 // 512][:, cols].bitcast(FP8X4),
+                    rhs_scale=xs[n0 // 512][:, cols],
                     start=True,
                     stop=True,
                 )
-                nc.scalar.copy(ht[:, 512 * half : 512 * half + 512], acc[:])
+                nc.scalar.copy(ht[:, n0:n1], acc)
 
         pos = (pos1_t, pos2_t)
         term = {}
@@ -199,19 +207,28 @@ def tile_picked_sage_none_e_kernel(tc, xT, w1, w2, gate, offs, pos1, pos2, out):
                     MULT,
                 )
 
-        def add_turned(dst, b, v):
-            for d in range(2):
+        def add_turned(dst, b, v, turns=(0, 1)):
+            for d in turns:
                 nc.tensor.matmul(
                     out=dst, lhsT=term[b, d][:, v : v + P], rhs=ident[:], start=d == 0, stop=d == 1, is_transpose=True
                 )
 
-        zt_lo = sb.tile([P, 4, 2, P, 2], BF16, name="zt_lo", tag="w1b_4", align_bytes=64)
+        zt_lo = sb.tile([P, 4, 2, P, 2], BF16, name="zt_lo", align_bytes=64)
         zt_hi = sb.tile([P, 3, 2, P, 2], BF16, name="zt_hi", align_bytes=64)
         z = {}
         for g, v0, v1 in ((0, 0, 512), (1, 0, 256), (1, 256, 384), (1, 384, 512)):
-            tag = "zt_hi" if v0 == TURN else "z_%d_%d" % (g, v0)
-            zg = sb.tile([P, v1 - v0, 4], BF16, name="z_%d_%d" % (g, v0), tag=tag, align_bytes=64)
+            zg = sb.tile([P, v1 - v0, 4], BF16, name="z_%d_%d" % (g, v0), align_bytes=64)
             z[g, v0] = zg[:]
+
+        plain = sb.tile([P, 2, PLAIN, P], F32, name="plain", tag="zt_lo", align_bytes=64)
+
+        def fetch_plain(b):
+            for d in range(2):
+                nc.scalar.activation(plain[:, d, b - 4, :], h[b][:].indirect(pos[d][:, TURN // 16 : V // 16]), COPY)
+
+        def gate_plain():
+            spread = gates[:, :, TURN:V].unsqueeze(2).to_broadcast([P, 2, PLAIN, P])
+            nc.vector.tensor_tensor(added[:, :, 0:PLAIN, :], plain[:], spread, MULT)
 
         def fold_lo(b, name):
             sums = bank[name][:].rearrange("p (vb c) -> p vb c", vb=4)
@@ -221,13 +238,13 @@ def tile_picked_sage_none_e_kernel(tc, xT, w1, w2, gate, offs, pos1, pos2, out):
                 zt_lo[:, :, :, 32 * b : 32 * b + 32, :], sums.rearrange("p vb (m u e) -> p vb u m e", u=2, e=2)
             )
 
-        def sum_hi(b, vb, name, slot):
+        def sum_hi(b, vb, name, slot, turns=(0, 1)):
             sums = bank[name][:].rearrange("p (q e m) -> p q e m", q=2, e=2)
-            add_turned(sums[:, slot, b % 2], b, P * vb)
+            add_turned(sums[:, slot, b % 2], b, P * vb, turns)
 
-        def round_hi(dst, name, slots):
+        def round_hi(dst, name, q0, q1):
             sums = bank[name][:].rearrange("p (q e m) -> p q m e", q=2, e=2)
-            nc.scalar.copy(dst, sums[:, 0:slots])
+            nc.scalar.copy(dst, sums[:, q0:q1])
 
         def turn_back(zt, vb0, count, dst, name):
             back = bank[name][:, 0 : 2 * P * count].rearrange("p (u v) -> p u v", u=2)
@@ -245,9 +262,7 @@ def tile_picked_sage_none_e_kernel(tc, xT, w1, w2, gate, offs, pos1, pos2, out):
             b = added[:, 1, :, v0 - TURN : v1 - TURN].rearrange("p t (c i) -> p c t i", i=4)
             nc.vector.tensor_tensor(dst, a, b, ADD)
 
-        zc0 = sb.tile([P, V], U32, name="zc_0", align_bytes=64)
-        zc1 = sb.tile([P, V], U32, name="zc_1", align_bytes=64)
-        zc = (zc0, zc1)
+        zc = {}
         zs = []
         for g in range(2):
             zsg = sb.tile([P, V], U8, name="zs_%d" % g, align_bytes=64)
@@ -265,8 +280,8 @@ def tile_picked_sage_none_e_kernel(tc, xT, w1, w2, gate, offs, pos1, pos2, out):
             for g in order:
                 nc.tensor.matmul_mx(
                     out=acc,
-                    lhsT=w2c[:, N * g : N * g + N].bitcast(FP8X4),
-                    lhsT_scale=w2s[:, N * g : N * g + N],
+                    lhsT=w2q[0][:, N * g : N * g + N].bitcast(FP8X4),
+                    lhsT_scale=w2q[1][:, N * g : N * g + N],
                     rhs=zc[g][:, v0:v1].bitcast(FP8X4),
                     rhs_scale=zs[g][:, v0:v1],
                     start=g == order[0],
@@ -276,34 +291,28 @@ def tile_picked_sage_none_e_kernel(tc, xT, w1, w2, gate, offs, pos1, pos2, out):
             nc.scalar.copy(out_t[:], acc)
             nc.sync.dma_start(out[:, v0:v1], out_t[:])
 
-        cast_x(0, 0, 640, False)
-        cast_x(0, 640, 1024, True)
-        cast_x(1, 0, 704, False)
-        cast_x(1, 704, 1024, True)
-        gather_x(0, 0, 512)
-        gather_x(0, 512, 1024)
-        cast_x(2, 0, 768, True)
-        cast_x(2, 768, 1024, False)
-        cast_x(3, 0, 512, False)
-        cast_x(3, 512, 768, True)
-        cast_x(4, 0, 160, False)
-        cast_x(4, 160, 256, True)
-        for n0 in range(0, S, 256):
-            gather_x(1, n0, n0 + 256)
-            weave_x(n0, n0 + 256)
-        cast_w1_lo(0)
-        cast_w1_lo(1)
-        cast_w1_lo(2)
-        quant_x(0)
+        for j in range(3):
+            for q in range(4):
+                gather_x(j, q)
+            for q in range(1, 4):
+                place_x(j, q)
+        for q in range(4):
+            gather_x(3, q)
+        cast_w1_lo(0, True)
+        cast_w1_lo(1, True)
+        place_x(3, 1)
+        place_x(3, 2)
+        quant_x(0, 512)
+        place_x(3, 3)
         quant_w1(0)
-        quant_x(1)
-        cast_w1_lo(3)
+        quant_x(512, 768)
+        quant_x(768, 1024)
         quant_w1(1)
-        cast_w2()
-        quant_w1(3)
-        quant_w2()
+        cast_w1_lo(2, False)
+        cast_w1_lo(3, False)
         quant_w1(2)
-        layer1(0, "AB")
+        quant_w1(3)
+        layer1(0, "ABG", (0, 512, 768, 1024))
         layer1(1, "CD")
         layer1(2, "AB")
         cast_w1_hi(0)
@@ -311,9 +320,10 @@ def tile_picked_sage_none_e_kernel(tc, xT, w1, w2, gate, offs, pos1, pos2, out):
         quant_w1(4)
         quant_w1(6)
         layer1(3, "CD")
-        layer1(4, "EF")
         gather_h(0, 0, V)
         fold_lo(0, "A")
+        cast_w2()
+        layer1(4, "EF")
         gather_h(1, 0, V)
         fold_lo(1, "C")
         layer1(5, "GH")
@@ -325,34 +335,40 @@ def tile_picked_sage_none_e_kernel(tc, xT, w1, w2, gate, offs, pos1, pos2, out):
         layer1(7, "FH")
         turn_back(zt_lo, 0, 2, z[0, 0][:, 0:256], "A")
         turn_back(zt_lo, 2, 2, z[0, 0][:, 256:512], "C")
+        for b in (7, 6, 5, 4):
+            fetch_plain(b)
         gather_h(4, 0, TURN)
         gather_h(5, 0, TURN)
         for b in (4, 5):
             for vb in range(2):
                 sum_hi(b, vb, "F", vb)
-        round_hi(zt_hi[:, 0:2, 0], "F", 2)
-        sum_hi(4, 2, "C", 0)
-        sum_hi(5, 2, "C", 0)
+        round_hi(zt_hi[:, 0:2, 0], "F", 0, 2)
+        sum_hi(4, 2, "H", 0)
+        sum_hi(5, 2, "H", 0)
+        round_hi(zt_hi[:, 2:3, 0], "H", 0, 1)
         for b in (6, 7):
-            gather_h(b, 0, TURN)
-            sum_hi(b, 0, "A", 0)
-            sum_hi(b, 1, "F", 0)
-            sum_hi(b, 2, "C", 1)
-        round_hi(zt_hi[:, 0:1, 1], "A", 1)
-        round_hi(zt_hi[:, 1:2, 1], "F", 1)
+            gather_h(b, 0, 2 * P)
+            for d in range(2):
+                sum_hi(b, 0, "A", 0, (d,))
+                sum_hi(b, 1, "C", 0, (d,))
+        round_hi(zt_hi[:, 0:1, 1], "A", 0, 1)
+        round_hi(zt_hi[:, 1:2, 1], "C", 0, 1)
+        for b in (6, 7):
+            gather_h(b, 2 * P, TURN)
+            sum_hi(b, 2, "F", 0)
         turn_back(zt_hi, 0, 1, z[1, 0][:, 0:P], "E")
         turn_back(zt_hi, 1, 1, z[1, 0][:, P : 2 * P], "G")
-        round_hi(zt_hi[:, 2], "C", 2)
-        turn_back(zt_hi, 2, 1, z[1, 256], "G")
-        gather_h(5, TURN, V)
-        gather_h(6, TURN, V)
+        round_hi(zt_hi[:, 2:3, 1], "F", 0, 1)
+        turn_back(zt_hi, 2, 1, z[1, 256], "B")
+        zc[0] = sb.tile([P, V], U32, name="zc_0", tag="h_4", align_bytes=64)
+        zc[1] = sb.tile([P, V], U32, name="zc_1", align_bytes=64)
+        quant_w2()
+        gate_plain()
         quant_z(0, 0, 512)
-        gather_h(4, TURN, V)
-        gather_h(7, TURN, V)
+        add_z(384, 512)
         quant_z(1, 0, 256)
         layer2(0, 256, "E", (0, 1))
-        add_z(384, 512)
-        quant_z(1, 256, 384)
-        layer2(256, 384, "G", (0, 1))
         quant_z(1, 384, 512)
-        layer2(384, 512, "F", (0, 1))
+        layer2(384, 512, "G", (0, 1))
+        quant_z(1, 256, 384)
+        layer2(256, 384, "B", (0, 1))

@@ -80,17 +80,18 @@ def tile_picked_sage_none_e_kernel(tc, xT, w1, w2, gate, offs, pos1, pos2, out):
             return x_raw[j][:].indirect(offs_t[:, n0 // 16 : n1 // 16])
 
         fetched = {}
+        for n0, n1 in ((256, 512), (512, 768), (768, 1024)):
+            ft = sb.tile([P, 4, n1 - n0], BF16, name="fetched_%d" % n0, align_bytes=64)
+            fetched[n0] = ft
 
-        def gather_x(j, q):
-            if q:
-                ft = sb.tile([P, 256], BF16, name="fetched_%d_%d" % (j, q), align_bytes=64)
-                nc.scalar.activation(ft[:], looked_up(j, 256 * q, 256 * q + 256), COPY)
-                fetched[j, q] = ft
-            else:
-                nc.vector.tensor_copy(slots(0, 256)[:, :, j], looked_up(j, 0, 256))
+        def gather_into_slots(j, n1):
+            nc.vector.tensor_copy(slots(0, n1)[:, :, j], looked_up(j, 0, n1))
 
-        def place_x(j, q):
-            nc.vector.tensor_copy(slots(256 * q, 256 * q + 256)[:, :, j], fetched[j, q][:])
+        def gather_plane(j, n0, n1):
+            nc.scalar.activation(fetched[n0][:, j, :], looked_up(j, n0, n1), COPY)
+
+        def place(j0, j1, n0, n1):
+            nc.vector.tensor_copy(slots(n0, n1)[:, :, j0:j1], fetched[n0][:, j0:j1, :].rearrange("p e n -> p n e"))
 
         xc, xs = [], []
         for half in range(2):
@@ -107,30 +108,13 @@ def tile_picked_sage_none_e_kernel(tc, xT, w1, w2, gate, offs, pos1, pos2, out):
                 in_=picked[n0 // 512][:, 4 * cols.start : 4 * cols.stop],
             )
 
-        term_lo = []
-        for b in range(4):
-            if b == 2:
-                lo = shared.tile([P, 2 * V], F32, name="term_2", offset=4 * S)
-            else:
-                lo = sb.tile([P, 2 * V], F32, name="term_%d" % b, align_bytes=64)
-            term_lo.append(lo)
-
         w1b, w1c, w1s = {}, {}, {}
 
-        w1b_mid = sb.tile([P, 8 * P], BF16, name="w1b_mid", tag="picked_1", align_bytes=64)
-
-        def cast_w1_lo(b, scalar):
-            if scalar:
-                own = sb.tile([P, 4 * P], BF16, name="w1b_%d" % b, align_bytes=64)
-                wide = own[:]
-            else:
-                wide = w1b_mid[:, 4 * P * (b - 2) : 4 * P * (b - 1)]
+        def cast_w1_lo(b):
+            own = sb.tile([P, 4 * P], BF16, name="w1b_%d" % b, align_bytes=64)
+            wide = own[:]
             dst = wide.rearrange("p (c i j) -> p c j i", i=4, j=4)
-            src = w1_lo[b].rearrange("p j (c i) -> p c j i", i=4)
-            if scalar:
-                nc.scalar.copy(dst, src)
-            else:
-                nc.vector.tensor_copy(dst, src)
+            nc.scalar.copy(dst, w1_lo[b].rearrange("p j (c i) -> p c j i", i=4))
             w1b[b] = (wide, 1)
 
         def cast_w1_hi(u):
@@ -184,13 +168,26 @@ def tile_picked_sage_none_e_kernel(tc, xT, w1, w2, gate, offs, pos1, pos2, out):
                     start=True,
                     stop=True,
                 )
-                nc.scalar.copy(ht[:, n0:n1], acc)
+                if n1 - n0 == P:
+                    nc.vector.tensor_copy(ht[:, n0:n1], acc)
+                else:
+                    nc.scalar.copy(ht[:, n0:n1], acc)
 
         pos = (pos1_t, pos2_t)
         term = {}
-        for b in range(4):
-            for d in range(2):
-                term[b, d] = term_lo[b][:, V * d : V * d + V]
+
+        def make_terms():
+            term_lo = []
+            for b in range(4):
+                if b == 2:
+                    lo = shared.tile([P, 2 * V], F32, name="term_2", offset=4 * S)
+                else:
+                    lo = sb.tile([P, 2 * V], F32, name="term_%d" % b, tag="term_%d" % b if b else "w1b_3", align_bytes=64)
+                term_lo.append(lo)
+            for b in range(4):
+                for d in range(2):
+                    term[b, d] = term_lo[b][:, V * d : V * d + V]
+
         turned = sb.tile([P, 2, 4 * TURN], F32, name="term_turned")
         added = turned[:, :, TURN - P : 2 * TURN].rearrange("p d (t v) -> p d t v", t=4)
         for d in range(2):
@@ -291,28 +288,29 @@ def tile_picked_sage_none_e_kernel(tc, xT, w1, w2, gate, offs, pos1, pos2, out):
             nc.scalar.copy(out_t[:], acc)
             nc.sync.dma_start(out[:, v0:v1], out_t[:])
 
-        for j in range(3):
-            for q in range(4):
-                gather_x(j, q)
-            for q in range(1, 4):
-                place_x(j, q)
-        for q in range(4):
-            gather_x(3, q)
-        cast_w1_lo(0, True)
-        cast_w1_lo(1, True)
-        place_x(3, 1)
-        place_x(3, 2)
+        for j in range(4):
+            cut = 256
+            pieces = ((cut, 512), (512, 768), (768, 1024))
+            gather_into_slots(j, cut)
+            for n0, n1 in pieces:
+                gather_plane(j, n0, n1)
+            for n0, n1 in pieces[: 3 if j < 2 else 1]:
+                place(j, j + 1, n0, n1)
+        cast_w1_lo(0)
+        cast_w1_lo(1)
+        cast_w1_lo(2)
+        cast_w1_lo(3)
+        place(2, 4, 512, 768)
         quant_x(0, 512)
-        place_x(3, 3)
+        place(2, 4, 768, 1024)
         quant_w1(0)
         quant_x(512, 768)
-        quant_x(768, 1024)
+        quant_x(768, 896)
+        quant_x(896, 1024)
         quant_w1(1)
-        cast_w1_lo(2, False)
-        cast_w1_lo(3, False)
         quant_w1(2)
         quant_w1(3)
-        layer1(0, "ABG", (0, 512, 768, 1024))
+        layer1(0, "ABGH", (0, 512, 768, 896, 1024))
         layer1(1, "CD")
         layer1(2, "AB")
         cast_w1_hi(0)
@@ -320,6 +318,7 @@ def tile_picked_sage_none_e_kernel(tc, xT, w1, w2, gate, offs, pos1, pos2, out):
         quant_w1(4)
         quant_w1(6)
         layer1(3, "CD")
+        make_terms()
         gather_h(0, 0, V)
         fold_lo(0, "A")
         cast_w2()

@@ -117,12 +117,13 @@ def tile_picked_sage_none_e_kernel(tc, xT, w1, w2, gate, offs, pos1, pos2, out):
             nc.scalar.copy(dst, w1_lo[b].rearrange("p j (c i) -> p c j i", i=4))
             w1b[b] = (wide, 1)
 
-        def cast_w1_hi(u):
-            own = sb.tile([P, 8 * P], BF16, name="w1b_%d" % (4 + 2 * u), align_bytes=64)
-            wide = own[:]
-            src = w1_hi[:].rearrange("p j (m t) -> p m j t", t=4)[:, :, :, 2 * u : 2 * u + 2]
-            nc.scalar.copy(wide.rearrange("p (e m j) -> p m j e", e=2, j=4), src)
-            w1b[4 + 2 * u] = (wide, 2)
+        w1b_hi = sb.tile([P, 16 * P], BF16, name="w1b_4", align_bytes=64)
+        w1b[4] = (w1b_hi[:], 4)
+
+        def cast_w1_hi(half):
+            cols = slice(64 * half, 64 * half + 64)
+            dst = w1b_hi[:].rearrange("p (t m j) -> p m j t", t=4, j=4)[:, cols]
+            nc.scalar.copy(dst, w1_hi[:].rearrange("p j (m t) -> p m j t", t=4)[:, cols])
 
         def quant_w1(b0):
             wide, blocks = w1b[b0]
@@ -316,7 +317,6 @@ def tile_picked_sage_none_e_kernel(tc, xT, w1, w2, gate, offs, pos1, pos2, out):
         cast_w1_hi(0)
         cast_w1_hi(1)
         quant_w1(4)
-        quant_w1(6)
         layer1(3, "CD")
         make_terms()
         gather_h(0, 0, V)
@@ -355,9 +355,9 @@ def tile_picked_sage_none_e_kernel(tc, xT, w1, w2, gate, offs, pos1, pos2, out):
         for b in (6, 7):
             gather_h(b, 2 * P, TURN)
             sum_hi(b, 2, "F", 0)
+        round_hi(zt_hi[:, 2:3, 1], "F", 0, 1)
         turn_back(zt_hi, 0, 1, z[1, 0][:, 0:P], "E")
         turn_back(zt_hi, 1, 1, z[1, 0][:, P : 2 * P], "G")
-        round_hi(zt_hi[:, 2:3, 1], "F", 0, 1)
         turn_back(zt_hi, 2, 1, z[1, 256], "B")
         zc[0] = sb.tile([P, V], U32, name="zc_0", tag="h_4", align_bytes=64)
         zc[1] = sb.tile([P, V], U32, name="zc_1", align_bytes=64)

@@ -5,8 +5,9 @@ from concourse.masks import make_identity
 
 K, T, S, V, H, N = 512, 2048, 1024, 512, 1024, 128
 P = 128
+BANK = 512
+QUARTER = S // 4
 TURN = 384
-PLAIN = 4
 FLOPS = 2 * K * H * S + 2 * H * N * V
 
 F32 = mybir.dt.float32
@@ -41,7 +42,7 @@ def tile_picked_sage_none_e_kernel(tc, xT, w1, w2, gate, offs, pos1, pos2, out):
 
         bank = {}
         for name in "ABCDEFGH":
-            whole = ps.tile([P, 512], F32, name="bank_" + name)
+            whole = ps.tile([P, BANK], F32, name="bank_" + name)
             bank[name] = whole
 
         x_view = xT.rearrange("(p j) t -> p j t", j=4)
@@ -57,101 +58,93 @@ def tile_picked_sage_none_e_kernel(tc, xT, w1, w2, gate, offs, pos1, pos2, out):
         w1_view = w1.rearrange("(p j) i -> p j i", j=4)
         w1_lo = []
         gates = sb.tile([P, 2, V], F32, name="gates")
-        for b0, b1 in ((0, 2), (2, 4)):
-            raw = sb.tile([P, 4, P * (b1 - b0)], F32, name="w1_lo_%d" % b0, align_bytes=64)
-            nc.sync.dma_start(raw[:], w1_view[:, :, P * b0 : P * b1])
-            w1_lo.extend(raw[:, :, P * i : P * i + P] for i in range(b1 - b0))
-        for d in range(2):
-            nc.sync.dma_start(gates[:, d, :], gate[d])
-        w1_hi = shared.tile([P, 4, 512], F32, name="w1_hi", offset=0)
-        nc.sync.dma_start(w1_hi[:], w1_view[:, :, 512:1024])
+        for b0 in (0, 2):
+            raw = sb.tile([P, 4, 2 * P], F32, name="w1_lo_%d" % b0, align_bytes=64)
+            nc.sync.dma_start(raw[:], w1_view[:, :, P * b0 : P * b0 + 2 * P])
+            w1_lo.extend([raw[:, :, 0:P], raw[:, :, P : 2 * P]])
+        nc.sync.dma_start(gates[:], gate.rearrange("d p v -> p d v"))
+        hi_first = sb.tile([P, 4, P], F32, name="w1_hi_0")
+        hi_rest = shared.tile([P, 4, 3 * P], F32, name="w1_hi_1", offset=S)
+        w1_hi = ((hi_first, H // 2, H // 2 + P), (hi_rest, H // 2 + P, H))
+        for raw, c0, c1 in w1_hi:
+            nc.sync.dma_start(raw[:], w1_view[:, :, c0:c1])
         w2_raw = sb.tile([P, 2, 4, N], F32, name="w2_raw")
         nc.sync.dma_start(w2_raw[:], w2.rearrange("(g p t) n -> p g t n", g=2, t=4))
 
         picked = []
         for half in range(2):
-            pk = sb.tile([P, 4 * 512], BF16, name="picked_%d" % half, align_bytes=64)
+            pk = sb.tile([P, 4 * BANK], BF16, name="picked_%d" % half, align_bytes=64)
             picked.append(pk)
 
         def slots(n0, n1):
-            return picked[n0 // 512][:].rearrange("p (n t) -> p n t", t=4)[:, n0 % 512 : n0 % 512 + n1 - n0]
+            return picked[n0 // BANK][:].rearrange("p (n t) -> p n t", t=4)[:, n0 % BANK : n0 % BANK + n1 - n0]
 
-        def looked_up(j, n0, n1):
-            return x_raw[j][:].indirect(offs_t[:, n0 // 16 : n1 // 16])
+        def looked_up(j, q):
+            return x_raw[j][:].indirect(offs_t[:, QUARTER * q // 16 : QUARTER * (q + 1) // 16])
 
         fetched = {}
-        for n0, n1 in ((256, 512), (512, 768), (768, 1024)):
-            ft = sb.tile([P, 4, n1 - n0], BF16, name="fetched_%d" % n0, align_bytes=64)
-            fetched[n0] = ft
+        for q in range(1, 4):
+            ft = sb.tile([P, 4, QUARTER], BF16, name="fetched_%d" % (QUARTER * q), align_bytes=64)
+            fetched[q] = ft
 
-        def gather_into_slots(j, n1):
-            nc.vector.tensor_copy(slots(0, n1)[:, :, j], looked_up(j, 0, n1))
+        def gather_plane(j):
+            nc.vector.tensor_copy(slots(0, QUARTER)[:, :, j], looked_up(j, 0))
+            for q in range(1, 4):
+                nc.scalar.activation(fetched[q][:, j, :], looked_up(j, q), COPY)
 
-        def gather_plane(j, n0, n1):
-            nc.scalar.activation(fetched[n0][:, j, :], looked_up(j, n0, n1), COPY)
-
-        def place(j0, j1, n0, n1):
-            nc.vector.tensor_copy(slots(n0, n1)[:, :, j0:j1], fetched[n0][:, j0:j1, :].rearrange("p e n -> p n e"))
+        def place(j0, j1, q):
+            dst = slots(QUARTER * q, QUARTER * (q + 1))[:, :, j0:j1]
+            nc.vector.tensor_copy(dst, fetched[q][:, j0:j1, :].rearrange("p e n -> p n e"))
 
         xc, xs = [], []
         for half in range(2):
-            codes = sb.tile([P, 512], U32, name="xc_%d" % half, tag="w1_lo_0" if half else "xc_0", align_bytes=64)
-            scales = sb.tile([P, 512], U8, name="xs_%d" % half, align_bytes=64)
+            codes = sb.tile([P, BANK], U32, name="xc_%d" % half, tag="w1_lo_0" if half else "xc_0", align_bytes=64)
+            scales = sb.tile([P, BANK], U8, name="xs_%d" % half, align_bytes=64)
             xc.append(codes)
             xs.append(scales)
 
         def quant_x(n0, n1):
-            cols = slice(n0 % 512, n0 % 512 + n1 - n0)
+            cols = slice(n0 % BANK, n0 % BANK + n1 - n0)
             nc.vector.quantize_mx(
-                out=xc[n0 // 512][:, cols].bitcast(FP8X4),
-                scales=xs[n0 // 512][:, cols],
-                in_=picked[n0 // 512][:, 4 * cols.start : 4 * cols.stop],
+                out=xc[n0 // BANK][:, cols].bitcast(FP8X4),
+                scales=xs[n0 // BANK][:, cols],
+                in_=picked[n0 // BANK][:, 4 * cols.start : 4 * cols.stop],
             )
 
         w1b, w1c, w1s = {}, {}, {}
 
-        def cast_w1_lo(b):
+        def round_w1_lo(b):
             own = sb.tile([P, 4 * P], BF16, name="w1b_%d" % b, align_bytes=64)
-            wide = own[:]
-            dst = wide.rearrange("p (c i j) -> p c j i", i=4, j=4)
+            dst = own[:].rearrange("p (c i j) -> p c j i", i=4, j=4)
             nc.scalar.copy(dst, w1_lo[b].rearrange("p j (c i) -> p c j i", i=4))
-            w1b[b] = (wide, 1)
+            w1b[b] = (own[:], 1)
 
         w1b_hi = sb.tile([P, 16 * P], BF16, name="w1b_4", align_bytes=64)
         w1b[4] = (w1b_hi[:], 4)
 
-        def cast_w1_hi(half):
-            cols = slice(64 * half, 64 * half + 64)
-            dst = w1b_hi[:].rearrange("p (t m j) -> p m j t", t=4, j=4)[:, cols]
-            nc.scalar.copy(dst, w1_hi[:].rearrange("p j (m t) -> p m j t", t=4)[:, cols])
+        def round_w1_hi(piece):
+            raw, c0, c1 = w1_hi[piece]
+            dst = w1b_hi[:].rearrange("p (t m j) -> p m j t", t=4, j=4)[:, (c0 - H // 2) // 4 : (c1 - H // 2) // 4]
+            nc.scalar.copy(dst, raw[:].rearrange("p j (m t) -> p m j t", t=4))
 
         def quant_w1(b0):
-            wide, blocks = w1b[b0]
-            codes = sb.tile([P, P * blocks], U32, name="w1c_%d" % b0, align_bytes=64)
-            scales = sb.tile([P, P * blocks], U8, name="w1s_%d" % b0, align_bytes=64)
+            wide, parts = w1b[b0]
+            codes = sb.tile([P, P * parts], U32, name="w1c_%d" % b0, align_bytes=64)
+            scales = sb.tile([P, P * parts], U8, name="w1s_%d" % b0, align_bytes=64)
             nc.vector.quantize_mx(out=codes[:].bitcast(FP8X4), scales=scales[:], in_=wide)
-            for i in range(blocks):
+            for i in range(parts):
                 w1c[b0 + i] = codes[:, P * i : P * i + P]
                 w1s[b0 + i] = scales[:, P * i : P * i + P]
 
-        w2b_t = sb.tile([P, 8 * N], BF16, name="w2b", align_bytes=64)
-        w2b = w2b_t[:]
-        w2q = []
+        w2b = sb.tile([P, 8 * N], BF16, name="w2b", align_bytes=64)
 
-        def cast_w2():
-            nc.scalar.copy(
-                w2b.rearrange("p (g c i t) -> p g c t i", g=2, i=4, t=4), w2_raw[:].rearrange("p g t (c i) -> p g c t i", i=4)
-            )
-
-        def quant_w2():
-            w2c = sb.tile([P, 2 * N], U32, name="w2c", tag="h_5", align_bytes=64)
-            w2s = sb.tile([P, 2 * N], U8, name="w2s", align_bytes=64)
-            w2q.extend([w2c, w2s])
-            nc.vector.quantize_mx(out=w2c[:].bitcast(FP8X4), scales=w2s[:], in_=w2b)
+        def round_w2():
+            dst = w2b[:].rearrange("p (g c i t) -> p g c t i", g=2, i=4, t=4)
+            nc.scalar.copy(dst, w2_raw[:].rearrange("p g t (c i) -> p g c t i", i=4))
 
         h = {}
 
-        def layer1(b, banks, cuts=(0, 512, 1024)):
+        def layer1(b, banks, cuts=(0, BANK, S)):
             if b == 3:
                 ht = shared.tile([P, S], F32, name="h_3", offset=0)
             else:
@@ -159,13 +152,13 @@ def tile_picked_sage_none_e_kernel(tc, xT, w1, w2, gate, offs, pos1, pos2, out):
             h[b] = ht
             for name, n0, n1 in zip(banks, cuts, cuts[1:]):
                 acc = bank[name][:, 0 : n1 - n0]
-                cols = slice(n0 % 512, n0 % 512 + n1 - n0)
+                cols = slice(n0 % BANK, n0 % BANK + n1 - n0)
                 nc.tensor.matmul_mx(
                     out=acc,
                     lhsT=w1c[b].bitcast(FP8X4),
                     lhsT_scale=w1s[b],
-                    rhs=xc[n0 // 512][:, cols].bitcast(FP8X4),
-                    rhs_scale=xs[n0 // 512][:, cols],
+                    rhs=xc[n0 // BANK][:, cols].bitcast(FP8X4),
+                    rhs_scale=xs[n0 // BANK][:, cols],
                     start=True,
                     stop=True,
                 )
@@ -177,29 +170,25 @@ def tile_picked_sage_none_e_kernel(tc, xT, w1, w2, gate, offs, pos1, pos2, out):
         pos = (pos1_t, pos2_t)
         term = {}
 
-        def make_terms():
-            term_lo = []
+        def make_low_terms():
             for b in range(4):
                 if b == 2:
-                    lo = shared.tile([P, 2 * V], F32, name="term_2", offset=4 * S)
+                    both = shared.tile([P, 2 * V], F32, name="term_2", offset=4 * S)
                 else:
-                    lo = sb.tile([P, 2 * V], F32, name="term_%d" % b, tag="term_%d" % b if b else "w1b_3", align_bytes=64)
-                term_lo.append(lo)
-            for b in range(4):
+                    both = sb.tile([P, 2 * V], F32, name="term_%d" % b, tag="term_%d" % b if b else "w1b_3", align_bytes=64)
                 for d in range(2):
-                    term[b, d] = term_lo[b][:, V * d : V * d + V]
+                    term[b, d] = both[:, V * d : V * d + V]
 
         turned = sb.tile([P, 2, 4 * TURN], F32, name="term_turned")
-        added = turned[:, :, TURN - P : 2 * TURN].rearrange("p d (t v) -> p d t v", t=4)
         for d in range(2):
             for t in range(4):
                 term[4 + t, d] = turned[:, d, TURN * t : TURN * t + TURN]
+        added = turned[:, :, TURN - P : 2 * TURN].rearrange("p d (t v) -> p d t v", t=4)
 
         def gather_h(b, v0, v1):
             for d in range(2):
-                dst = term[b, d][:, v0:v1] if v0 < TURN else added[:, d, b - 4, v0 - TURN : v1 - TURN]
                 nc.vector.tensor_tensor(
-                    dst,
+                    term[b, d][:, v0:v1],
                     h[b][:].indirect(pos[d][:, v0 // 16 : v1 // 16]),
                     gates[:, d, v0:v1],
                     MULT,
@@ -214,19 +203,25 @@ def tile_picked_sage_none_e_kernel(tc, xT, w1, w2, gate, offs, pos1, pos2, out):
         zt_lo = sb.tile([P, 4, 2, P, 2], BF16, name="zt_lo", align_bytes=64)
         zt_hi = sb.tile([P, 3, 2, P, 2], BF16, name="zt_hi", align_bytes=64)
         z = {}
-        for g, v0, v1 in ((0, 0, 512), (1, 0, 256), (1, 256, 384), (1, 384, 512)):
+        for g, v0, v1 in ((0, 0, V), (1, 0, 2 * P), (1, 2 * P, TURN), (1, TURN, V)):
             zg = sb.tile([P, v1 - v0, 4], BF16, name="z_%d_%d" % (g, v0), align_bytes=64)
             z[g, v0] = zg[:]
 
-        plain = sb.tile([P, 2, PLAIN, P], F32, name="plain", tag="zt_lo", align_bytes=64)
+        plain = sb.tile([P, 2, 4, P], F32, name="plain", tag="zt_lo", align_bytes=64)
 
         def fetch_plain(b):
             for d in range(2):
                 nc.scalar.activation(plain[:, d, b - 4, :], h[b][:].indirect(pos[d][:, TURN // 16 : V // 16]), COPY)
 
         def gate_plain():
-            spread = gates[:, :, TURN:V].unsqueeze(2).to_broadcast([P, 2, PLAIN, P])
-            nc.vector.tensor_tensor(added[:, :, 0:PLAIN, :], plain[:], spread, MULT)
+            spread = gates[:, :, TURN:V].unsqueeze(2).to_broadcast([P, 2, 4, P])
+            nc.vector.tensor_tensor(added, plain[:], spread, MULT)
+
+        def add_plain():
+            dst = z[1, TURN].rearrange("p (c i) t -> p c t i", i=4)
+            first = added[:, 0].rearrange("p t (c i) -> p c t i", i=4)
+            second = added[:, 1].rearrange("p t (c i) -> p c t i", i=4)
+            nc.vector.tensor_tensor(dst, first, second, ADD)
 
         def fold_lo(b, name):
             sums = bank[name][:].rearrange("p (vb c) -> p vb c", vb=4)
@@ -236,13 +231,13 @@ def tile_picked_sage_none_e_kernel(tc, xT, w1, w2, gate, offs, pos1, pos2, out):
                 zt_lo[:, :, :, 32 * b : 32 * b + 32, :], sums.rearrange("p vb (m u e) -> p vb u m e", u=2, e=2)
             )
 
-        def sum_hi(b, vb, name, slot, turns=(0, 1)):
+        def sum_hi(b, vb, name, q, turns=(0, 1)):
             sums = bank[name][:].rearrange("p (q e m) -> p q e m", q=2, e=2)
-            add_turned(sums[:, slot, b % 2], b, P * vb, turns)
+            add_turned(sums[:, q, b % 2], b, P * vb, turns)
 
-        def round_hi(dst, name, q0, q1):
+        def round_hi(vb0, count, u, name):
             sums = bank[name][:].rearrange("p (q e m) -> p q m e", q=2, e=2)
-            nc.scalar.copy(dst, sums[:, q0:q1])
+            nc.scalar.copy(zt_hi[:, vb0 : vb0 + count, u], sums[:, 0:count])
 
         def turn_back(zt, vb0, count, dst, name):
             back = bank[name][:, 0 : 2 * P * count].rearrange("p (u v) -> p u v", u=2)
@@ -251,16 +246,9 @@ def tile_picked_sage_none_e_kernel(tc, xT, w1, w2, gate, offs, pos1, pos2, out):
                 for u in range(2):
                     w0 = P * (2 * (vb0 + vb) + u)
                     nc.tensor.transpose(back[:, u, P * vb : P * vb + P], words[:, w0 : w0 + P], ident[:])
-            dst = dst.rearrange("p v t -> p (v t)").bitcast(F32)
-            nc.scalar.copy(dst.rearrange("p (v u) -> p v u", u=2), back.rearrange("p u v -> p v u"))
+            dst_words = dst.rearrange("p v t -> p (v t)").bitcast(F32)
+            nc.scalar.copy(dst_words.rearrange("p (v u) -> p v u", u=2), back.rearrange("p u v -> p v u"))
 
-        def add_z(v0, v1):
-            dst = z[1, v0].rearrange("p (c i) t -> p c t i", i=4)
-            a = added[:, 0, :, v0 - TURN : v1 - TURN].rearrange("p t (c i) -> p c t i", i=4)
-            b = added[:, 1, :, v0 - TURN : v1 - TURN].rearrange("p t (c i) -> p c t i", i=4)
-            nc.vector.tensor_tensor(dst, a, b, ADD)
-
-        zc = {}
         zs = []
         for g in range(2):
             zsg = sb.tile([P, V], U8, name="zs_%d" % g, align_bytes=64)
@@ -273,67 +261,57 @@ def tile_picked_sage_none_e_kernel(tc, xT, w1, w2, gate, offs, pos1, pos2, out):
                 in_=z[g, v0].rearrange("p v t -> p (v t)"),
             )
 
-        def layer2(v0, v1, name, order):
+        def layer2(v0, v1, name):
             acc = bank[name][:, 0 : v1 - v0]
-            for g in order:
+            for g in range(2):
                 nc.tensor.matmul_mx(
                     out=acc,
-                    lhsT=w2q[0][:, N * g : N * g + N].bitcast(FP8X4),
-                    lhsT_scale=w2q[1][:, N * g : N * g + N],
+                    lhsT=w2c[:, N * g : N * g + N].bitcast(FP8X4),
+                    lhsT_scale=w2s[:, N * g : N * g + N],
                     rhs=zc[g][:, v0:v1].bitcast(FP8X4),
                     rhs_scale=zs[g][:, v0:v1],
-                    start=g == order[0],
-                    stop=g == order[1],
+                    start=g == 0,
+                    stop=g == 1,
                 )
             out_t = sb.tile([P, v1 - v0], F32, name="out_%d" % v0)
             nc.scalar.copy(out_t[:], acc)
             nc.sync.dma_start(out[:, v0:v1], out_t[:])
 
         for j in range(4):
-            cut = 256
-            pieces = ((cut, 512), (512, 768), (768, 1024))
-            gather_into_slots(j, cut)
-            for n0, n1 in pieces:
-                gather_plane(j, n0, n1)
-            for n0, n1 in pieces[: 3 if j < 2 else 1]:
-                place(j, j + 1, n0, n1)
-        cast_w1_lo(0)
-        cast_w1_lo(1)
-        cast_w1_lo(2)
-        cast_w1_lo(3)
-        place(2, 4, 512, 768)
-        quant_x(0, 512)
-        place(2, 4, 768, 1024)
+            gather_plane(j)
+            for q in range(1, 4 if j < 2 else 2):
+                place(j, j + 1, q)
+        for b in range(4):
+            round_w1_lo(b)
+        place(2, 4, 2)
+        quant_x(0, BANK)
+        place(2, 4, 3)
         quant_w1(0)
-        quant_x(512, 768)
-        quant_x(768, 896)
-        quant_x(896, 1024)
-        quant_w1(1)
-        quant_w1(2)
-        quant_w1(3)
-        layer1(0, "ABGH", (0, 512, 768, 896, 1024))
+        head_cuts = (0, BANK, 3 * QUARTER, S - P, S)
+        for n0, n1 in zip(head_cuts[1:], head_cuts[2:]):
+            quant_x(n0, n1)
+        for b in range(1, 4):
+            quant_w1(b)
+        layer1(0, "ABGH", head_cuts)
+        round_w1_hi(0)
         layer1(1, "CD")
         layer1(2, "AB")
-        cast_w1_hi(0)
-        cast_w1_hi(1)
+        round_w1_hi(1)
         quant_w1(4)
         layer1(3, "CD")
-        make_terms()
+
+        make_low_terms()
         gather_h(0, 0, V)
         fold_lo(0, "A")
-        cast_w2()
-        layer1(4, "EF")
-        gather_h(1, 0, V)
-        fold_lo(1, "C")
-        layer1(5, "GH")
-        gather_h(2, 0, V)
-        fold_lo(2, "A")
-        layer1(6, "BD")
-        gather_h(3, 0, V)
-        fold_lo(3, "C")
+        round_w2()
+        for b, banks in zip(range(1, 4), ("EF", "GH", "BD")):
+            layer1(3 + b, banks)
+            gather_h(b, 0, V)
+            fold_lo(b, "AC"[b % 2])
         layer1(7, "FH")
-        turn_back(zt_lo, 0, 2, z[0, 0][:, 0:256], "A")
-        turn_back(zt_lo, 2, 2, z[0, 0][:, 256:512], "C")
+        turn_back(zt_lo, 0, 2, z[0, 0][:, 0 : 2 * P], "A")
+        turn_back(zt_lo, 2, 2, z[0, 0][:, 2 * P : V], "C")
+
         for b in (7, 6, 5, 4):
             fetch_plain(b)
         gather_h(4, 0, TURN)
@@ -341,33 +319,34 @@ def tile_picked_sage_none_e_kernel(tc, xT, w1, w2, gate, offs, pos1, pos2, out):
         for b in (4, 5):
             for vb in range(2):
                 sum_hi(b, vb, "F", vb)
-        round_hi(zt_hi[:, 0:2, 0], "F", 0, 2)
-        sum_hi(4, 2, "H", 0)
-        sum_hi(5, 2, "H", 0)
-        round_hi(zt_hi[:, 2:3, 0], "H", 0, 1)
+        round_hi(0, 2, 0, "F")
+        for b in (4, 5):
+            sum_hi(b, 2, "H", 0)
+        round_hi(2, 1, 0, "H")
         for b in (6, 7):
             gather_h(b, 0, 2 * P)
             for d in range(2):
                 sum_hi(b, 0, "A", 0, (d,))
                 sum_hi(b, 1, "C", 0, (d,))
-        round_hi(zt_hi[:, 0:1, 1], "A", 0, 1)
-        round_hi(zt_hi[:, 1:2, 1], "C", 0, 1)
+        round_hi(0, 1, 1, "A")
+        round_hi(1, 1, 1, "C")
         for b in (6, 7):
             gather_h(b, 2 * P, TURN)
             sum_hi(b, 2, "F", 0)
-        round_hi(zt_hi[:, 2:3, 1], "F", 0, 1)
+        round_hi(2, 1, 1, "F")
         turn_back(zt_hi, 0, 1, z[1, 0][:, 0:P], "E")
         turn_back(zt_hi, 1, 1, z[1, 0][:, P : 2 * P], "G")
-        turn_back(zt_hi, 2, 1, z[1, 256], "B")
-        zc[0] = sb.tile([P, V], U32, name="zc_0", tag="h_4", align_bytes=64)
-        zc[1] = sb.tile([P, V], U32, name="zc_1", align_bytes=64)
-        quant_w2()
+        turn_back(zt_hi, 2, 1, z[1, 2 * P], "B")
+
+        zc_lo = sb.tile([P, V], U32, name="zc_0", tag="h_4", align_bytes=64)
+        zc_hi = sb.tile([P, V], U32, name="zc_1", align_bytes=64)
+        zc = (zc_lo, zc_hi)
+        w2c = sb.tile([P, 2 * N], U32, name="w2c", tag="h_5", align_bytes=64)
+        w2s = sb.tile([P, 2 * N], U8, name="w2s", align_bytes=64)
+        nc.vector.quantize_mx(out=w2c[:].bitcast(FP8X4), scales=w2s[:], in_=w2b[:])
         gate_plain()
-        quant_z(0, 0, 512)
-        add_z(384, 512)
-        quant_z(1, 0, 256)
-        layer2(0, 256, "E", (0, 1))
-        quant_z(1, 384, 512)
-        layer2(384, 512, "G", (0, 1))
-        quant_z(1, 256, 384)
-        layer2(256, 384, "B", (0, 1))
+        quant_z(0, 0, V)
+        add_plain()
+        for v0, v1, name in ((0, 2 * P, "E"), (TURN, V, "G"), (2 * P, TURN, "B")):
+            quant_z(1, v0, v1)
+            layer2(v0, v1, name)

@@ -32,6 +32,7 @@ def tile_picked_sage_none_e_kernel(tc, xT, w1, w2, gate, offs, pos1, pos2, out):
         offs_t = lists.tile([P, S // 16], U16, name="offs_t")
         pos1_t = lists.tile([P, V // 16], U16, name="pos1_t")
         pos2_t = lists.tile([P, V // 16], U16, name="pos2_t")
+        pos = (pos1_t, pos2_t)
 
         ident = sb.tile([P, P], F32, name="ident")
         make_identity(nc, ident[:])
@@ -57,19 +58,27 @@ def tile_picked_sage_none_e_kernel(tc, xT, w1, w2, gate, offs, pos1, pos2, out):
         nc.sync.dma_start(pos2_t[:], pos2)
         w1_view = w1.rearrange("(p j) i -> p j i", j=4)
         w1_lo = []
+        for pair in range(2):
+            raw = sb.tile([P, 4, 2 * P], F32, name="w1_lo_%d" % pair, align_bytes=64)
+            nc.sync.dma_start(raw[:], w1_view[:, :, 2 * P * pair : 2 * P * (pair + 1)])
+            w1_lo.append(raw)
         gates = sb.tile([P, 2, V], F32, name="gates")
-        for b0 in (0, 2):
-            raw = sb.tile([P, 4, 2 * P], F32, name="w1_lo_%d" % b0, align_bytes=64)
-            nc.sync.dma_start(raw[:], w1_view[:, :, P * b0 : P * b0 + 2 * P])
-            w1_lo.extend([raw[:, :, 0:P], raw[:, :, P : 2 * P]])
-        nc.sync.dma_start(gates[:], gate.rearrange("d p v -> p d v"))
-        hi_first = sb.tile([P, 4, P], F32, name="w1_hi_0")
-        hi_rest = shared.tile([P, 4, 3 * P], F32, name="w1_hi_1", offset=S)
-        w1_hi = ((hi_first, H // 2, H // 2 + P), (hi_rest, H // 2 + P, H))
-        for raw, c0, c1 in w1_hi:
-            nc.sync.dma_start(raw[:], w1_view[:, :, c0:c1])
+        w1_hi = []
+        for piece in range(2):
+            if piece:
+                raw = sb.tile([P, 4, 2 * P], F32, name="w1_hi_1", align_bytes=64)
+            else:
+                raw = shared.tile([P, 4, 2 * P], F32, name="w1_hi_0", offset=8192, align_bytes=64)
+            nc.sync.dma_start(raw[:], w1_view[:, :, 2 * P * (2 + piece) : 2 * P * (3 + piece)])
+            w1_hi.append(raw)
+            if piece == 0:
+                nc.sync.dma_start(gates[:], gate.rearrange("d p v -> p d v"))
         w2_raw = sb.tile([P, 2, 4, N], F32, name="w2_raw")
         nc.sync.dma_start(w2_raw[:], w2.rearrange("(g p t) n -> p g t n", g=2, t=4))
+        gate_col = sb.tile([P, 2, 4], F32, name="gate_col")
+        with nc.allow_non_contiguous_dma("one gate a partition"):
+            runs = gate.rearrange("d r (vb p) -> p (d r vb)", p=P)
+            nc.sync.dma_start(gate_col[:].rearrange("p d vb -> p (d vb)"), runs[:, 0 : 8 * P : P + 1])
 
         picked = []
         for half in range(2):
@@ -79,18 +88,18 @@ def tile_picked_sage_none_e_kernel(tc, xT, w1, w2, gate, offs, pos1, pos2, out):
         def slots(n0, n1):
             return picked[n0 // BANK][:].rearrange("p (n t) -> p n t", t=4)[:, n0 % BANK : n0 % BANK + n1 - n0]
 
-        def looked_up(j, q):
-            return x_raw[j][:].indirect(offs_t[:, QUARTER * q // 16 : QUARTER * (q + 1) // 16])
+        def looked_up(j, q0, q1):
+            return x_raw[j][:].indirect(offs_t[:, QUARTER * q0 // 16 : QUARTER * q1 // 16])
 
         fetched = {}
         for q in range(1, 4):
             ft = sb.tile([P, 4, QUARTER], BF16, name="fetched_%d" % (QUARTER * q), align_bytes=64)
             fetched[q] = ft
 
-        def gather_plane(j):
-            nc.vector.tensor_copy(slots(0, QUARTER)[:, :, j], looked_up(j, 0))
-            for q in range(1, 4):
-                nc.scalar.activation(fetched[q][:, j, :], looked_up(j, q), COPY)
+        def gather_plane(j, own):
+            nc.vector.tensor_copy(slots(0, QUARTER * own)[:, :, j], looked_up(j, 0, own))
+            for q in range(own, 4):
+                nc.scalar.activation(fetched[q][:, j, :], looked_up(j, q, q + 1), COPY)
 
         def place(j0, j1, q):
             dst = slots(QUARTER * q, QUARTER * (q + 1))[:, :, j0:j1]
@@ -113,44 +122,50 @@ def tile_picked_sage_none_e_kernel(tc, xT, w1, w2, gate, offs, pos1, pos2, out):
 
         w1b, w1c, w1s = {}, {}, {}
 
-        def round_w1_lo(b):
-            own = sb.tile([P, 4 * P], BF16, name="w1b_%d" % b, align_bytes=64)
-            dst = own[:].rearrange("p (c i j) -> p c j i", i=4, j=4)
-            nc.scalar.copy(dst, w1_lo[b].rearrange("p j (c i) -> p c j i", i=4))
-            w1b[b] = (own[:], 1)
+        def round_w1_lo(pair):
+            own = sb.tile([P, 2, 4 * P], BF16, name="w1b_lo_%d" % pair, align_bytes=64)
+            dst = own[:].rearrange("p u (c e j) -> p c j u e", e=2, j=4)
+            nc.scalar.copy(dst, w1_lo[pair][:].rearrange("p j (c u e) -> p c j u e", u=2, e=2))
+            if pair:
+                w1b[2] = (own[:].rearrange("p u c -> p (u c)"), 2)
+            else:
+                w1b[0], w1b[1] = (own[:, 0, :], 1), (own[:, 1, :], 1)
 
         w1b_hi = sb.tile([P, 16 * P], BF16, name="w1b_4", align_bytes=64)
         w1b[4] = (w1b_hi[:], 4)
 
         def round_w1_hi(piece):
-            raw, c0, c1 = w1_hi[piece]
-            dst = w1b_hi[:].rearrange("p (t m j) -> p m j t", t=4, j=4)[:, (c0 - H // 2) // 4 : (c1 - H // 2) // 4]
-            nc.scalar.copy(dst, raw[:].rearrange("p j (m t) -> p m j t", t=4))
+            dst = w1b_hi[:].rearrange("p (t m j) -> p m t j", t=4, j=4)[:, 64 * piece : 64 * piece + 64]
+            nc.vector.tensor_copy(dst, w1_hi[piece][:].rearrange("p j (m t) -> p m t j", t=4))
 
         def quant_w1(b0):
             wide, parts = w1b[b0]
-            codes = sb.tile([P, P * parts], U32, name="w1c_%d" % b0, align_bytes=64)
+            if b0 == 2:
+                codes = shared.tile([P, P * parts], U32, name="w1c_%d" % b0, offset=8192 + 512 * (b0 - 1), align_bytes=64)
+            else:
+                codes = sb.tile([P, P * parts], U32, name="w1c_%d" % b0, align_bytes=64)
             scales = sb.tile([P, P * parts], U8, name="w1s_%d" % b0, align_bytes=64)
             nc.vector.quantize_mx(out=codes[:].bitcast(FP8X4), scales=scales[:], in_=wide)
             for i in range(parts):
                 w1c[b0 + i] = codes[:, P * i : P * i + P]
                 w1s[b0 + i] = scales[:, P * i : P * i + P]
 
-        w2b = sb.tile([P, 8 * N], BF16, name="w2b", align_bytes=64)
+        w2c = sb.tile([P, 2 * N], U32, name="w2c", align_bytes=64)
+        w2s = sb.tile([P, 2 * N], U8, name="w2s", align_bytes=64)
 
-        def round_w2():
+        def make_w2():
             dst = w2b[:].rearrange("p (g c i t) -> p g c t i", g=2, i=4, t=4)
             nc.scalar.copy(dst, w2_raw[:].rearrange("p g t (c i) -> p g c t i", i=4))
 
+        def quant_w2():
+            nc.vector.quantize_mx(out=w2c[:].bitcast(FP8X4), scales=w2s[:], in_=w2b[:])
+
         h = {}
 
-        def layer1(b, banks, cuts=(0, BANK, S)):
-            if b == 3:
-                ht = shared.tile([P, S], F32, name="h_3", offset=0)
-            else:
-                ht = sb.tile([P, S], F32, name="h_%d" % b, align_bytes=64)
+        def layer1(b, banks, engines, cuts=(0, BANK, S)):
+            ht = sb.tile([P, S], F32, name="h_%d" % b, align_bytes=64)
             h[b] = ht
-            for name, n0, n1 in zip(banks, cuts, cuts[1:]):
+            for name, engine, n0, n1 in zip(banks, engines, cuts, cuts[1:]):
                 acc = bank[name][:, 0 : n1 - n0]
                 cols = slice(n0 % BANK, n0 % BANK + n1 - n0)
                 nc.tensor.matmul_mx(
@@ -162,86 +177,78 @@ def tile_picked_sage_none_e_kernel(tc, xT, w1, w2, gate, offs, pos1, pos2, out):
                     start=True,
                     stop=True,
                 )
-                if n1 - n0 == P:
+                if engine == "V":
                     nc.vector.tensor_copy(ht[:, n0:n1], acc)
                 else:
                     nc.scalar.copy(ht[:, n0:n1], acc)
 
-        pos = (pos1_t, pos2_t)
         term = {}
 
-        def make_low_terms():
-            for b in range(4):
-                if b == 2:
-                    both = shared.tile([P, 2 * V], F32, name="term_2", offset=4 * S)
-                else:
-                    both = sb.tile([P, 2 * V], F32, name="term_%d" % b, tag="term_%d" % b if b else "w1b_3", align_bytes=64)
-                for d in range(2):
-                    term[b, d] = both[:, V * d : V * d + V]
+        def piece(b, d, v0, v1):
+            if (b, d) == (3, 0) and v0 >= 2 * P:
+                return rest[:, v0 - 2 * P : v1 - 2 * P]
+            return term[b, d][:, v0:v1]
 
-        turned = sb.tile([P, 2, 4 * TURN], F32, name="term_turned")
-        for d in range(2):
-            for t in range(4):
-                term[4 + t, d] = turned[:, d, TURN * t : TURN * t + TURN]
-        added = turned[:, :, TURN - P : 2 * TURN].rearrange("p d (t v) -> p d t v", t=4)
+        def new_term(b, d, width, tag=None):
+            name = "term_%d_%d" % (b, d)
+            own = sb.tile([P, width], F32, name=name, tag=tag or name, align_bytes=64)
+            term[b, d] = own
 
-        def gather_h(b, v0, v1):
+        def gather_gated(b, d, v1):
+            nc.vector.tensor_tensor(term[b, d][:], h[b][:].indirect(pos[d][:, 0 : v1 // 16]), gates[:, d, 0:v1], MULT)
+
+        def gather_plain(b, d, v0=0, v1=V):
+            nc.scalar.activation(piece(b, d, v0, v1), h[b][:].indirect(pos[d][:, v0 // 16 : v1 // 16]), COPY)
+
+        def add_turned(dst, b, v):
             for d in range(2):
-                nc.vector.tensor_tensor(
-                    term[b, d][:, v0:v1],
-                    h[b][:].indirect(pos[d][:, v0 // 16 : v1 // 16]),
-                    gates[:, d, v0:v1],
-                    MULT,
-                )
-
-        def add_turned(dst, b, v, turns=(0, 1)):
-            for d in turns:
                 nc.tensor.matmul(
                     out=dst, lhsT=term[b, d][:, v : v + P], rhs=ident[:], start=d == 0, stop=d == 1, is_transpose=True
                 )
 
-        zt_lo = sb.tile([P, 4, 2, P, 2], BF16, name="zt_lo", align_bytes=64)
+        zt_lo = sb.tile([P, 4, 2, 2, P], BF16, name="zt_lo", align_bytes=64)
         zt_hi = sb.tile([P, 3, 2, P, 2], BF16, name="zt_hi", align_bytes=64)
-        z = {}
-        for g, v0, v1 in ((0, 0, V), (1, 0, 2 * P), (1, 2 * P, TURN), (1, TURN, V)):
-            zg = sb.tile([P, v1 - v0, 4], BF16, name="z_%d_%d" % (g, v0), align_bytes=64)
-            z[g, v0] = zg[:]
-
-        plain = sb.tile([P, 2, 4, P], F32, name="plain", tag="zt_lo", align_bytes=64)
-
-        def fetch_plain(b):
-            for d in range(2):
-                nc.scalar.activation(plain[:, d, b - 4, :], h[b][:].indirect(pos[d][:, TURN // 16 : V // 16]), COPY)
-
-        def gate_plain():
-            spread = gates[:, :, TURN:V].unsqueeze(2).to_broadcast([P, 2, 4, P])
-            nc.vector.tensor_tensor(added, plain[:], spread, MULT)
-
-        def add_plain():
-            dst = z[1, TURN].rearrange("p (c i) t -> p c t i", i=4)
-            first = added[:, 0].rearrange("p t (c i) -> p c t i", i=4)
-            second = added[:, 1].rearrange("p t (c i) -> p c t i", i=4)
-            nc.vector.tensor_tensor(dst, first, second, ADD)
+        first = shared.tile([P, 4, 2 * P], F32, name="first", offset=0, align_bytes=64)
 
         def fold_lo(b, name):
-            sums = bank[name][:].rearrange("p (vb c) -> p vb c", vb=4)
+            sums = bank[name][:].rearrange("p (vb q) -> p vb q", vb=4)
             for vb in range(4):
                 add_turned(sums[:, vb], b, P * vb)
-            nc.scalar.copy(
-                zt_lo[:, :, :, 32 * b : 32 * b + 32, :], sums.rearrange("p vb (m u e) -> p vb u m e", u=2, e=2)
+            nc.scalar.copy(zt_lo[:, :, b, 0, :], sums)
+
+        def turned(d, vb):
+            return bank["ABEF"[2 * d + vb // 2]][:, 2 * P * (vb % 2) : 2 * P * (vb % 2 + 1)]
+
+        def turn(b, d):
+            for vb in range(4):
+                dst = turned(d, vb)[:, P * (b % 2) : P * (b % 2 + 1)]
+                nc.tensor.transpose(dst, piece(b, d, P * vb, P * vb + P), ident[:])
+
+        def weigh_first(vb):
+            nc.scalar.activation(first[:, vb, :], turned(0, vb), COPY, scale=gate_col[:, 0, vb : vb + 1])
+
+        def weigh_second(vb):
+            nc.vector.scalar_tensor_tensor(
+                out=zt_lo[:, vb, :, 1, :],
+                in0=turned(1, vb).rearrange("p (u q) -> p u q", u=2),
+                scalar=gate_col[:, 1, vb : vb + 1],
+                in1=first[:, vb, :].rearrange("p (u q) -> p u q", u=2),
+                op0=MULT,
+                op1=ADD,
             )
 
-        def sum_hi(b, vb, name, q, turns=(0, 1)):
-            sums = bank[name][:].rearrange("p (q e m) -> p q e m", q=2, e=2)
-            add_turned(sums[:, q, b % 2], b, P * vb, turns)
+        def fold_hi(u, names):
+            for name, vb0, count in zip(names, (0, 2), (2, 1)):
+                sums = bank[name][:].rearrange("p (q e m) -> p q e m", q=2, e=2)
+                for e in range(2):
+                    for q in range(count):
+                        add_turned(sums[:, q, e], 4 + 2 * u + e, P * (vb0 + q))
+            for name, vb0, count in zip(names, (0, 2), (2, 1)):
+                sums = bank[name][:].rearrange("p (q e m) -> p q m e", q=2, e=2)
+                nc.scalar.copy(zt_hi[:, vb0 : vb0 + count, u], sums[:, 0:count])
 
-        def round_hi(vb0, count, u, name):
-            sums = bank[name][:].rearrange("p (q e m) -> p q m e", q=2, e=2)
-            nc.scalar.copy(zt_hi[:, vb0 : vb0 + count, u], sums[:, 0:count])
-
-        def turn_back(zt, vb0, count, dst, name):
+        def turn_back(words, vb0, count, dst, name):
             back = bank[name][:, 0 : 2 * P * count].rearrange("p (u v) -> p u v", u=2)
-            words = zt[:].rearrange("p vb u m e -> p (vb u m e)").bitcast(F32)
             for vb in range(count):
                 for u in range(2):
                     w0 = P * (2 * (vb0 + vb) + u)
@@ -249,104 +256,136 @@ def tile_picked_sage_none_e_kernel(tc, xT, w1, w2, gate, offs, pos1, pos2, out):
             dst_words = dst.rearrange("p v t -> p (v t)").bitcast(F32)
             nc.scalar.copy(dst_words.rearrange("p (v u) -> p v u", u=2), back.rearrange("p u v -> p v u"))
 
-        zs = []
+        z_lo = []
+        for half in range(2):
+            zl = sb.tile([P, 2 * P, 4], BF16, name="z_lo_%d" % half, align_bytes=64)
+            z_lo.append(zl)
+        z_hi = sb.tile([P, TURN, 4], BF16, name="z_hi", align_bytes=64)
+
+        last = {}
+
+        def gather_last(d):
+            if d:
+                own = shared.tile([P, 4, V - TURN], F32, name="last_1", offset=0, align_bytes=64)
+            else:
+                own = sb.tile([P, 4, V - TURN], F32, name="last_0", tag="h_2", align_bytes=64)
+            last[d] = own
+            for t in range(4):
+                looked = h[4 + t][:].indirect(pos[d][:, TURN // 16 : V // 16])
+                nc.vector.tensor_tensor(own[:, t, :], looked, gates[:, d, TURN:V], MULT)
+
+        def add_last():
+            z_last = sb.tile([P, V - TURN, 4], BF16, name="z_last", align_bytes=64)
+            dst = z_last[:].rearrange("p (c i) t -> p c t i", i=4)
+            one = last[0][:].rearrange("p t (c i) -> p c t i", i=4)
+            two = last[1][:].rearrange("p t (c i) -> p c t i", i=4)
+            nc.vector.tensor_tensor(dst, one, two, ADD)
+            return z_last
+
+        zc, zs = [], []
         for g in range(2):
+            zcg = sb.tile([P, V], U32, name="zc_%d" % g, align_bytes=64)
             zsg = sb.tile([P, V], U8, name="zs_%d" % g, align_bytes=64)
+            zc.append(zcg)
             zs.append(zsg)
 
-        def quant_z(g, v0, v1):
+        def quant_z(g, v0, v1, rounded):
             nc.vector.quantize_mx(
                 out=zc[g][:, v0:v1].bitcast(FP8X4),
                 scales=zs[g][:, v0:v1],
-                in_=z[g, v0].rearrange("p v t -> p (v t)"),
+                in_=rounded.rearrange("p v t -> p (v t)"),
             )
 
-        def layer2(v0, v1, name):
+        def layer2(v0, v1, name, passes):
             acc = bank[name][:, 0 : v1 - v0]
-            for g in range(2):
+            for g in passes:
                 nc.tensor.matmul_mx(
                     out=acc,
                     lhsT=w2c[:, N * g : N * g + N].bitcast(FP8X4),
                     lhsT_scale=w2s[:, N * g : N * g + N],
                     rhs=zc[g][:, v0:v1].bitcast(FP8X4),
                     rhs_scale=zs[g][:, v0:v1],
-                    start=g == 0,
-                    stop=g == 1,
+                    start=g == passes[0],
+                    stop=g == passes[1],
                 )
             out_t = sb.tile([P, v1 - v0], F32, name="out_%d" % v0)
             nc.scalar.copy(out_t[:], acc)
             nc.sync.dma_start(out[:, v0:v1], out_t[:])
 
         for j in range(4):
-            gather_plane(j)
-            for q in range(1, 4 if j < 2 else 2):
+            gather_plane(j, 2 if j == 3 else 1)
+            for q in range(1, (4, 4, 2, 1)[j]):
                 place(j, j + 1, q)
-        for b in range(4):
-            round_w1_lo(b)
+        for pair in range(2):
+            round_w1_lo(pair)
         place(2, 4, 2)
         quant_x(0, BANK)
-        place(2, 4, 3)
         quant_w1(0)
-        head_cuts = (0, BANK, 3 * QUARTER, S - P, S)
-        for n0, n1 in zip(head_cuts[1:], head_cuts[2:]):
-            quant_x(n0, n1)
-        for b in range(1, 4):
-            quant_w1(b)
-        layer1(0, "ABGH", head_cuts)
+        place(2, 4, 3)
+        quant_x(BANK, 3 * QUARTER)
+        quant_x(3 * QUARTER, S)
+        quant_w1(1)
+        layer1(0, "ABG", "SSS", (0, BANK, 3 * QUARTER, S))
         round_w1_hi(0)
-        layer1(1, "CD")
-        layer1(2, "AB")
+        quant_w1(2)
+        layer1(1, "CD", "SS")
+        one = shared.tile([P, V], F32, name="term_0_0", offset=8192 + 2048, align_bytes=64)
+        term[0, 0] = one[:]
+        gather_gated(0, 0, V)
         round_w1_hi(1)
+        new_term(0, 1, V, "w1_hi_1")
+        gather_gated(0, 1, V)
         quant_w1(4)
-        layer1(3, "CD")
-
-        make_low_terms()
-        gather_h(0, 0, V)
-        fold_lo(0, "A")
-        round_w2()
-        for b, banks in zip(range(1, 4), ("EF", "GH", "BD")):
-            layer1(3 + b, banks)
-            gather_h(b, 0, V)
-            fold_lo(b, "AC"[b % 2])
-        layer1(7, "FH")
-        turn_back(zt_lo, 0, 2, z[0, 0][:, 0 : 2 * P], "A")
-        turn_back(zt_lo, 2, 2, z[0, 0][:, 2 * P : V], "C")
-
-        for b in (7, 6, 5, 4):
-            fetch_plain(b)
-        gather_h(4, 0, TURN)
-        gather_h(5, 0, TURN)
-        for b in (4, 5):
-            for vb in range(2):
-                sum_hi(b, vb, "F", vb)
-        round_hi(0, 2, 0, "F")
-        for b in (4, 5):
-            sum_hi(b, 2, "H", 0)
-        round_hi(2, 1, 0, "H")
-        for b in (6, 7):
-            gather_h(b, 0, 2 * P)
+        early = sb.tile([P, 2, V], F32, name="term_1", tag="w1b_4", align_bytes=64)
+        for d in range(2):
+            term[1, d] = early[:, d, :]
+            gather_gated(1, d, V)
+        layer1(2, "AB", "SS")
+        layer1(3, "EF", "SS")
+        new_term(2, 0, V)
+        gather_plain(2, 0)
+        new_term(3, 0, 2 * P)
+        gather_plain(3, 0, 0, 2 * P)
+        layer1(4, "GH", "SS")
+        layer1(5, "CD", "SS")
+        layer1(6, "AB", "SS")
+        layer1(7, "EF", "SS")
+        for b in range(4, 8):
             for d in range(2):
-                sum_hi(b, 0, "A", 0, (d,))
-                sum_hi(b, 1, "C", 0, (d,))
-        round_hi(0, 1, 1, "A")
-        round_hi(1, 1, 1, "C")
-        for b in (6, 7):
-            gather_h(b, 2 * P, TURN)
-            sum_hi(b, 2, "F", 0)
-        round_hi(2, 1, 1, "F")
-        turn_back(zt_hi, 0, 1, z[1, 0][:, 0:P], "E")
-        turn_back(zt_hi, 1, 1, z[1, 0][:, P : 2 * P], "G")
-        turn_back(zt_hi, 2, 1, z[1, 2 * P], "B")
-
-        zc_lo = sb.tile([P, V], U32, name="zc_0", tag="h_4", align_bytes=64)
-        zc_hi = sb.tile([P, V], U32, name="zc_1", align_bytes=64)
-        zc = (zc_lo, zc_hi)
-        w2c = sb.tile([P, 2 * N], U32, name="w2c", tag="h_5", align_bytes=64)
-        w2s = sb.tile([P, 2 * N], U8, name="w2s", align_bytes=64)
-        nc.vector.quantize_mx(out=w2c[:].bitcast(FP8X4), scales=w2s[:], in_=w2b[:])
-        gate_plain()
-        quant_z(0, 0, V)
-        add_plain()
-        for v0, v1, name in ((0, 2 * P, "E"), (TURN, V, "G"), (2 * P, TURN, "B")):
-            quant_z(1, v0, v1)
-            layer2(v0, v1, name)
+                new_term(b, d, TURN)
+                gather_gated(b, d, TURN)
+        new_term(2, 1, V, "w1c_4")
+        gather_plain(2, 1)
+        rest = sb.tile([P, 2 * P], F32, name="term_rest", tag="w1_lo_0", align_bytes=64)
+        gather_plain(3, 0, 2 * P, V)
+        new_term(3, 1, V, "xc_0")
+        gather_plain(3, 1)
+        gather_last(0)
+        for d in range(2):
+            for b in (2, 3):
+                turn(b, d)
+        for vb in range(4):
+            weigh_first(vb)
+            weigh_second(vb)
+        gather_last(1)
+        fold_lo(0, "G")
+        fold_lo(1, "H")
+        fold_hi(0, "CD")
+        fold_hi(1, "GH")
+        w2b = sb.tile([P, 8 * N], BF16, name="w2b", tag="h_3", align_bytes=64)
+        make_w2()
+        words_hi = zt_hi[:].rearrange("p vb u m e -> p (vb u m e)").bitcast(F32)
+        words_lo = zt_lo[:].rearrange("p vb u r q -> p (vb u r q)").bitcast(F32)
+        turn_back(words_lo, 0, 2, z_lo[0][:], "A")
+        turn_back(words_lo, 2, 2, z_lo[1][:], "B")
+        turn_back(words_hi, 0, 2, z_hi[:, 0 : 2 * P], "C")
+        turn_back(words_hi, 2, 1, z_hi[:, 2 * P : TURN], "D")
+        z_last = add_last()
+        quant_w2()
+        quant_z(1, TURN, V, z_last[:])
+        quant_z(0, 0, 2 * P, z_lo[0][:])
+        quant_z(0, 2 * P, V, z_lo[1][:])
+        quant_z(1, 0, 2 * P, z_hi[:, 0 : 2 * P])
+        quant_z(1, 2 * P, TURN, z_hi[:, 2 * P : TURN])
+        layer2(0, 2 * P, "E", (0, 1))
+        layer2(2 * P, V, "F", (0, 1))

@@ -135,8 +135,8 @@ def tile_picked_sage_none_e_kernel(tc, xT, w1, w2, gate, offs, pos1, pos2, out):
         w1b[4] = (w1b_hi[:], 4)
 
         def round_w1_hi(piece):
-            dst = w1b_hi[:].rearrange("p (t m j) -> p m t j", t=4, j=4)[:, 64 * piece : 64 * piece + 64]
-            nc.vector.tensor_copy(dst, w1_hi[piece][:].rearrange("p j (m t) -> p m t j", t=4))
+            dst = w1b_hi[:].rearrange("p (t m j) -> p m j t", t=4, j=4)[:, 64 * piece : 64 * piece + 64]
+            nc.vector.tensor_copy(dst, w1_hi[piece][:].rearrange("p j (m t) -> p m j t", t=4))
 
         def quant_w1(b0):
             wide, parts = w1b[b0]

@@ -26,7 +26,6 @@ def tile_picked_sage_none_e_kernel(tc, xT, w1, w2, gate, offs, pos1, pos2, out):
     with ExitStack() as ctx:
         lists = ctx.enter_context(tc.tile_pool(name="lists", bufs=1))
         sb = ctx.enter_context(tc.tile_pool(name="sb", bufs=1))
-        shared = ctx.enter_context(tc.tile_pool(name="shared", bufs=1))
         ps = ctx.enter_context(tc.psum_pool(name="ps", bufs=1))
 
         offs_t = lists.tile([P, S // 16], U16, name="offs_t")
@@ -54,8 +53,6 @@ def tile_picked_sage_none_e_kernel(tc, xT, w1, w2, gate, offs, pos1, pos2, out):
             x_raw.append(raw)
             if j == 0:
                 nc.sync.dma_start(offs_t[:], offs)
-        nc.sync.dma_start(pos1_t[:], pos1)
-        nc.sync.dma_start(pos2_t[:], pos2)
         w1_view = w1.rearrange("(p j) i -> p j i", j=4)
         w1_lo = []
         for pair in range(2):
@@ -65,14 +62,13 @@ def tile_picked_sage_none_e_kernel(tc, xT, w1, w2, gate, offs, pos1, pos2, out):
         gates = sb.tile([P, 2, V], F32, name="gates")
         w1_hi = []
         for piece in range(2):
-            if piece:
-                raw = sb.tile([P, 4, 2 * P], F32, name="w1_hi_1", align_bytes=64)
-            else:
-                raw = shared.tile([P, 4, 2 * P], F32, name="w1_hi_0", offset=8192, align_bytes=64)
+            raw = sb.tile([P, 4, 2 * P], F32, name="w1_hi_%d" % piece, align_bytes=64)
             nc.sync.dma_start(raw[:], w1_view[:, :, 2 * P * (2 + piece) : 2 * P * (3 + piece)])
             w1_hi.append(raw)
             if piece == 0:
+                nc.sync.dma_start(pos1_t[:], pos1)
                 nc.sync.dma_start(gates[:], gate.rearrange("d p v -> p d v"))
+        nc.sync.dma_start(pos2_t[:], pos2)
         w2_raw = sb.tile([P, 2, 4, N], F32, name="w2_raw")
         nc.sync.dma_start(w2_raw[:], w2.rearrange("(g p t) n -> p g t n", g=2, t=4))
         gate_col = sb.tile([P, 2, 4], F32, name="gate_col")
@@ -140,10 +136,7 @@ def tile_picked_sage_none_e_kernel(tc, xT, w1, w2, gate, offs, pos1, pos2, out):
 
         def quant_w1(b0):
             wide, parts = w1b[b0]
-            if b0 == 2:
-                codes = shared.tile([P, P * parts], U32, name="w1c_%d" % b0, offset=8192 + 512 * (b0 - 1), align_bytes=64)
-            else:
-                codes = sb.tile([P, P * parts], U32, name="w1c_%d" % b0, align_bytes=64)
+            codes = sb.tile([P, P * parts], U32, name="w1c_%d" % b0, align_bytes=64)
             scales = sb.tile([P, P * parts], U8, name="w1s_%d" % b0, align_bytes=64)
             nc.vector.quantize_mx(out=codes[:].bitcast(FP8X4), scales=scales[:], in_=wide)
             for i in range(parts):
@@ -208,7 +201,10 @@ def tile_picked_sage_none_e_kernel(tc, xT, w1, w2, gate, offs, pos1, pos2, out):
 
         zt_lo = sb.tile([P, 4, 2, 2, P], BF16, name="zt_lo", align_bytes=64)
         zt_hi = sb.tile([P, 3, 2, P, 2], BF16, name="zt_hi", align_bytes=64)
-        first = shared.tile([P, 4, 2 * P], F32, name="first", offset=0, align_bytes=64)
+        first = []
+        for half in range(2):
+            ft = sb.tile([P, 2, 2 * P], F32, name="first_%d" % half, align_bytes=64)
+            first.append(ft)
 
         def fold_lo(b, name):
             sums = bank[name][:].rearrange("p (vb q) -> p vb q", vb=4)
@@ -225,14 +221,14 @@ def tile_picked_sage_none_e_kernel(tc, xT, w1, w2, gate, offs, pos1, pos2, out):
                 nc.tensor.transpose(dst, piece(b, d, P * vb, P * vb + P), ident[:])
 
         def weigh_first(vb):
-            nc.scalar.activation(first[:, vb, :], turned(0, vb), COPY, scale=gate_col[:, 0, vb : vb + 1])
+            nc.scalar.activation(first[vb // 2][:, vb % 2, :], turned(0, vb), COPY, scale=gate_col[:, 0, vb : vb + 1])
 
         def weigh_second(vb):
             nc.vector.scalar_tensor_tensor(
                 out=zt_lo[:, vb, :, 1, :],
                 in0=turned(1, vb).rearrange("p (u q) -> p u q", u=2),
                 scalar=gate_col[:, 1, vb : vb + 1],
-                in1=first[:, vb, :].rearrange("p (u q) -> p u q", u=2),
+                in1=first[vb // 2][:, vb % 2, :].rearrange("p (u q) -> p u q", u=2),
                 op0=MULT,
                 op1=ADD,
             )
@@ -265,10 +261,7 @@ def tile_picked_sage_none_e_kernel(tc, xT, w1, w2, gate, offs, pos1, pos2, out):
         last = {}
 
         def gather_last(d):
-            if d:
-                own = shared.tile([P, 4, V - TURN], F32, name="last_1", offset=0, align_bytes=64)
-            else:
-                own = sb.tile([P, 4, V - TURN], F32, name="last_0", tag="h_2", align_bytes=64)
+            own = sb.tile([P, 4, V - TURN], F32, name="last_%d" % d, tag=("h_2", "first_0")[d], align_bytes=64)
             last[d] = own
             for t in range(4):
                 looked = h[4 + t][:].indirect(pos[d][:, TURN // 16 : V // 16])
@@ -308,9 +301,13 @@ def tile_picked_sage_none_e_kernel(tc, xT, w1, w2, gate, offs, pos1, pos2, out):
                     start=g == passes[0],
                     stop=g == passes[1],
                 )
-            out_t = sb.tile([P, v1 - v0], F32, name="out_%d" % v0)
-            nc.scalar.copy(out_t[:], acc)
-            nc.sync.dma_start(out[:, v0:v1], out_t[:])
+            half = v0 // (2 * P)
+            nc.scalar.copy(out_t[half][:, v0 % (2 * P) : v0 % (2 * P) + v1 - v0], acc)
+
+        out_t = []
+        for half in range(2):
+            ot = sb.tile([P, 2 * P], F32, name="out_%d" % half)
+            out_t.append(ot)
 
         for j in range(4):
             gather_plane(j, 2 if j == 3 else 1)
@@ -329,16 +326,15 @@ def tile_picked_sage_none_e_kernel(tc, xT, w1, w2, gate, offs, pos1, pos2, out):
         round_w1_hi(0)
         quant_w1(2)
         layer1(1, "CD", "SS")
-        one = shared.tile([P, V], F32, name="term_0_0", offset=8192 + 2048, align_bytes=64)
-        term[0, 0] = one[:]
+        new_term(0, 0, V)
         gather_gated(0, 0, V)
         round_w1_hi(1)
-        new_term(0, 1, V, "w1_hi_1")
+        early = sb.tile([P, 2, V], F32, name="term_1", tag="w1_hi_1", align_bytes=64)
+        term[1, 0], term[1, 1] = early[:, 0, :], early[:, 1, :]
+        new_term(0, 1, V)
         gather_gated(0, 1, V)
         quant_w1(4)
-        early = sb.tile([P, 2, V], F32, name="term_1", tag="w1b_4", align_bytes=64)
         for d in range(2):
-            term[1, d] = early[:, d, :]
             gather_gated(1, d, V)
         layer1(2, "AB", "SS")
         layer1(3, "EF", "SS")
@@ -356,6 +352,8 @@ def tile_picked_sage_none_e_kernel(tc, xT, w1, w2, gate, offs, pos1, pos2, out):
                 gather_gated(b, d, TURN)
         new_term(2, 1, V, "w1c_4")
         gather_plain(2, 1)
+        fold_lo(0, "G")
+        fold_lo(1, "H")
         rest = sb.tile([P, 2 * P], F32, name="term_rest", tag="w1_lo_0", align_bytes=64)
         gather_plain(3, 0, 2 * P, V)
         new_term(3, 1, V, "xc_0")
@@ -368,8 +366,6 @@ def tile_picked_sage_none_e_kernel(tc, xT, w1, w2, gate, offs, pos1, pos2, out):
             weigh_first(vb)
             weigh_second(vb)
         gather_last(1)
-        fold_lo(0, "G")
-        fold_lo(1, "H")
         fold_hi(0, "CD")
         fold_hi(1, "GH")
         w2b = sb.tile([P, 8 * N], BF16, name="w2b", tag="h_3", align_bytes=64)
@@ -377,15 +373,18 @@ def tile_picked_sage_none_e_kernel(tc, xT, w1, w2, gate, offs, pos1, pos2, out):
         words_hi = zt_hi[:].rearrange("p vb u m e -> p (vb u m e)").bitcast(F32)
         words_lo = zt_lo[:].rearrange("p vb u r q -> p (vb u r q)").bitcast(F32)
         turn_back(words_lo, 0, 2, z_lo[0][:], "A")
-        turn_back(words_lo, 2, 2, z_lo[1][:], "B")
         turn_back(words_hi, 0, 2, z_hi[:, 0 : 2 * P], "C")
+        turn_back(words_lo, 2, 2, z_lo[1][:], "B")
         turn_back(words_hi, 2, 1, z_hi[:, 2 * P : TURN], "D")
-        z_last = add_last()
         quant_w2()
-        quant_z(1, TURN, V, z_last[:])
+        z_last = add_last()
         quant_z(0, 0, 2 * P, z_lo[0][:])
-        quant_z(0, 2 * P, V, z_lo[1][:])
+        quant_z(1, TURN, V, z_last[:])
         quant_z(1, 0, 2 * P, z_hi[:, 0 : 2 * P])
-        quant_z(1, 2 * P, TURN, z_hi[:, 2 * P : TURN])
         layer2(0, 2 * P, "E", (0, 1))
-        layer2(2 * P, V, "F", (0, 1))
+        nc.sync.dma_start(out[:, 0 : 2 * P], out_t[0][:])
+        quant_z(0, 2 * P, V, z_lo[1][:])
+        quant_z(1, 2 * P, TURN, z_hi[:, 2 * P : TURN])
+        layer2(TURN, V, "G", (1, 0))
+        layer2(2 * P, TURN, "F", (0, 1))
+        nc.sync.dma_start(out[:, 2 * P : V], out_t[1][:])

@@ -143,15 +143,9 @@ def tile_picked_sage_none_e_kernel(tc, xT, w1, w2, gate, offs, pos1, pos2, out):
                 w1c[b0 + i] = codes[:, P * i : P * i + P]
                 w1s[b0 + i] = scales[:, P * i : P * i + P]
 
-        w2c = sb.tile([P, 2 * N], U32, name="w2c", align_bytes=64)
-        w2s = sb.tile([P, 2 * N], U8, name="w2s", align_bytes=64)
-
         def make_w2():
-            dst = w2b[:].rearrange("p (g c i t) -> p g c t i", g=2, i=4, t=4)
+            dst = joined[:, 0 : 8 * N].rearrange("p (g c i t) -> p g c t i", g=2, i=4, t=4)
             nc.scalar.copy(dst, w2_raw[:].rearrange("p g t (c i) -> p g c t i", i=4))
-
-        def quant_w2():
-            nc.vector.quantize_mx(out=w2c[:].bitcast(FP8X4), scales=w2s[:], in_=w2b[:])
 
         h = {}
 
@@ -187,8 +181,9 @@ def tile_picked_sage_none_e_kernel(tc, xT, w1, w2, gate, offs, pos1, pos2, out):
             own = sb.tile([P, width], F32, name=name, tag=tag or name, align_bytes=64)
             term[b, d] = own
 
-        def gather_gated(b, d, v1):
-            nc.vector.tensor_tensor(term[b, d][:], h[b][:].indirect(pos[d][:, 0 : v1 // 16]), gates[:, d, 0:v1], MULT)
+        def gather_gated(b, d, v1, v0=0):
+            looked = h[b][:].indirect(pos[d][:, v0 // 16 : v1 // 16])
+            nc.vector.tensor_tensor(term[b, d][:, v0:v1], looked, gates[:, d, v0:v1], MULT)
 
         def gather_plain(b, d, v0=0, v1=V):
             nc.scalar.activation(piece(b, d, v0, v1), h[b][:].indirect(pos[d][:, v0 // 16 : v1 // 16]), COPY)
@@ -202,8 +197,8 @@ def tile_picked_sage_none_e_kernel(tc, xT, w1, w2, gate, offs, pos1, pos2, out):
         zt_lo = sb.tile([P, 4, 2, 2, P], BF16, name="zt_lo", align_bytes=64)
         zt_hi = sb.tile([P, 3, 2, P, 2], BF16, name="zt_hi", align_bytes=64)
         first = []
-        for half in range(2):
-            ft = sb.tile([P, 2, 2 * P], F32, name="first_%d" % half, align_bytes=64)
+        for vb in range(4):
+            ft = sb.tile([P, 2 * P], F32, name="first_%d" % vb, align_bytes=64)
             first.append(ft)
 
         def fold_lo(b, name):
@@ -221,14 +216,14 @@ def tile_picked_sage_none_e_kernel(tc, xT, w1, w2, gate, offs, pos1, pos2, out):
                 nc.tensor.transpose(dst, piece(b, d, P * vb, P * vb + P), ident[:])
 
         def weigh_first(vb):
-            nc.scalar.activation(first[vb // 2][:, vb % 2, :], turned(0, vb), COPY, scale=gate_col[:, 0, vb : vb + 1])
+            nc.scalar.activation(first[vb][:], turned(0, vb), COPY, scale=gate_col[:, 0, vb : vb + 1])
 
         def weigh_second(vb):
             nc.vector.scalar_tensor_tensor(
                 out=zt_lo[:, vb, :, 1, :],
                 in0=turned(1, vb).rearrange("p (u q) -> p u q", u=2),
                 scalar=gate_col[:, 1, vb : vb + 1],
-                in1=first[vb // 2][:, vb % 2, :].rearrange("p (u q) -> p u q", u=2),
+                in1=first[vb][:].rearrange("p (u q) -> p u q", u=2),
                 op0=MULT,
                 op1=ADD,
             )
@@ -249,57 +244,49 @@ def tile_picked_sage_none_e_kernel(tc, xT, w1, w2, gate, offs, pos1, pos2, out):
                 for u in range(2):
                     w0 = P * (2 * (vb0 + vb) + u)
                     nc.tensor.transpose(back[:, u, P * vb : P * vb + P], words[:, w0 : w0 + P], ident[:])
-            dst_words = dst.rearrange("p v t -> p (v t)").bitcast(F32)
+            dst_words = dst.bitcast(F32)
             nc.scalar.copy(dst_words.rearrange("p (v u) -> p v u", u=2), back.rearrange("p u v -> p v u"))
 
-        z_lo = []
-        for half in range(2):
-            zl = sb.tile([P, 2 * P, 4], BF16, name="z_lo_%d" % half, align_bytes=64)
-            z_lo.append(zl)
-        z_hi = sb.tile([P, TURN, 4], BF16, name="z_hi", align_bytes=64)
+        z_late = []
+        for g, width in ((0, 2 * P), (1, P)):
+            zl = sb.tile([P, 4 * width], BF16, name="z_late_%d" % g, align_bytes=64)
+            z_late.append(zl)
+        z_early = sb.tile([P, 4 * TURN], BF16, name="z_early", align_bytes=64)
 
-        last = {}
+        high = sb.tile([P, 4, V], F32, name="high", align_bytes=64)
+        for b in range(4, 8):
+            term[b, 0] = high[:, b - 4, :]
 
-        def gather_last(d):
-            own = sb.tile([P, 4, V - TURN], F32, name="last_%d" % d, tag=("h_2", "first_0")[d], align_bytes=64)
-            last[d] = own
+        def gather_last():
+            last = sb.tile([P, 4, V - TURN], F32, name="last", tag="first_0", align_bytes=64)
             for t in range(4):
-                looked = h[4 + t][:].indirect(pos[d][:, TURN // 16 : V // 16])
-                nc.vector.tensor_tensor(own[:, t, :], looked, gates[:, d, TURN:V], MULT)
+                looked = h[4 + t][:].indirect(pos[1][:, TURN // 16 : V // 16])
+                nc.vector.tensor_tensor(last[:, t, :], looked, gates[:, 1, TURN:V], MULT)
+            return last
 
         def add_last():
-            z_last = sb.tile([P, V - TURN, 4], BF16, name="z_last", align_bytes=64)
-            dst = z_last[:].rearrange("p (c i) t -> p c t i", i=4)
-            one = last[0][:].rearrange("p t (c i) -> p c t i", i=4)
-            two = last[1][:].rearrange("p t (c i) -> p c t i", i=4)
-            nc.vector.tensor_tensor(dst, one, two, ADD)
-            return z_last
+            dst = z_early[:, 8 * P :].rearrange("p (c i t) -> p c t i", i=4, t=4)
+            lhs = high[:, :, TURN:V].rearrange("p t (c i) -> p c t i", i=4)
+            rhs = last[:].rearrange("p t (c i) -> p c t i", i=4)
+            nc.vector.tensor_tensor(dst, lhs, rhs, ADD)
 
-        zc, zs = [], []
-        for g in range(2):
-            zcg = sb.tile([P, V], U32, name="zc_%d" % g, align_bytes=64)
-            zsg = sb.tile([P, V], U8, name="zs_%d" % g, align_bytes=64)
-            zc.append(zcg)
-            zs.append(zsg)
-
-        def quant_z(g, v0, v1, rounded):
-            nc.vector.quantize_mx(
-                out=zc[g][:, v0:v1].bitcast(FP8X4),
-                scales=zs[g][:, v0:v1],
-                in_=rounded.rearrange("p v t -> p (v t)"),
-            )
+        def quantise(name, rounded, width):
+            codes = sb.tile([P, width], U32, name=name + "_codes", align_bytes=64)
+            scales = sb.tile([P, width], U8, name=name + "_scales", align_bytes=64)
+            nc.vector.quantize_mx(out=codes[:].bitcast(FP8X4), scales=scales[:], in_=rounded)
+            return codes, scales
 
         def layer2(v0, v1, name, passes):
             acc = bank[name][:, 0 : v1 - v0]
-            for g in passes:
+            for i, (g, (codes, scales), c0) in enumerate(passes):
                 nc.tensor.matmul_mx(
                     out=acc,
-                    lhsT=w2c[:, N * g : N * g + N].bitcast(FP8X4),
-                    lhsT_scale=w2s[:, N * g : N * g + N],
-                    rhs=zc[g][:, v0:v1].bitcast(FP8X4),
-                    rhs_scale=zs[g][:, v0:v1],
-                    start=g == passes[0],
-                    stop=g == passes[1],
+                    lhsT=one[0][:, N * g : N * g + N].bitcast(FP8X4),
+                    lhsT_scale=one[1][:, N * g : N * g + N],
+                    rhs=codes[:, c0 : c0 + v1 - v0].bitcast(FP8X4),
+                    rhs_scale=scales[:, c0 : c0 + v1 - v0],
+                    start=i == 0,
+                    stop=i == 1,
                 )
             half = v0 // (2 * P)
             nc.scalar.copy(out_t[half][:, v0 % (2 * P) : v0 % (2 * P) + v1 - v0], acc)
@@ -347,44 +334,43 @@ def tile_picked_sage_none_e_kernel(tc, xT, w1, w2, gate, offs, pos1, pos2, out):
         layer1(6, "AB", "SS")
         layer1(7, "EF", "SS")
         for b in range(4, 8):
-            for d in range(2):
-                new_term(b, d, TURN)
-                gather_gated(b, d, TURN)
+            gather_gated(b, 0, V if b < 7 else TURN)
+            new_term(b, 1, TURN)
+            gather_gated(b, 1, TURN)
+        gather_gated(7, 0, V, TURN)
         new_term(2, 1, V, "w1c_4")
         gather_plain(2, 1)
         fold_lo(0, "G")
-        fold_lo(1, "H")
         rest = sb.tile([P, 2 * P], F32, name="term_rest", tag="w1_lo_0", align_bytes=64)
         gather_plain(3, 0, 2 * P, V)
+        fold_lo(1, "H")
         new_term(3, 1, V, "xc_0")
         gather_plain(3, 1)
-        gather_last(0)
         for d in range(2):
             for b in (2, 3):
                 turn(b, d)
         for vb in range(4):
             weigh_first(vb)
+            if vb == 3:
+                last = gather_last()
             weigh_second(vb)
-        gather_last(1)
         fold_hi(0, "CD")
         fold_hi(1, "GH")
-        w2b = sb.tile([P, 8 * N], BF16, name="w2b", tag="h_3", align_bytes=64)
+        joined = sb.tile([P, 8 * N + 8 * P], BF16, name="joined", tag="h_3", align_bytes=64)
         make_w2()
         words_hi = zt_hi[:].rearrange("p vb u m e -> p (vb u m e)").bitcast(F32)
         words_lo = zt_lo[:].rearrange("p vb u r q -> p (vb u r q)").bitcast(F32)
-        turn_back(words_lo, 0, 2, z_lo[0][:], "A")
-        turn_back(words_hi, 0, 2, z_hi[:, 0 : 2 * P], "C")
-        turn_back(words_lo, 2, 2, z_lo[1][:], "B")
-        turn_back(words_hi, 2, 1, z_hi[:, 2 * P : TURN], "D")
-        quant_w2()
-        z_last = add_last()
-        quant_z(0, 0, 2 * P, z_lo[0][:])
-        quant_z(1, TURN, V, z_last[:])
-        quant_z(1, 0, 2 * P, z_hi[:, 0 : 2 * P])
-        layer2(0, 2 * P, "E", (0, 1))
+        turn_back(words_lo, 0, 2, joined[:, 8 * N :], "A")
+        turn_back(words_hi, 0, 2, z_early[:, 0 : 8 * P], "C")
+        turn_back(words_lo, 2, 2, z_late[0][:], "B")
+        turn_back(words_hi, 2, 1, z_late[1][:], "D")
+        add_last()
+        one = quantise("one", joined[:], 2 * N + 2 * P)
+        two = quantise("two", z_early[:], TURN)
+        layer2(0, 2 * P, "E", ((0, one, 2 * N), (1, two, 0)))
         nc.sync.dma_start(out[:, 0 : 2 * P], out_t[0][:])
-        quant_z(0, 2 * P, V, z_lo[1][:])
-        quant_z(1, 2 * P, TURN, z_hi[:, 2 * P : TURN])
-        layer2(TURN, V, "G", (1, 0))
-        layer2(2 * P, TURN, "F", (0, 1))
+        three = quantise("three", z_late[0][:], 2 * P)
+        four = quantise("four", z_late[1][:], P)
+        layer2(TURN, V, "G", ((1, two, 2 * P), (0, three, P)))
+        layer2(2 * P, TURN, "F", ((0, three, 0), (1, four, 0)))
         nc.sync.dma_start(out[:, 2 * P : V], out_t[1][:])

@@ -48,7 +48,7 @@ def tile_picked_sage_none_e_kernel(tc, xT, w1, w2, gate, offs, pos1, pos2, out):
         x_view = xT.rearrange("(p j) t -> p j t", j=4)
         x_raw = []
         for j in range(4):
-            raw = sb.tile([P, T], F32, name="x_raw_%d" % j)
+            raw = sb.tile([P, T], F32, name="x_raw_%d" % j, align_bytes=256)
             nc.sync.dma_start(raw[:], x_view[:, j, :])
             x_raw.append(raw)
             if j == 0:
@@ -56,20 +56,20 @@ def tile_picked_sage_none_e_kernel(tc, xT, w1, w2, gate, offs, pos1, pos2, out):
         w1_view = w1.rearrange("(p j) i -> p j i", j=4)
         w1_lo = []
         for pair in range(2):
-            raw = sb.tile([P, 4, 2 * P], F32, name="w1_lo_%d" % pair, align_bytes=64)
+            raw = sb.tile([P, 4, 2 * P], F32, name="w1_lo_%d" % pair, align_bytes=256)
             nc.sync.dma_start(raw[:], w1_view[:, :, 2 * P * pair : 2 * P * (pair + 1)])
             w1_lo.append(raw)
-        gates = sb.tile([P, 2, V], F32, name="gates")
+        gates = sb.tile([P, 2, V], F32, name="gates", align_bytes=256)
         w1_hi = []
         for piece in range(2):
-            raw = sb.tile([P, 4, 2 * P], F32, name="w1_hi_%d" % piece, align_bytes=64)
+            raw = sb.tile([P, 4, 2 * P], F32, name="w1_hi_%d" % piece, align_bytes=256)
             nc.sync.dma_start(raw[:], w1_view[:, :, 2 * P * (2 + piece) : 2 * P * (3 + piece)])
             w1_hi.append(raw)
             if piece == 0:
                 nc.sync.dma_start(pos1_t[:], pos1)
                 nc.sync.dma_start(gates[:], gate.rearrange("d p v -> p d v"))
         nc.sync.dma_start(pos2_t[:], pos2)
-        w2_raw = sb.tile([P, 2, 4, N], F32, name="w2_raw")
+        w2_raw = sb.tile([P, 2, 4, N], F32, name="w2_raw", align_bytes=256)
         nc.sync.dma_start(w2_raw[:], w2.rearrange("(g p t) n -> p g t n", g=2, t=4))
         gate_col = sb.tile([P, 2, 4], F32, name="gate_col")
         with nc.allow_non_contiguous_dma("one gate a partition"):
@@ -103,7 +103,7 @@ def tile_picked_sage_none_e_kernel(tc, xT, w1, w2, gate, offs, pos1, pos2, out):
 
         xc, xs = [], []
         for half in range(2):
-            codes = sb.tile([P, BANK], U32, name="xc_%d" % half, tag="w1_lo_0" if half else "xc_0", align_bytes=64)
+            codes = sb.tile([P, BANK], U32, name="xc_%d" % half, tag="w1_lo_0" if half else "xc_0", align_bytes=256)
             scales = sb.tile([P, BANK], U8, name="xs_%d" % half, align_bytes=64)
             xc.append(codes)
             xs.append(scales)
@@ -178,7 +178,7 @@ def tile_picked_sage_none_e_kernel(tc, xT, w1, w2, gate, offs, pos1, pos2, out):
 
         def new_term(b, d, width, tag=None):
             name = "term_%d_%d" % (b, d)
-            own = sb.tile([P, width], F32, name=name, tag=tag or name, align_bytes=64)
+            own = sb.tile([P, width], F32, name=name, tag=tag or name, align_bytes=256 if tag == "xc_0" else 64)
             term[b, d] = own
 
         def gather_gated(b, d, v1, v0=0):
@@ -293,7 +293,7 @@ def tile_picked_sage_none_e_kernel(tc, xT, w1, w2, gate, offs, pos1, pos2, out):
 
         out_t = []
         for half in range(2):
-            ot = sb.tile([P, 2 * P], F32, name="out_%d" % half)
+            ot = sb.tile([P, 2 * P], F32, name="out_%d" % half, align_bytes=256)
             out_t.append(ot)
 
         for j in range(4):
@@ -316,7 +316,7 @@ def tile_picked_sage_none_e_kernel(tc, xT, w1, w2, gate, offs, pos1, pos2, out):
         new_term(0, 0, V)
         gather_gated(0, 0, V)
         round_w1_hi(1)
-        early = sb.tile([P, 2, V], F32, name="term_1", tag="w1_hi_1", align_bytes=64)
+        early = sb.tile([P, 2, V], F32, name="term_1", tag="w1_hi_1", align_bytes=256)
         term[1, 0], term[1, 1] = early[:, 0, :], early[:, 1, :]
         new_term(0, 1, V)
         gather_gated(0, 1, V)
@@ -341,7 +341,7 @@ def tile_picked_sage_none_e_kernel(tc, xT, w1, w2, gate, offs, pos1, pos2, out):
         new_term(2, 1, V, "w1c_4")
         gather_plain(2, 1)
         fold_lo(0, "G")
-        rest = sb.tile([P, 2 * P], F32, name="term_rest", tag="w1_lo_0", align_bytes=64)
+        rest = sb.tile([P, 2 * P], F32, name="term_rest", tag="w1_lo_0", align_bytes=256)
         gather_plain(3, 0, 2 * P, V)
         fold_lo(1, "H")
         new_term(3, 1, V, "xc_0")

@@ -26,6 +26,7 @@ def tile_picked_sage_none_e_kernel(tc, xT, w1, w2, gate, offs, pos1, pos2, out):
     with ExitStack() as ctx:
         lists = ctx.enter_context(tc.tile_pool(name="lists", bufs=1))
         sb = ctx.enter_context(tc.tile_pool(name="sb", bufs=1))
+        shared = ctx.enter_context(tc.tile_pool(name="shared", bufs=1))
         ps = ctx.enter_context(tc.psum_pool(name="ps", bufs=1))
 
         offs_t = lists.tile([P, S // 16], U16, name="offs_t")
@@ -56,7 +57,7 @@ def tile_picked_sage_none_e_kernel(tc, xT, w1, w2, gate, offs, pos1, pos2, out):
         w1_view = w1.rearrange("(p j) i -> p j i", j=4)
         w1_lo = []
         for pair in range(2):
-            raw = sb.tile([P, 4, 2 * P], F32, name="w1_lo_%d" % pair, align_bytes=256)
+            raw = shared.tile([P, 4, 2 * P], F32, name="w1_lo_%d" % pair, align_bytes=256, offset=4096 * pair)
             nc.sync.dma_start(raw[:], w1_view[:, :, 2 * P * pair : 2 * P * (pair + 1)])
             w1_lo.append(raw)
         gates = sb.tile([P, 2, V], F32, name="gates", align_bytes=256)
@@ -76,13 +77,17 @@ def tile_picked_sage_none_e_kernel(tc, xT, w1, w2, gate, offs, pos1, pos2, out):
             runs = gate.rearrange("d r (vb p) -> p (d r vb)", p=P)
             nc.sync.dma_start(gate_col[:].rearrange("p d vb -> p (d vb)"), runs[:, 0 : 8 * P : P + 1])
 
-        picked = []
-        for half in range(2):
-            pk = sb.tile([P, 4 * BANK], BF16, name="picked_%d" % half, align_bytes=64)
-            picked.append(pk)
+        picked = {}
+        picked[0] = sb.tile([P, 4 * BANK], BF16, name="picked_0", align_bytes=64)
+        picked[2 * QUARTER] = sb.tile([P, 4 * QUARTER], BF16, name="picked_2", align_bytes=64)
+        picked[3 * QUARTER] = shared.tile([P, 4 * QUARTER], BF16, name="picked_3", align_bytes=256, offset=0)
+
+        def rows(n0, n1):
+            base = max(start for start in picked if start <= n0)
+            return picked[base][:, 4 * (n0 - base) : 4 * (n1 - base)]
 
         def slots(n0, n1):
-            return picked[n0 // BANK][:].rearrange("p (n t) -> p n t", t=4)[:, n0 % BANK : n0 % BANK + n1 - n0]
+            return rows(n0, n1).rearrange("p (n t) -> p n t", t=4)
 
         def looked_up(j, q0, q1):
             return x_raw[j][:].indirect(offs_t[:, QUARTER * q0 // 16 : QUARTER * q1 // 16])
@@ -103,7 +108,10 @@ def tile_picked_sage_none_e_kernel(tc, xT, w1, w2, gate, offs, pos1, pos2, out):
 
         xc, xs = [], []
         for half in range(2):
-            codes = sb.tile([P, BANK], U32, name="xc_%d" % half, tag="w1_lo_0" if half else "xc_0", align_bytes=256)
+            if half:
+                codes = shared.tile([P, BANK], U32, name="xc_1", align_bytes=256, offset=2048)
+            else:
+                codes = sb.tile([P, BANK], U32, name="xc_0", align_bytes=256)
             scales = sb.tile([P, BANK], U8, name="xs_%d" % half, align_bytes=64)
             xc.append(codes)
             xs.append(scales)
@@ -113,7 +121,7 @@ def tile_picked_sage_none_e_kernel(tc, xT, w1, w2, gate, offs, pos1, pos2, out):
             nc.vector.quantize_mx(
                 out=xc[n0 // BANK][:, cols].bitcast(FP8X4),
                 scales=xs[n0 // BANK][:, cols],
-                in_=picked[n0 // BANK][:, 4 * cols.start : 4 * cols.stop],
+                in_=rows(n0, n1),
             )
 
         w1b, w1c, w1s = {}, {}, {}
@@ -145,13 +153,16 @@ def tile_picked_sage_none_e_kernel(tc, xT, w1, w2, gate, offs, pos1, pos2, out):
 
         def make_w2():
             dst = joined[:, 0 : 8 * N].rearrange("p (g c i t) -> p g c t i", g=2, i=4, t=4)
-            nc.scalar.copy(dst, w2_raw[:].rearrange("p g t (c i) -> p g c t i", i=4))
+            src = w2_raw[:].rearrange("p g t (c i) -> p g c t i", i=4)
+            nc.scalar.copy(dst[:, 0], src[:, 0])
+            nc.vector.tensor_copy(dst[:, 1], src[:, 1])
 
         h = {}
 
         def layer1(b, banks, engines, cuts=(0, BANK, S)):
             ht = sb.tile([P, S], F32, name="h_%d" % b, align_bytes=64)
             h[b] = ht
+            pieces = []
             for name, engine, n0, n1 in zip(banks, engines, cuts, cuts[1:]):
                 acc = bank[name][:, 0 : n1 - n0]
                 cols = slice(n0 % BANK, n0 % BANK + n1 - n0)
@@ -164,16 +175,13 @@ def tile_picked_sage_none_e_kernel(tc, xT, w1, w2, gate, offs, pos1, pos2, out):
                     start=True,
                     stop=True,
                 )
-                if engine == "V":
-                    nc.vector.tensor_copy(ht[:, n0:n1], acc)
-                else:
-                    nc.scalar.copy(ht[:, n0:n1], acc)
+                pieces.append((ht[:, n0:n1], acc))
+            for dst, acc in reversed(pieces) if b in (3, 5, 6, 7) else pieces:
+                nc.scalar.copy(dst, acc)
 
         term = {}
 
         def piece(b, d, v0, v1):
-            if (b, d) == (3, 0) and v0 >= 2 * P:
-                return rest[:, v0 - 2 * P : v1 - 2 * P]
             return term[b, d][:, v0:v1]
 
         def new_term(b, d, width, tag=None):
@@ -194,8 +202,12 @@ def tile_picked_sage_none_e_kernel(tc, xT, w1, w2, gate, offs, pos1, pos2, out):
                     out=dst, lhsT=term[b, d][:, v : v + P], rhs=ident[:], start=d == 0, stop=d == 1, is_transpose=True
                 )
 
-        zt_lo = sb.tile([P, 4, 2, 2, P], BF16, name="zt_lo", align_bytes=64)
-        zt_hi = sb.tile([P, 3, 2, P, 2], BF16, name="zt_hi", align_bytes=64)
+        zt_lo, zt_hi = [], []
+        for half in range(2):
+            lo = sb.tile([P, 2, 2, 2, P], BF16, name="zt_lo_%d" % half, align_bytes=64)
+            hi = sb.tile([P, 2 - half, 2, P, 2], BF16, name="zt_hi_%d" % half, align_bytes=64)
+            zt_lo.append(lo)
+            zt_hi.append(hi)
         first = []
         for vb in range(4):
             ft = sb.tile([P, 2 * P], F32, name="first_%d" % vb, align_bytes=64)
@@ -205,13 +217,14 @@ def tile_picked_sage_none_e_kernel(tc, xT, w1, w2, gate, offs, pos1, pos2, out):
             sums = bank[name][:].rearrange("p (vb q) -> p vb q", vb=4)
             for vb in range(4):
                 add_turned(sums[:, vb], b, P * vb)
-            nc.scalar.copy(zt_lo[:, :, b, 0, :], sums)
+            for half in (1, 0):
+                nc.scalar.copy(zt_lo[half][:, :, b, 0, :], sums[:, 2 * half : 2 * half + 2])
 
         def turned(d, vb):
             return bank["ABEF"[2 * d + vb // 2]][:, 2 * P * (vb % 2) : 2 * P * (vb % 2 + 1)]
 
         def turn(b, d):
-            for vb in range(4):
+            for vb in range(4) if d else reversed(range(4)):
                 dst = turned(d, vb)[:, P * (b % 2) : P * (b % 2 + 1)]
                 nc.tensor.transpose(dst, piece(b, d, P * vb, P * vb + P), ident[:])
 
@@ -220,7 +233,7 @@ def tile_picked_sage_none_e_kernel(tc, xT, w1, w2, gate, offs, pos1, pos2, out):
 
         def weigh_second(vb):
             nc.vector.scalar_tensor_tensor(
-                out=zt_lo[:, vb, :, 1, :],
+                out=zt_lo[vb // 2][:, vb % 2, :, 1, :],
                 in0=turned(1, vb).rearrange("p (u q) -> p u q", u=2),
                 scalar=gate_col[:, 1, vb : vb + 1],
                 in1=first[vb][:].rearrange("p (u q) -> p u q", u=2),
@@ -234,15 +247,16 @@ def tile_picked_sage_none_e_kernel(tc, xT, w1, w2, gate, offs, pos1, pos2, out):
                 for e in range(2):
                     for q in range(count):
                         add_turned(sums[:, q, e], 4 + 2 * u + e, P * (vb0 + q))
-            for name, vb0, count in zip(names, (0, 2), (2, 1)):
+            stretches = list(zip(names, (0, 2), (2, 1)))
+            for name, vb0, count in stretches if u else reversed(stretches):
                 sums = bank[name][:].rearrange("p (q e m) -> p q m e", q=2, e=2)
-                nc.scalar.copy(zt_hi[:, vb0 : vb0 + count, u], sums[:, 0:count])
+                nc.scalar.copy(zt_hi[vb0 // 2][:, :, u], sums[:, 0:count])
 
-        def turn_back(words, vb0, count, dst, name):
+        def turn_back(words, count, dst, name):
             back = bank[name][:, 0 : 2 * P * count].rearrange("p (u v) -> p u v", u=2)
             for vb in range(count):
                 for u in range(2):
-                    w0 = P * (2 * (vb0 + vb) + u)
+                    w0 = P * (2 * vb + u)
                     nc.tensor.transpose(back[:, u, P * vb : P * vb + P], words[:, w0 : w0 + P], ident[:])
             dst_words = dst.bitcast(F32)
             nc.scalar.copy(dst_words.rearrange("p (v u) -> p v u", u=2), back.rearrange("p u v -> p v u"))
@@ -298,14 +312,15 @@ def tile_picked_sage_none_e_kernel(tc, xT, w1, w2, gate, offs, pos1, pos2, out):
 
         for j in range(4):
             gather_plane(j, 2 if j == 3 else 1)
-            for q in range(1, (4, 4, 2, 1)[j]):
+            for q in range(1, (3, 3, 2, 1)[j]):
                 place(j, j + 1, q)
         for pair in range(2):
             round_w1_lo(pair)
         place(2, 4, 2)
         quant_x(0, BANK)
         quant_w1(0)
-        place(2, 4, 3)
+        weave = slots(3 * QUARTER, S).rearrange("p (c i) t -> p c t i", i=4)
+        nc.vector.tensor_copy(weave, fetched[3][:].rearrange("p t (c i) -> p c t i", i=4))
         quant_x(BANK, 3 * QUARTER)
         quant_x(3 * QUARTER, S)
         quant_w1(1)
@@ -319,16 +334,15 @@ def tile_picked_sage_none_e_kernel(tc, xT, w1, w2, gate, offs, pos1, pos2, out):
         early = sb.tile([P, 2, V], F32, name="term_1", tag="w1_hi_1", align_bytes=256)
         term[1, 0], term[1, 1] = early[:, 0, :], early[:, 1, :]
         new_term(0, 1, V)
-        gather_gated(0, 1, V)
+        gather_gated(0, 1, 2 * P)
         quant_w1(4)
+        gather_gated(0, 1, V, 2 * P)
         for d in range(2):
             gather_gated(1, d, V)
         layer1(2, "AB", "SS")
         layer1(3, "EF", "SS")
         new_term(2, 0, V)
         gather_plain(2, 0)
-        new_term(3, 0, 2 * P)
-        gather_plain(3, 0, 0, 2 * P)
         layer1(4, "GH", "SS")
         layer1(5, "CD", "SS")
         layer1(6, "AB", "SS")
@@ -341,8 +355,8 @@ def tile_picked_sage_none_e_kernel(tc, xT, w1, w2, gate, offs, pos1, pos2, out):
         new_term(2, 1, V, "w1c_4")
         gather_plain(2, 1)
         fold_lo(0, "G")
-        rest = sb.tile([P, 2 * P], F32, name="term_rest", tag="w1_lo_0", align_bytes=256)
-        gather_plain(3, 0, 2 * P, V)
+        term[3, 0] = shared.tile([P, V], F32, name="term_3_0", align_bytes=256, offset=2048)
+        gather_plain(3, 0)
         fold_lo(1, "H")
         new_term(3, 1, V, "xc_0")
         gather_plain(3, 1)
@@ -358,19 +372,19 @@ def tile_picked_sage_none_e_kernel(tc, xT, w1, w2, gate, offs, pos1, pos2, out):
         fold_hi(1, "GH")
         joined = sb.tile([P, 8 * N + 8 * P], BF16, name="joined", tag="h_3", align_bytes=64)
         make_w2()
-        words_hi = zt_hi[:].rearrange("p vb u m e -> p (vb u m e)").bitcast(F32)
-        words_lo = zt_lo[:].rearrange("p vb u r q -> p (vb u r q)").bitcast(F32)
-        turn_back(words_lo, 0, 2, joined[:, 8 * N :], "A")
-        turn_back(words_hi, 0, 2, z_early[:, 0 : 8 * P], "C")
-        turn_back(words_lo, 2, 2, z_late[0][:], "B")
-        turn_back(words_hi, 2, 1, z_late[1][:], "D")
+        words_hi = [zt[:].rearrange("p vb u m e -> p (vb u m e)").bitcast(F32) for zt in zt_hi]
+        words_lo = [zt[:].rearrange("p vb u r q -> p (vb u r q)").bitcast(F32) for zt in zt_lo]
+        turn_back(words_lo[0], 2, joined[:, 8 * N :], "A")
+        turn_back(words_hi[0], 2, z_early[:, 0 : 8 * P], "C")
+        turn_back(words_hi[1], 1, z_late[1][:], "D")
+        turn_back(words_lo[1], 2, z_late[0][:], "B")
         add_last()
         one = quantise("one", joined[:], 2 * N + 2 * P)
         two = quantise("two", z_early[:], TURN)
         layer2(0, 2 * P, "E", ((0, one, 2 * N), (1, two, 0)))
         nc.sync.dma_start(out[:, 0 : 2 * P], out_t[0][:])
-        three = quantise("three", z_late[0][:], 2 * P)
         four = quantise("four", z_late[1][:], P)
+        three = quantise("three", z_late[0][:], 2 * P)
+        layer2(2 * P, TURN, "F", ((1, four, 0), (0, three, 0)))
         layer2(TURN, V, "G", ((1, two, 2 * P), (0, three, P)))
-        layer2(2 * P, TURN, "F", ((0, three, 0), (1, four, 0)))
         nc.sync.dma_start(out[:, 2 * P : V], out_t[1][:])

from contextlib import ExitStack

import concourse.mybir as mybir
from concourse.masks import make_identity

K, T, S, V, H, N = 512, 2048, 1024, 512, 1024, 128
P = 128
BANK = 512
QUARTER = S // 4
TURN = 384
FLOPS = 2 * K * H * S + 2 * H * N * V

F32 = mybir.dt.float32
BF16 = mybir.dt.bfloat16
U32 = mybir.dt.uint32
U16 = mybir.dt.uint16
U8 = mybir.dt.uint8
FP8X4 = mybir.dt.float8_e4m3fn_x4
MULT = mybir.AluOpType.mult
ADD = mybir.AluOpType.add
COPY = mybir.ActivationFunctionType.Copy


def tile_picked_sage_none_e_kernel(tc, xT, w1, w2, gate, offs, pos1, pos2, out):
    nc = tc.nc
    with ExitStack() as ctx:
        lists = ctx.enter_context(tc.tile_pool(name="lists", bufs=1))
        sb = ctx.enter_context(tc.tile_pool(name="sb", bufs=1))
        shared = ctx.enter_context(tc.tile_pool(name="shared", bufs=1))
        ps = ctx.enter_context(tc.psum_pool(name="ps", bufs=1))

        offs_t = lists.tile([P, S // 16], U16, name="offs_t")
        pos1_t = lists.tile([P, V // 16], U16, name="pos1_t")
        pos2_t = lists.tile([P, V // 16], U16, name="pos2_t")
        pos = (pos1_t, pos2_t)

        ident = sb.tile([P, P], F32, name="ident")
        make_identity(nc, ident[:])

        warm = sb.tile([P, 2], F32, name="warm")
        nc.vector.memset(warm[:, 0:1], 0.0)
        nc.scalar.activation(warm[:, 1:2], warm[:, 0:1], COPY)

        bank = {}
        for name in "ABCDEFGH":
            whole = ps.tile([P, BANK], F32, name="bank_" + name)
            bank[name] = whole

        x_view = xT.rearrange("(p j) t -> p j t", j=4)
        x_raw = []
        for j in range(4):
            raw = sb.tile([P, T], F32, name="x_raw_%d" % j, align_bytes=256)
            nc.sync.dma_start(raw[:], x_view[:, j, :])
            x_raw.append(raw)
            if j == 0:
                nc.sync.dma_start(offs_t[:], offs)
        w1_view = w1.rearrange("(p j) i -> p j i", j=4)
        w1_lo = []
        for pair in range(2):
            raw = shared.tile([P, 4, 2 * P], F32, name="w1_lo_%d" % pair, align_bytes=256, offset=4096 * pair)
            nc.sync.dma_start(raw[:], w1_view[:, :, 2 * P * pair : 2 * P * (pair + 1)])
            w1_lo.append(raw)
        gates = sb.tile([P, 2, V], F32, name="gates", align_bytes=256)
        w1_hi = []
        for piece in range(2):
            raw = sb.tile([P, 4, 2 * P], F32, name="w1_hi_%d" % piece, align_bytes=256)
            nc.sync.dma_start(raw[:], w1_view[:, :, 2 * P * (2 + piece) : 2 * P * (3 + piece)])
            w1_hi.append(raw)
            if piece == 0:
                nc.sync.dma_start(pos1_t[:], pos1)
                nc.sync.dma_start(gates[:], gate.rearrange("d p v -> p d v"))
        nc.sync.dma_start(pos2_t[:], pos2)
        w2_raw = sb.tile([P, 2, 4, N], F32, name="w2_raw", align_bytes=256)
        nc.sync.dma_start(w2_raw[:], w2.rearrange("(g p t) n -> p g t n", g=2, t=4))
        gate_col = sb.tile([P, 2, 4], F32, name="gate_col")
        with nc.allow_non_contiguous_dma("one gate a partition"):
            runs = gate.rearrange("d r (vb p) -> p (d r vb)", p=P)
            nc.sync.dma_start(gate_col[:].rearrange("p d vb -> p (d vb)"), runs[:, 0 : 8 * P : P + 1])

        picked = {}
        picked[0] = sb.tile([P, 4 * BANK], BF16, name="picked_0", align_bytes=64)
        picked[2 * QUARTER] = sb.tile([P, 4 * QUARTER], BF16, name="picked_2", align_bytes=64)
        picked[3 * QUARTER] = shared.tile([P, 4 * QUARTER], BF16, name="picked_3", align_bytes=256, offset=0)

        def rows(n0, n1):
            base = max(start for start in picked if start <= n0)
            return picked[base][:, 4 * (n0 - base) : 4 * (n1 - base)]

        def slots(n0, n1):
            return rows(n0, n1).rearrange("p (n t) -> p n t", t=4)

        def looked_up(j, q0, q1):
            return x_raw[j][:].indirect(offs_t[:, QUARTER * q0 // 16 : QUARTER * q1 // 16])

        fetched = {}
        for q in range(1, 4):
            ft = sb.tile([P, 4, QUARTER], BF16, name="fetched_%d" % (QUARTER * q), align_bytes=64)
            fetched[q] = ft

        def gather_plane(j, own):
            nc.vector.tensor_copy(slots(0, QUARTER * own)[:, :, j], looked_up(j, 0, own))
            for q in range(own, 4):
                nc.scalar.activation(fetched[q][:, j, :], looked_up(j, q, q + 1), COPY)

        def place(j0, j1, q):
            dst = slots(QUARTER * q, QUARTER * (q + 1))[:, :, j0:j1]
            nc.vector.tensor_copy(dst, fetched[q][:, j0:j1, :].rearrange("p e n -> p n e"))

        xc, xs = [], []
        for half in range(2):
            if half:
                codes = shared.tile([P, BANK], U32, name="xc_1", align_bytes=256, offset=2048)
            else:
                codes = sb.tile([P, BANK], U32, name="xc_0", align_bytes=256)
            scales = sb.tile([P, BANK], U8, name="xs_%d" % half, align_bytes=64)
            xc.append(codes)
            xs.append(scales)

        def quant_x(n0, n1):
            cols = slice(n0 % BANK, n0 % BANK + n1 - n0)
            nc.vector.quantize_mx(
                out=xc[n0 // BANK][:, cols].bitcast(FP8X4),
                scales=xs[n0 // BANK][:, cols],
                in_=rows(n0, n1),
            )

        w1b, w1c, w1s = {}, {}, {}

        def round_w1_lo(pair):
            own = sb.tile([P, 2, 4 * P], BF16, name="w1b_lo_%d" % pair, align_bytes=64)
            dst = own[:].rearrange("p u (c e j) -> p c j u e", e=2, j=4)
            nc.scalar.copy(dst, w1_lo[pair][:].rearrange("p j (c u e) -> p c j u e", u=2, e=2))
            if pair:
                w1b[2] = (own[:].rearrange("p u c -> p (u c)"), 2)
            else:
                w1b[0], w1b[1] = (own[:, 0, :], 1), (own[:, 1, :], 1)

        w1b_hi = sb.tile([P, 16 * P], BF16, name="w1b_4", align_bytes=64)
        w1b[4] = (w1b_hi[:], 4)

        def round_w1_hi(piece):
            dst = w1b_hi[:].rearrange("p (t m j) -> p m j t", t=4, j=4)[:, 64 * piece : 64 * piece + 64]
            nc.vector.tensor_copy(dst, w1_hi[piece][:].rearrange("p j (m t) -> p m j t", t=4))

        def quant_w1(b0):
            wide, parts = w1b[b0]
            codes = sb.tile([P, P * parts], U32, name="w1c_%d" % b0, align_bytes=64)
            scales = sb.tile([P, P * parts], U8, name="w1s_%d" % b0, align_bytes=64)
            nc.vector.quantize_mx(out=codes[:].bitcast(FP8X4), scales=scales[:], in_=wide)
            for i in range(parts):
                w1c[b0 + i] = codes[:, P * i : P * i + P]
                w1s[b0 + i] = scales[:, P * i : P * i + P]

        def make_w2():
            dst = joined[:, 0 : 8 * N].rearrange("p (g c i t) -> p g c t i", g=2, i=4, t=4)
            src = w2_raw[:].rearrange("p g t (c i) -> p g c t i", i=4)
            nc.scalar.copy(dst[:, 0], src[:, 0])
            nc.vector.tensor_copy(dst[:, 1], src[:, 1])

        h = {}

        def layer1(b, banks, engines, cuts=(0, BANK, S)):
            ht = sb.tile([P, S], F32, name="h_%d" % b, align_bytes=64)
            h[b] = ht
            pieces = []
            for name, engine, n0, n1 in zip(banks, engines, cuts, cuts[1:]):
                acc = bank[name][:, 0 : n1 - n0]
                cols = slice(n0 % BANK, n0 % BANK + n1 - n0)
                nc.tensor.matmul_mx(
                    out=acc,
                    lhsT=w1c[b].bitcast(FP8X4),
                    lhsT_scale=w1s[b],
                    rhs=xc[n0 // BANK][:, cols].bitcast(FP8X4),
                    rhs_scale=xs[n0 // BANK][:, cols],
                    start=True,
                    stop=True,
                )
                pieces.append((ht[:, n0:n1], acc))
            for dst, acc in reversed(pieces) if b in (3, 5, 6, 7) else pieces:
                nc.scalar.copy(dst, acc)

        term = {}

        def piece(b, d, v0, v1):
            return term[b, d][:, v0:v1]

        def new_term(b, d, width, tag=None):
            name = "term_%d_%d" % (b, d)
            own = sb.tile([P, width], F32, name=name, tag=tag or name, align_bytes=256 if tag == "xc_0" else 64)
            term[b, d] = own

        def gather_gated(b, d, v1, v0=0):
            looked = h[b][:].indirect(pos[d][:, v0 // 16 : v1 // 16])
            nc.vector.tensor_tensor(term[b, d][:, v0:v1], looked, gates[:, d, v0:v1], MULT)

        def gather_plain(b, d, v0=0, v1=V):
            nc.scalar.activation(piece(b, d, v0, v1), h[b][:].indirect(pos[d][:, v0 // 16 : v1 // 16]), COPY)

        def add_turned(dst, b, v):
            for d in range(2):
                nc.tensor.matmul(
                    out=dst, lhsT=term[b, d][:, v : v + P], rhs=ident[:], start=d == 0, stop=d == 1, is_transpose=True
                )

        zt_lo, zt_hi = [], []
        for half in range(2):
            lo = sb.tile([P, 2, 2, 2, P], BF16, name="zt_lo_%d" % half, align_bytes=64)
            hi = sb.tile([P, 2 - half, 2, P, 2], BF16, name="zt_hi_%d" % half, align_bytes=64)
            zt_lo.append(lo)
            zt_hi.append(hi)
        first = []
        for vb in range(4):
            ft = sb.tile([P, 2 * P], F32, name="first_%d" % vb, align_bytes=64)
            first.append(ft)

        def fold_lo(b, name):
            sums = bank[name][:].rearrange("p (vb q) -> p vb q", vb=4)
            for vb in range(4):
                add_turned(sums[:, vb], b, P * vb)
            for half in (1, 0):
                nc.scalar.copy(zt_lo[half][:, :, b, 0, :], sums[:, 2 * half : 2 * half + 2])

        def turned(d, vb):
            return bank["ABEF"[2 * d + vb // 2]][:, 2 * P * (vb % 2) : 2 * P * (vb % 2 + 1)]

        def turn(b, d):
            for vb in range(4) if d else reversed(range(4)):
                dst = turned(d, vb)[:, P * (b % 2) : P * (b % 2 + 1)]
                nc.tensor.transpose(dst, piece(b, d, P * vb, P * vb + P), ident[:])

        def weigh_first(vb):
            nc.scalar.activation(first[vb][:], turned(0, vb), COPY, scale=gate_col[:, 0, vb : vb + 1])

        def weigh_second(vb):
            nc.vector.scalar_tensor_tensor(
                out=zt_lo[vb // 2][:, vb % 2, :, 1, :],
                in0=turned(1, vb).rearrange("p (u q) -> p u q", u=2),
                scalar=gate_col[:, 1, vb : vb + 1],
                in1=first[vb][:].rearrange("p (u q) -> p u q", u=2),
                op0=MULT,
                op1=ADD,
            )

        def fold_hi(u, names):
            for name, vb0, count in zip(names, (0, 2), (2, 1)):
                sums = bank[name][:].rearrange("p (q e m) -> p q e m", q=2, e=2)
                for e in range(2):
                    for q in range(count):
                        add_turned(sums[:, q, e], 4 + 2 * u + e, P * (vb0 + q))
            stretches = list(zip(names, (0, 2), (2, 1)))
            for name, vb0, count in stretches if u else reversed(stretches):
                sums = bank[name][:].rearrange("p (q e m) -> p q m e", q=2, e=2)
                nc.scalar.copy(zt_hi[vb0 // 2][:, :, u], sums[:, 0:count])

        def turn_back(words, count, dst, name):
            back = bank[name][:, 0 : 2 * P * count].rearrange("p (u v) -> p u v", u=2)
            for vb in range(count):
                for u in range(2):
                    w0 = P * (2 * vb + u)
                    nc.tensor.transpose(back[:, u, P * vb : P * vb + P], words[:, w0 : w0 + P], ident[:])
            dst_words = dst.bitcast(F32)
            nc.scalar.copy(dst_words.rearrange("p (v u) -> p v u", u=2), back.rearrange("p u v -> p v u"))

        z_late = []
        for g, width in ((0, 2 * P), (1, P)):
            zl = sb.tile([P, 4 * width], BF16, name="z_late_%d" % g, align_bytes=64)
            z_late.append(zl)
        z_early = sb.tile([P, 4 * TURN], BF16, name="z_early", align_bytes=64)

        high = sb.tile([P, 4, V], F32, name="high", align_bytes=64)
        for b in range(4, 8):
            term[b, 0] = high[:, b - 4, :]

        def gather_last():
            last = sb.tile([P, 4, V - TURN], F32, name="last", tag="first_0", align_bytes=64)
            for t in range(4):
                looked = h[4 + t][:].indirect(pos[1][:, TURN // 16 : V // 16])
                nc.vector.tensor_tensor(last[:, t, :], looked, gates[:, 1, TURN:V], MULT)
            return last

        def add_last():
            dst = z_early[:, 8 * P :].rearrange("p (c i t) -> p c t i", i=4, t=4)
            lhs = high[:, :, TURN:V].rearrange("p t (c i) -> p c t i", i=4)
            rhs = last[:].rearrange("p t (c i) -> p c t i", i=4)
            nc.vector.tensor_tensor(dst, lhs, rhs, ADD)

        def quantise(name, rounded, width):
            codes = sb.tile([P, width], U32, name=name + "_codes", align_bytes=64)
            scales = sb.tile([P, width], U8, name=name + "_scales", align_bytes=64)
            nc.vector.quantize_mx(out=codes[:].bitcast(FP8X4), scales=scales[:], in_=rounded)
            return codes, scales

        def layer2(v0, v1, name, passes):
            acc = bank[name][:, 0 : v1 - v0]
            for i, (g, (codes, scales), c0) in enumerate(passes):
                nc.tensor.matmul_mx(
                    out=acc,
                    lhsT=one[0][:, N * g : N * g + N].bitcast(FP8X4),
                    lhsT_scale=one[1][:, N * g : N * g + N],
                    rhs=codes[:, c0 : c0 + v1 - v0].bitcast(FP8X4),
                    rhs_scale=scales[:, c0 : c0 + v1 - v0],
                    start=i == 0,
                    stop=i == 1,
                )
            half = v0 // (2 * P)
            nc.scalar.copy(out_t[half][:, v0 % (2 * P) : v0 % (2 * P) + v1 - v0], acc)

        out_t = []
        for half in range(2):
            ot = sb.tile([P, 2 * P], F32, name="out_%d" % half, align_bytes=256)
            out_t.append(ot)

        for j in range(4):
            gather_plane(j, 2 if j == 3 else 1)
            for q in range(1, (3, 3, 2, 1)[j]):
                place(j, j + 1, q)
        for pair in range(2):
            round_w1_lo(pair)
        place(2, 4, 2)
        quant_x(0, BANK)
        quant_w1(0)
        weave = slots(3 * QUARTER, S).rearrange("p (c i) t -> p c t i", i=4)
        nc.vector.tensor_copy(weave, fetched[3][:].rearrange("p t (c i) -> p c t i", i=4))
        quant_x(BANK, 3 * QUARTER)
        quant_x(3 * QUARTER, S)
        quant_w1(1)
        layer1(0, "ABG", "SSS", (0, BANK, 3 * QUARTER, S))
        round_w1_hi(0)
        quant_w1(2)
        layer1(1, "CD", "SS")
        new_term(0, 0, V)
        gather_gated(0, 0, V)
        round_w1_hi(1)
        early = sb.tile([P, 2, V], F32, name="term_1", tag="w1_hi_1", align_bytes=256)
        term[1, 0], term[1, 1] = early[:, 0, :], early[:, 1, :]
        new_term(0, 1, V)
        gather_gated(0, 1, 2 * P)
        quant_w1(4)
        gather_gated(0, 1, V, 2 * P)
        for d in range(2):
            gather_gated(1, d, V)
        layer1(2, "AB", "SS")
        layer1(3, "EF", "SS")
        new_term(2, 0, V)
        gather_plain(2, 0)
        layer1(4, "GH", "SS")
        layer1(5, "CD", "SS")
        layer1(6, "AB", "SS")
        layer1(7, "EF", "SS")
        for b in range(4, 8):
            gather_gated(b, 0, V if b < 7 else TURN)
            new_term(b, 1, TURN)
            gather_gated(b, 1, TURN)
        gather_gated(7, 0, V, TURN)
        new_term(2, 1, V, "w1c_4")
        gather_plain(2, 1)
        fold_lo(0, "G")
        term[3, 0] = shared.tile([P, V], F32, name="term_3_0", align_bytes=256, offset=2048)
        gather_plain(3, 0)
        fold_lo(1, "H")
        new_term(3, 1, V, "xc_0")
        gather_plain(3, 1)
        for d in range(2):
            for b in (2, 3):
                turn(b, d)
        for vb in range(4):
            weigh_first(vb)
            if vb == 3:
                last = gather_last()
            weigh_second(vb)
        fold_hi(0, "CD")
        fold_hi(1, "GH")
        joined = sb.tile([P, 8 * N + 8 * P], BF16, name="joined", tag="h_3", align_bytes=64)
        make_w2()
        words_hi = [zt[:].rearrange("p vb u m e -> p (vb u m e)").bitcast(F32) for zt in zt_hi]
        words_lo = [zt[:].rearrange("p vb u r q -> p (vb u r q)").bitcast(F32) for zt in zt_lo]
        turn_back(words_lo[0], 2, joined[:, 8 * N :], "A")
        turn_back(words_hi[0], 2, z_early[:, 0 : 8 * P], "C")
        turn_back(words_hi[1], 1, z_late[1][:], "D")
        turn_back(words_lo[1], 2, z_late[0][:], "B")
        add_last()
        one = quantise("one", joined[:], 2 * N + 2 * P)
        two = quantise("two", z_early[:], TURN)
        layer2(0, 2 * P, "E", ((0, one, 2 * N), (1, two, 0)))
        nc.sync.dma_start(out[:, 0 : 2 * P], out_t[0][:])
        four = quantise("four", z_late[1][:], P)
        three = quantise("three", z_late[0][:], 2 * P)
        layer2(2 * P, TURN, "F", ((1, four, 0), (0, three, 0)))
        layer2(TURN, V, "G", ((1, two, 2 * P), (0, three, P)))
        nc.sync.dma_start(out[:, 2 * P : V], out_t[1][:])
